import numpy as np, ml_dtypes
CORES = [48,51,52,55]
N = 4
import mx_ref
BF = ml_dtypes.bfloat16
def gcols(t, e):
    v = np.concatenate([t.reshape(8, 16, -1, 4), np.zeros((8, 16, 1, 4), BF)], axis=2)
    return np.ascontiguousarray(np.stack([v[g][:, e[g]] for g in range(8)])).reshape(128, -1)
def gpick(z, e):
    return np.concatenate([z[16 * g:16 * g + 16][:, e[g]] for g in range(8)])
def pick(q, e):
    c = np.concatenate([q[0].reshape(128, -1, 4), np.zeros((128, 1, 4), np.uint8)], axis=1); s = np.concatenate([q[1], np.ones((16, 1), np.uint8)], axis=1)
    return (np.ascontiguousarray(c[:, e].reshape(128, -1)), np.ascontiguousarray(s[:, e]))
def join(*qs):
    return (np.concatenate([q[0] for q in qs], axis=1), np.concatenate([q[1] for q in qs], axis=1))
def put(q, e, v):
    c, s = q[0].reshape(128, -1, 4).copy(), q[1].copy(); c[:, e] = v[0].reshape(128, -1, 4); s[:, e] = v[1]
    return (c.reshape(128, -1), s)
def pk(c, s):
    return (np.ascontiguousarray(c), mx_ref.live(s))
def emit(q):
    return q[0], q[1]
def packed(v, rng):
    q = [mx_ref.quantize(np.ascontiguousarray(v[r])) for r in range(N)]
    return np.stack([a for a, b in q]), np.stack([mx_ref.plane(b, rng) for a, b in q])
def values_of_codes():
    e, c = np.zeros((128, 128, 4), np.float32), np.zeros((128, 2, 4), np.uint8)
    e[np.arange(128), np.arange(128), 0] = 1
    c[:127, :, 0] = np.arange(256).reshape(2, 128).T[:127]
    return mx_ref.matmul(mx_ref.quantize(e.reshape(128, 512).astype(BF)), (c.reshape(128, 8), np.full((16, 2), 127, np.uint8))).T.reshape(-1).astype(np.float64)
CODE_VALUE, SCALE_VALUE = values_of_codes(), 2.0 ** (np.arange(256) - 127.0)
def decode(q):
    return (CODE_VALUE[q[0]].reshape(16, 8, -1, 4) * SCALE_VALUE[q[1]][:, None, :, None] + 0.0).reshape(128, -1).astype(np.float32)
def f(rng, *shape):
    return mx_ref.flush((rng.standard_normal(shape, dtype=np.float32) * np.exp2(rng.integers(-2, 3, shape[:-1] + (1,)))).astype(BF))
def wide(rng, *shape, cols=0):
    v = rng.standard_normal(shape, dtype=np.float32) * np.exp2(rng.integers(-12, 13, shape)).astype(np.float32)
    if cols: v *= np.repeat(np.exp2(rng.integers(-cols, cols + 1, shape[:-2] + (1, shape[-1] // 4))) * (rng.random(shape[:-2] + (1, shape[-1] // 4)) > 0.0625), 4, axis=-1).astype(np.float32)
    return mx_ref.flush(v.astype(BF))
C, R = 192, 2
DECIDE = np.flatnonzero(np.arange(128) % 16 < 8)
def partner(r, t):
    return r ^ (1 << t)
def parents(s):
    b = np.packbits(s.reshape(8 * N, 16, C)[:, :8] > 0, axis=1, bitorder="little")[:, 0].astype(np.int64)
    return b * np.arange(C) >> 8
def places(p):
    i, size = np.arange(len(p)), np.ones(p.shape, np.int64)
    for j in range(C - 1, 0, -1): size[i, p[:, j]] += size[:, j]
    place, free = np.zeros(p.shape, np.int64), np.ones(p.shape, np.int64)
    for j in range(1, C):
        place[:, j] = free[i, p[:, j]]
        free[i, p[:, j]] += size[:, j]
        free[:, j] = place[:, j] + 1
    return place
def highest(h, p):
    i = np.arange(len(p))
    for j in range(C - 1, 0, -1):
        k = p[:, j]
        h[i, :, k] = np.maximum(h[i, :, k], h[:, :, j])
    return h
def numbers_of(rng):
    return {"x": np.array(f(rng, N, 128, 4 * C)), "u": np.array(f(rng, N, 128, 512)), "v": np.array(f(rng, N, 128, 512))}
def weights(rng, w):
    c, p = packed(w, rng)
    return {"wc": c, "ws": p}
def setup_inputs(rng):
    return {**numbers_of(rng), **weights(rng, f(rng, N, 128, 2048))}
def setup_inputs_trees(rng):
    d = numbers_of(rng)
    x = d["x"].astype(np.float32).reshape(N, 8, 16, C, 4)
    w = np.array(f(rng, N, 128, 2048)).astype(np.float32).reshape(N, 8, 16, 4, 8, 16, 4)
    u = d["u"].reshape(N, 128, 128, 4)
    low = rng.permutation(N) < N // 2
    size, one = np.where(low, 2.0 ** -28, 1.0), np.where(low, 2.0 ** -30, 1.0)
    x[:, :, :8] = 0
    x[:, :, 8, :, 0] = 1
    w[:, :, :, :, :, :9] = 0
    for r in range(N):
        for g, k in enumerate(rng.permutation(8)):
            way = -1.0 if k == 1 or k == 3 and r % 2 else 1.0
            a = np.full((8, C), (-0.75, -0.75, 1.0, 0.0, 0.0, -4.0, 1.0, -1.0)[k])
            if k == 3: a = rng.choice([1.0, -0.75, -1.0, -4.0], (8, C))
            if k == 5: a[7] = 1
            if k == 6: a[0] = rng.choice([1.0, -4.0], C)
            x[r, g, :8, :, 0] = way * a * size[r]
            w[r, g, 8, 0, g, :8, 0] = 32 * way * size[r]
    u[:, :, DECIDE] = 0
    u[:, DECIDE, DECIDE, 0] = one.astype(np.float32).astype(BF)[:, None]
    return {"x": x.reshape(N, 128, 4 * C).astype(BF), "u": u.reshape(N, 128, 512), "v": d["v"], **weights(rng, w.reshape(N, 128, 2048).astype(BF))}
def setup_inputs_zeros(rng):
    d = numbers_of(rng)
    x = d["x"].reshape(N, 128, C, 4)
    for r in range(N):
        a = x[r][:, :5].copy()
        a[:, :2] = 0
        x[r] = a[:, rng.permutation(C) % 5]
    x[rng.integers(N)] = 0
    return {"x": x.reshape(N, 128, 4 * C), "u": d["u"], "v": d["v"], **weights(rng, f(rng, N, 128, 2048))}
def setup_inputs_huge(rng):
    d = numbers_of(rng)
    high = int(rng.integers(N))
    size = np.full(N, 0.25)
    size[high] = 1
    x = 2.0 ** 30 * (0.5 + 0.5 * rng.random((N, 8, 16, C, 4)))
    x[:, :, :8] *= size[:, None, None, None, None]
    x[high, :, 0, :, 0] = 2.0 ** 30
    c = np.stack([rng.permutation(C) % 2 * 2.0 - 1.0 for r in range(N)])
    x[:, :, :8, :, 2:] *= c[:, None, None, :, None]
    u = d["u"].reshape(N, 8, 16, 128, 4)
    a = 2.0 ** 30 * (0.75 + 0.25 * rng.random((N, 8, 8, 64, 2))) * rng.choice([-1.0, 1.0], (N, 1, 1, 64, 1))
    u[:, :, :, DECIDE] = 0
    u[:, :, :8, DECIDE, 2:] = a.astype(np.float32).astype(BF)
    w = np.zeros((N, 8, 16, 4, 8, 16, 4), np.float32)
    for g in range(8):
        for p in range(8):
            for b in range(2): w[:, g, p, b, g, p + 8, b] = -32
    return {"x": x.astype(np.float32).reshape(N, 128, 4 * C).astype(BF), "u": u.reshape(N, 128, 512), "v": d["v"], **weights(rng, w.reshape(N, 128, 2048).astype(BF))}
def setup_inputs_spread(rng):
    d = setup_inputs(rng)
    d["x"] = wide(rng, N, 128, 4 * C, cols=6)
    return d
def check_inputs(d):
    b = []
    for k in ("x", "u", "v"):
        a = np.abs(d[k].astype(np.float32))
        if not (np.isfinite(a).all() and ((a == 0) | (a >= 2.0 ** -30) & (a <= 2.0 ** 30)).all()): b.append("a value of " + k)
    if ((d["wc"] == 127) | (d["wc"] == 255)).any(): b.append("a code of wc that is no number")
    ends = np.tile(np.repeat(np.array([0.0, 2.0 ** -30, 2.0 ** 30, 0.0]), 4), (128, 1)).astype(BF)
    none, least, most = emit(mx_ref.quantize(ends))[1][0, :3]
    s = np.stack([mx_ref.live(p) for p in d["ws"]])
    if not ((s == none) | (s >= least) & (s <= most)).all(): b.append("a scale of ws")
    return b
def reference(x, u, v, wc, ws):
    qu = [mx_ref.quantize(u[r]) for r in range(N)]
    lay = [pk(wc[r], ws[r]) for r in range(N)]
    now = x
    for t in range(R):
        held = [mx_ref.quantize(now[r]) for r in range(N)]
        own = np.stack([decode(q).astype(BF) for q in held])
        p = parents(np.stack([mx_ref.matmul(qu[r], held[r]) for r in range(N)]))
        place = places(p)
        o, place = np.argsort(place, axis=1).reshape(N, 8, C), place.reshape(N, 8, C)
        sent = [mx_ref.quantize(gcols(own[r], o[r])) for r in range(N)]
        h = np.zeros((N, 128, C, 4), np.float32)
        for r in range(N):
            for b in range(4):
                z = mx_ref.matmul(pick(lay[r], np.arange(128 * b, 128 * b + 128)), sent[partner(r, t)]) * np.float32(0.03125)
                h[r, :, :, b] = gpick(z, place[r])
        m = highest(h.reshape(8 * N, 16, C, 4), p).reshape(N, 128, 4 * C)
        now = (own.astype(np.float32) + m).astype(BF)
    y, op = np.zeros((N, 128, C), np.float32), p.reshape(N, 8, C).astype(np.float32)
    oc, osc = np.zeros((N, 128, 4 * C), np.uint8), np.zeros((N, 16, C), np.uint8)
    for r in range(N):
        q = mx_ref.quantize(now[r])
        y[r] = mx_ref.matmul(mx_ref.quantize(v[r]), q)
        oc[r], osc[r] = emit(q)
    return {"y": y, "op": op, "oc": oc, "osc": osc}

@@ -1,0 +1,540 @@
+from concourse.mybir import dt, AluOpType, ActivationFunctionType
+
+A = AluOpType
+F = ActivationFunctionType
+C = 192
+BIG = 2.0 ** 60
+MAGIC = 12582912.0
+W16 = [4913.0, 289.0, 17.0, 1.0]
+W64 = [278920.0, 4290.0, 65.0]
+KB0 = [0, 64, 192]
+XB0 = [0, 0, 128]
+TW = 1296
+NV = 5
+X4, U8, U16, F32, B16, I32 = "float8_e4m3fn_x4", "uint8", "uint16", "float32", "bfloat16", "int32"
+
+SCRATCH = {}
+for _n, _w, _d in [
+    ("X0", 768, B16), ("X1", 768, B16), ("X2", 768, B16),
+    ("qx0", C, X4), ("qx1", C, X4), ("qx2", C, X4), ("sx0", C, U8), ("sx1", C, U8), ("sx2", C, U8),
+    ("lq0", C, X4), ("lq1", C, X4), ("lp0", C, U8), ("lp1", C, U8),
+    ("ol0", 12, U16), ("ol1", 12, U16), ("lo0", 12, U16), ("lo1", 12, U16),
+    ("Bt0", 768, B16), ("Bt1", 768, B16), ("qf0", C, X4), ("qf1", C, X4), ("sf0", C, U8), ("sf1", C, U8),
+    ("ut", 512, B16), ("vt", 512, B16), ("qu", 128, X4), ("su", 128, U8), ("qv", 128, X4), ("sv", 128, U8),
+    ("qw", 512, X4), ("sw", 512, U8), ("Z", 528, B16), ("qe", 512, X4), ("se", 512, U8),
+    ("Tp", 768, B16), ("TB", 384, B16), ("RB", 384, B16), ("cm", 384, B16),
+    ("pi", 4, I32), ("col", 16, F32), ("pat", 48, F32), ("tmp", 128, F32), ("c16", 12, F32), ("c16m", 12, F32),
+    ("cj", 12, F32), ("thr", 12, F32), ("w16m", 12, F32), ("w64m", 12, F32), ("tiem", 12, F32),
+    ("IO", 384, F32), ("MOD", 384, F32), ("ext", C, F32), ("ones", 768, B16), ("m16", C, B16), ("m64", 768, B16),
+    ("m8", C, F32), ("w16", C, F32), ("tie", C, F32), ("TE", 216, F32),
+    ("PA", 384, F32), ("PB", 384, F32), ("V0", 384, F32), ("VA", 384, F32), ("VB", 384, F32),
+    ("V0D", C, F32), ("VD", C, F32),
+    ("RAW", C, F32), ("RAW2", C, F32), ("RK", C, F32), ("RE", C, F32), ("RX", 128, F32),
+    ("sm", 192, F32), ("LS", 48, U16), ("LX", 24, U16), ("LR", 12, U16), ("LR2", 12, U16), ("LE", 12, U16),
+    ("LY", 8, U16), ("LP", 12, U16), ("LL", 24, U16),
+    ("CMP", 960, B16), ("CNT", 960, B16), ("JK", 1344, B16), ("AC", 48, F32),
+    ("U", C, F32), ("KB", 384, F32), ("XS", 320, F32), ("G", 128, F32), ("U1", 64, F32), ("EP", 128, F32),
+    ("E", C, F32), ("O", C, F32), ("LV", C, F32), ("LW", C, F32), ("PR", C, F32),
+    ("TAB", 4 * TW, F32), ("G1", 768, F32), ("MX", 768, F32), ("Y", C, F32),
+]:
+    SCRATCH[_n] = ("sbuf", [128, _w], _d)
+SCRATCH["BT"] = ("sbuf", [128, 12, 32], B16)
+SCRATCH["ps"] = ("psum", [128, 4096], F32)
+
+POOL = {"v": 40, "s": 30, "t": 10, "g": 10}
+DMAS = ["dx", "du", "dv", "dwc", "dws", "dop", "doc", "ds0", "ds1", "ds2", "ds3", "dy"]
+SEMAPHORES = [e + str(i) for e in POOL for i in range(POOL[e])] + DMAS + ["ax0", "ax1", "al0", "al1", "ls"]
+
+
+def rank_program(g, core, T, topo):
+    rank = T.rank_of(core)
+    if rank is None:
+        return
+    Q = {"v": g.vector, "s": g.scalar, "t": g.tensor, "g": g, "y": g.sync}
+    known = {e: set() for e in Q}
+    cur = {e: None for e in Q}
+    nxt = {e: 0 for e in Q}
+    last = {}
+    batches = []
+    hist = {}
+
+    def new_batch(e, sem, base):
+        b = {"id": len(batches), "e": e, "sem": sem, "n": base, "known": set(known[e]) if e else set(), "waited": False}
+        batches.append(b)
+        last[sem] = b
+        return b
+
+    def wait(e, b):
+        if b["id"] in known[e]:
+            return
+        if b["e"] and cur[b["e"]] is b:
+            cur[b["e"]] = None
+        Q[e].wait_ge(T.sem[b["sem"]], b["n"])
+        b["waited"] = True
+        known[e].add(b["id"])
+        known[e].update(b["known"])
+        cur[e] = None
+
+    def cut(e):
+        cur[e] = None
+
+    def reg(r):
+        return (r, 0, 1 << 20) if isinstance(r, str) else r
+
+    def depend(e, reads, writes):
+        deps = {}
+        for w, rs in ((False, reads), (True, writes)):
+            for r in rs:
+                n, lo, hi = reg(r)
+                for (l2, h2, w2, b) in hist.get(n, []):
+                    if l2 < hi and lo < h2 and (w or w2 or (n == "ps" and b["e"] != e)):
+                        deps[b["id"]] = b
+        for i in sorted(deps, reverse=True):
+            wait(e, deps[i])
+
+    def note(b, reads, writes):
+        for w, rs in ((False, reads), (True, writes)):
+            for r in rs:
+                n, lo, hi = reg(r)
+                h = hist.setdefault(n, [])
+                if w:
+                    h[:] = [x for x in h if not (lo <= x[0] and x[1] <= hi)]
+                h.append((lo, hi, w, b))
+
+    def op(e, fn, reads, writes):
+        depend(e, reads, writes)
+        if cur[e] is None:
+            sem = e + str(nxt[e] % POOL[e])
+            nxt[e] += 1
+            base = 0
+            if sem in last:
+                wait(e, last[sem])
+                base = last[sem]["n"]
+            cur[e] = new_batch(e, sem, base)
+        b = cur[e]
+        fn().then_inc(T.sem[b["sem"]], 1)
+        b["n"] += 1
+        note(b, reads, writes)
+
+    def dma(e, sem, out, in_, reads, writes):
+        depend(e, reads, writes)
+        Q[e].dma_start(out, in_).then_inc(T.sem[sem], 16)
+        b = new_batch(e, sem, 16)
+        note(b, reads, writes)
+
+    def ts(out, in0, s1, s2, o0, o1, reads, writes):
+        if o1 is None:
+            op("v", lambda: g.vector.tensor_scalar(out, in0, s1, None, o0), reads, writes)
+        else:
+            op("v", lambda: g.vector.tensor_scalar(out, in0, s1, s2, o0, o1), reads, writes)
+
+    def tt(out, in0, in1, o, reads, writes):
+        op("v", lambda: g.vector.tensor_tensor(out, in0, in1, o), reads, writes)
+
+    def scan(out, d0, d1, init, o0, o1, reads, writes):
+        op("v", lambda: g.vector.tensor_tensor_scan(out, d0, d1, init, o0, o1), reads, writes)
+
+    def cp(out, in_, reads, writes):
+        op("v", lambda: g.vector.tensor_copy(out, in_), reads, writes)
+
+    def ms(ap, c, writes):
+        op("v", lambda: g.vector.memset(ap, c), [], writes)
+
+    def act(out, in_, reads, writes, scale=None, bias=None, func=None, acc=None):
+        kw = {}
+        if scale is not None:
+            kw["scale"] = scale
+        if bias is not None:
+            kw["bias"] = bias
+        if acc is not None:
+            kw["accum_out"] = acc
+        fu = func if func is not None else (F.Identity if bias is not None else F.Copy)
+        op("s", lambda: g.scalar.activation(out, in_, fu, **kw), reads, writes)
+
+    def quant(q, s, x, reads, writes):
+        op("v", lambda: g.vector.quantize_mx(q, s, x), reads, writes)
+
+    def mm(bank, lq, lsc, rq, rs, reads):
+        op("t", lambda: g.tensor.matmul_mx(T.ps[:, 512 * bank:512 * bank + C], lq, lsc, rq, rs, True, True),
+           reads, [("ps", bank, bank + 1)])
+
+    def iota(name, pattern, base):
+        op("g", lambda: g.iota(T[name][:], pattern, base, 0, allow_small_or_imprecise_dtypes=True), [], [name])
+
+    def mask(name, n, period):
+        op("g", lambda: g.affine_select(T[name][:], T.ones[:, 0:n], [[0, n // period], [1, period]], A.not_equal,
+                                        0.0, 0, 0), ["ones"], [name])
+
+    sent = [0]
+
+    def send(peer, dst, src, sem, reads):
+        depend("g", reads, [])
+        rid, pid, _ = topo.addr(peer)
+        g.remote_dma(dst, src, T.sem[sem], T.sem.ls, pid, rid, topo.mask(core, peer))
+        n = len(topo.engines(core, peer))
+        sent[0] += n
+        cut("g")
+
+    def arrival(peer, sem, calls, writes):
+        note(new_batch(None, sem, calls * len(topo.engines(peer, core))), [], writes)
+
+    def bank(b):
+        return T.ps[:, 512 * b:512 * b + C]
+
+    col = lambda i: T.col[:, i:i + 1]
+    cq, ch, cnh, c1q, cq1, ccj, cim, cmt, cM, cnM, cbm = [col(i) for i in range(11)]
+    rc = lambda i: ("col", i, i + 1)
+
+    dma("y", "dx", T.X0[:], T.x[:], [], ["X0"])
+    dma("s", "du", T.ut[:], T.u[:], [], ["ut"])
+    dma("y", "dwc", T.qw[:].bitcast(dt.uint8), T.wc[:], [], ["qw"])
+    dma("y", "dws", T.sw[:], T.ws[:], [], ["sw"])
+    dma("y", "dv", T.vt[:], T.v[:], [], ["vt"])
+
+    op("g", lambda: g.iota(T.pi[:, 0:1], [[0, 1]], 0, 1), [], [("pi", 0, 1)])
+    cut("g")
+    iota("c16", [[16, 12]], 0)
+    cut("g")
+    iota("IO", [[1, 384]], 0)
+    cut("g")
+    ms(T.ones[:, 0:C], 1.0, [("ones", 0, C)])
+    ms(T.Z[:], 0.0, ["Z"])
+    cut("v")
+    for lo, hi, c in ((0, 16, 1.0), (16, 17, 0.0), (17, 24, 0.5), (24, 25, BIG), (25, 48, 1.0)):
+        ms(T.pat[:, lo:hi], c, [("pat", lo, hi)])
+    ms(T.tmp[:, 96:112], 0.5, [("tmp", 96, 112)])
+    ms(T.tmp[:, 112:128], 0.0, [("tmp", 112, 128)])
+    op("g", lambda: g.affine_select(T.Z[:, 3:515:4], T.ones[:, 0:128], [[-1, 128]], A.is_equal, 0.0, 0, 1),
+       [("ones", 0, C)], ["Z"])
+    ts(T.pi[:, 2:3], T.pi[:, 0:1], 15, None, A.bitwise_and, None, [("pi", 0, 1)], [("pi", 2, 3)])
+    ts(T.pi[:, 3:4], T.pi[:, 0:1], 4, 1, A.arith_shift_right, A.bitwise_and, [("pi", 0, 1)], [("pi", 3, 4)])
+    scan(T.V0[:, 0:16], T.tmp[:, 96:112], T.tmp[:, 112:128], 65536.0, A.mult, A.add, [("tmp", 96, 128)], [("V0", 0, 16)])
+    cp(T.col[:, 0:2], T.pi[:, 2:4], [("pi", 2, 4)], [("col", 0, 2)])
+    ts(cnh, ch, -1.0, 1.0, A.mult, A.add, [rc(1)], [rc(2)])
+    ts(c1q, cq, -1.0, 1.0, A.mult, A.add, [rc(0)], [rc(3)])
+    ts(cq1, cq, 1.0, None, A.add, None, [rc(0)], [rc(4)])
+    ts(ccj, ch, 1.0 / BIG, 0.5, A.max, A.mult, [rc(1)], [rc(5)])
+    ts(cim, cq, 15.0, 1.0 / BIG, A.is_equal, A.max, [rc(0)], [rc(6)])
+    ts(cmt, cq, 15.0, BIG, A.not_equal, A.mult, [rc(0)], [rc(7)])
+    ts(T.tmp[:, 0:32], T.pat[:, 0:32], ch, None, A.mult, None, ["pat", rc(1)], [("tmp", 0, 32)])
+    ts(T.tmp[:, 32:64], T.pat[:, 16:48], cnh, None, A.mult, None, ["pat", rc(2)], [("tmp", 32, 64)])
+    ts(T.cj[:], T.c16[:], cq, ccj, A.add, A.mult, ["c16", rc(0), rc(5)], ["cj"])
+    ts(T.thr[:], T.c16[:], c1q, None, A.max, None, ["c16", rc(3)], ["thr"])
+    ts(cM, cmt, 1.0, None, A.max, None, [rc(7)], [rc(8)])
+    ts(cnM, cmt, 1.0, -1.0, A.max, A.mult, [rc(7)], [rc(9)])
+    ts(T.tmp[:, 64:80], T.IO[:, 0:16], cq, None, A.not_equal, None, ["IO", rc(0)], [("tmp", 64, 80)])
+    ts(T.tmp[:, 80:96], T.IO[:, 0:16], cq1, BIG, A.is_equal, A.mult, ["IO", rc(4)], [("tmp", 80, 96)])
+    tt(T.cm[:, 0:32], T.tmp[:, 0:32], T.tmp[:, 32:64], A.add, [("tmp", 0, 64)], [("cm", 0, 32)])
+    tt(T.ext[:, 0:16], T.tmp[:, 64:80], T.tmp[:, 80:96], A.add, [("tmp", 64, 96)], [("ext", 0, 16)])
+    quant(T.qu[:], T.su[:], T.ut[:], ["ut"], ["qu"])
+    for n in ("V0", "VA", "VB"):
+        act(T[n][:, C:384], T.IO[:, 0:C], ["IO"], [(n, C, 384)], scale=0.0)
+    for n in ("PA", "PB"):
+        act(T[n][:, C:384], T.IO[:, C:384], ["IO"], [(n, C, 384)])
+    for n, w in (("cm", 32), ("ext", 16), ("V0", 16)):
+        act(T[n][:, w:2 * w], T[n][:, 0:w], [(n, 0, w)], [(n, w, 2 * w)])
+    for n, w in (("cm", 32), ("ext", 16), ("V0", 16)):
+        act(T[n][:, 2 * w:4 * w], T[n][:, 0:2 * w], [(n, 0, 2 * w)], [(n, 2 * w, 4 * w)])
+    for n, w in (("cm", 32), ("ext", 16), ("V0", 16)):
+        act(T[n][:, 4 * w:8 * w], T[n][:, 0:4 * w], [(n, 0, 4 * w)], [(n, 4 * w, 8 * w)])
+        act(T[n][:, 8 * w:12 * w], T[n][:, 0:4 * w], [(n, 0, 4 * w)], [(n, 8 * w, 12 * w)])
+    cut("s")
+
+    def late_vector():
+        for b in range(4):
+            quant(T.qe[:, 128 * b:128 * b + 128], T.se[:, 128 * b:128 * b + 128], T.Z[:, 3 - b:515 - b], ["Z"],
+                  [("qe", b, b + 1)])
+
+    def late_scalar():
+        act(T.ones[:, C:576], T.IO[:], ["IO"], [("ones", C, 576)], scale=0.0, bias=1.0)
+        act(T.ones[:, 576:768], T.IO[:, 0:C], ["IO"], [("ones", 576, 768)], scale=0.0, bias=1.0)
+        for k in range(4):
+            act(T.w16[:, 16 * k:16 * k + 16], T.ones[:, 0:16], [("ones", 0, C)], [("w16", 16 * k, 16 * k + 16)], scale=W16[k])
+        act(T.V0D[:], T.V0[:, 0:C], [("V0", 0, C)], ["V0D"])
+        act(T.KB[:, 64:128], T.IO[:, 0:64], ["IO"], [("KB", 64, 128)], scale=0.0)
+        act(T.KB[:, C:320], T.IO[:, 0:128], ["IO"], [("KB", C, 320)], scale=0.0)
+        act(T.XS[:, 0:64], T.IO[:, 0:64], ["IO"], [("XS", 0, 64)])
+        act(T.XS[:, 128:256], T.IO[:, 0:128], ["IO"], [("XS", 128, 256)])
+
+    def late_scalar2(k):
+        if k == 0:
+            for s in (1, 2):
+                act(T.w16[:, 64 * s:64 * s + 64], T.w16[:, 0:64], [("w16", 0, 64)], [("w16", 64 * s, 64 * s + 64)])
+        elif k == 1:
+            for s in range(3):
+                act(T.TE[:, 72 * s:72 * s + 72], T.IO[:, 0:72], ["IO"], [("TE", 72 * s, 72 * s + 72)], scale=W64[s],
+                    bias=W64[s] * (-32.0 if s == 0 else 1.0))
+        else:
+            for s in range(3):
+                act(T.w64m[:, 4 * s:4 * s + 4], T.ones[:, 0:4], [("ones", 0, C)], [("w64m", 4 * s, 4 * s + 4)],
+                    scale=W64[s])
+
+    def late_gpsimd():
+        iota("c16m", [[0, 3], [16, 4]], 1)
+        cut("g")
+        mask("m16", C, 16)
+        cut("g")
+        mask("m64", 768, 64)
+        cut("g")
+        iota("tie", [[0, 3], [-1, 64]], -33)
+        cut("g")
+        mask("m8", C, 8)
+        iota("MOD", [[0, 2], [1, C]], 0)
+
+    def unwrap(out, row, n, reads, writes):
+        scan(out, T.ext[:, 0:n], row, 0.0, A.mult, A.add, ["ext"] + reads, writes)
+
+    def count_all(raw, rraw, a0):
+        for c in range(NV, 12):
+            k = c - NV
+            act(T.JK[:, C * k:C * k + C], T.E[:], ["E", rraw, rc(9)], [("JK", C * k, C * k + C), ("AC", a0 + c, a0 + c + 1)],
+                scale=cnM, bias=raw(c), func=F.Sign, acc=T.AC[:, a0 + c:a0 + c + 1])
+        for c in range(NV):
+            ts(T.CMP[:, C * c:C * c + C], T.E[:], cM, raw(c), A.mult, A.is_gt, ["E", rraw, rc(8)], [("CMP", C * c, C * c + C)])
+            if c % 2 == 1:
+                cut("v")
+        cut("v")
+        for c in range(NV):
+            scan(T.CNT[:, C * c:C * c + C], T.ones[:, 0:C], T.CMP[:, C * c:C * c + C], 0.0, A.mult, A.add,
+                 [("ones", 0, C), ("CMP", C * c, C * c + C)], [("CNT", C * c, C * c + C)])
+
+    sm = lambda k: T.sm[:, 12 * k:12 * k + 12]
+    rs = lambda k: ("sm", 12 * k, 12 * k + 12)
+
+    for t in range(2):
+        peer = T.cores[rank ^ (1 << t)]
+        X, qx, sx = "X%d" % t, "qx%d" % t, "sx%d" % t
+        lq, lp, ol, lo, Bt, qf, sf = ["%s%d" % (n, t) for n in ("lq", "lp", "ol", "lo", "Bt", "qf", "sf")]
+        xr = [X] if t == 0 else [X + "b%d" % b for b in range(4)]
+        quant(T[qx][:], T[sx][:], T[X][:], xr, [qx])
+        mm(4, T.qu[:], T.su[:], T[qx][:], T[sx][:], ["qu", qx])
+        cut("t")
+        send(peer, T[lq][:].bitcast(dt.uint8), T[qx][:].bitcast(dt.uint8), "ax%d" % t, [qx])
+        send(peer, T[lp][:], T[sx][:], "ax%d" % t, [qx])
+        arrival(peer, "ax%d" % t, 2, [lq])
+        if t == 0:
+            late_vector()
+            late_scalar()
+            late_gpsimd()
+        for k in range(2):
+            ts(T.BT[:, :, 16 * k:16 * k + 16], bank(4), 0.0, None, A.is_gt, None, [("ps", 4, 5)], [("BT", k, k + 1)])
+        for b in range(4):
+            mm(b, T.qe[:, 128 * b:128 * b + 128], T.se[:, 128 * b:128 * b + 128], T[qx][:], T[sx][:], [("qe", b, b + 1), qx])
+        cut("t")
+        op("v", lambda: g.vector.transpose(T.TB[:], T.BT[:]), ["BT"], ["TB"])
+        scan(T.RB[:], T.cm[:], T.TB[:], 0.0, A.mult, A.add, ["cm", "TB"], ["RB"])
+        tt(sm(0), T.RB[:, 23:384:32], T.cj[:], A.mult, ["RB", "cj"], [rs(0)])
+        tt(sm(1), sm(0), T.thr[:], A.is_lt, [rs(0), "thr"], [rs(1)])
+        ts(sm(2), sm(0), -0.498046875, MAGIC, A.add, A.add, [rs(0)], [rs(2)])
+        ts(sm(3), sm(1), float(C), -MAGIC, A.mult, A.add, [rs(1)], [rs(3)])
+        tt(sm(4), sm(3), sm(2), A.add, [rs(2), rs(3)], [rs(4)])
+        cp(T.LS[:, 0:12], sm(4), [rs(4)], [("LS", 0, 12)])
+        act(T.PA[:, 0:C], T.IO[:].indirect(T.LS[:, 0:12]), ["IO", ("LS", 0, 12)], [("PA", 0, C)])
+        pn, vn = ["PA", "PB", "PA", "PB", "PA"], ["V0", "VA", "VB", "VA", "VB"]
+        for r in range(4):
+            L, rl = T.LS[:, 12 * r:12 * r + 12], ("LS", 12 * r, 12 * r + 12)
+            own = "V0D" if r == 0 else "VD"
+            act(T[pn[r + 1]][:, 0:C], T[pn[r]][:].indirect(L), [pn[r], rl], [(pn[r + 1], 0, C)])
+            cut("s")
+            tt(T[vn[r + 1]][:, 0:C], T[vn[r]][:].indirect(L), T[own][:], A.add, [vn[r], own, rl], [(vn[r + 1], 0, C)])
+            cut("v")
+            if r == 0 and t == 0:
+                scan(T.tmp[:, 0:16], T.ext[:, 0:16], T.V0[:, 0:16], 0.0, A.mult, A.add, ["ext", "V0"], [("tmp", 0, 16)])
+                quant(T.qv[:], T.sv[:], T.vt[:], ["vt"], ["qv"])
+            if r < 3:
+                act(T.VD[:], T[vn[r + 1]][:, 0:C], [(vn[r + 1], 0, C)], ["VD"])
+                cut("s")
+                if t == 0:
+                    late_scalar2(r)
+                unwrap(T.RAW[:], T[pn[r + 1]][:, 0:C], C, [(pn[r + 1], 0, C)], ["RAW"])
+                ts(T.LS[:, 12 * r + 12:12 * r + 24], T.RAW[:, 15:C:16], cim, 0.25, A.mult, A.add, ["RAW", rc(6)],
+                   [("LS", 12 * r + 12, 12 * r + 24)])
+        for b in range(4):
+            mm(4 + b, T.qe[:, 128 * b:128 * b + 128], T.se[:, 128 * b:128 * b + 128], T[lq][:], T[lp][:], [("qe", b, b + 1), lq])
+            cut("t")
+        unwrap(T.RAW2[:], T.VB[:, 0:C], C, [("VB", 0, C)], ["RAW2"])
+        for c in range(12):
+            act(T.JK[:, 16 * c:16 * c + 16], T.VB[:, 16 * c:16 * c + 16], [("VB", 0, C), "RAW2", rc(9)],
+                [("JK", 16 * c, 16 * c + 16), ("AC", c, c + 1)], scale=cnM, bias=T.RAW2[:, 16 * c + 15:16 * c + 16],
+                func=F.Sign, acc=T.AC[:, c:c + 1])
+        ts(sm(5), T.RAW2[:, 15:C:16], T.tmp[:, 15:16], None, A.add, None, ["RAW2", ("tmp", 0, 16)], [rs(5)])
+        cut("v")
+        unwrap(T.RAW[:], T.PA[:, 0:C], C, [("PA", 0, C)], ["RAW"])
+        cut("v")
+        for c in range(12):
+            ts(T.CMP[:, 16 * c:16 * c + 16], T.VB[:, 16 * c:16 * c + 16], cM, T.sm[:, 60 + c:61 + c], A.mult, A.is_lt,
+               [("VB", 0, C), rs(5), rc(8)], [("CMP", 16 * c, 16 * c + 16)])
+        cut("v")
+        ts(T.LX[:, 0:24:2], T.RAW[:, 15:C:16], cim, 0.25 - C, A.mult, A.add, ["RAW", rc(6)], ["LX"])
+        scan(T.CNT[:, 0:C], T.m16[:], T.CMP[:, 0:C], 0.0, A.mult, A.add, ["m16", ("CMP", 0, C)], [("CNT", 0, C)])
+        if t == 0:
+            ts(T.w16m[:], T.w16[:, 0:C:16], cM, None, A.mult, None, ["w16", rc(8)], ["w16m"])
+        cut("v")
+        ts(T.LR[:], T.AC[:, 0:12], 0.5, 8.75, A.mult, A.add, [("AC", 0, 12)], ["LR"])
+        for s in range(3):
+            o0 = KB0[s] + 64 * s
+            ts(T.KB[:, o0:o0 + 16], T.IO[:, 0:24].indirect(T.LR[:, 4 * s:4 * s + 1]), W16[0], None, A.mult, None,
+               ["IO", "LR"], [("KB", o0, o0 + 16)])
+        tt(T.U[:], T.IO[:, 0:24].indirect(T.LR[:]), T.w16[:], A.mult, ["IO", "LR", "w16"], ["U"])
+        for be in range(4):
+            for s in (1, 2):
+                c = 4 * s + be
+                o0 = XB0[s] + 16 * c
+                act(T.XS[:, o0:o0 + 16], T.XS[:, XB0[s]:o0].indirect(T.LX[:, 2 * c:2 * c + 1]), [("XS", XB0[s], o0), "LX"],
+                    [("XS", o0, o0 + 16)])
+        for b in range(2):
+            act(T.Tp[:, C * b:C * b + C], bank(4 + b), [("ps", 4 + b, 5 + b)], [("Tp", b, b + 1)])
+        for be in range(1, 4):
+            for s in range(3):
+                c = 4 * s + be
+                o0 = KB0[s] + 16 * c
+                tt(T.KB[:, o0:o0 + 16], T.KB[:, KB0[s]:o0].indirect(T.LX[:, 2 * c:2 * c + 1]), T.U[:, 16 * c:16 * c + 16],
+                   A.add, [("KB", KB0[s], o0), "LX", "U"], [("KB", o0, o0 + 16)])
+            cut("v")
+            if be == 1:
+                ts(sm(6), T.AC[:, 0:12], -0.5, -7.5, A.mult, A.add, [("AC", 0, 12)], [rs(6)])
+            elif be == 2:
+                tt(sm(7), sm(6), T.CNT[:, 15:C:16], A.add, [rs(6), ("CNT", 0, C)], [rs(7)])
+            else:
+                tt(sm(8), sm(7), T.w16m[:], A.mult, [rs(7), "w16m"], [rs(8)])
+            cut("v")
+        live = lambda s: T.KB[:, KB0[s] + 64 * s:KB0[s] + 64 * s + 64]
+        rlive = lambda s: ("KB", KB0[s] + 64 * s, KB0[s] + 64 * s + 64)
+        for s in range(3):
+            unwrap(T.RK[:, 64 * s:64 * s + 64], live(s), 64, [rlive(s)], [("RK", 64 * s, 64 * s + 64)])
+        for c in range(12):
+            act(T.JK[:, 64 * c:64 * c + 64], live(c // 4), [rlive(c // 4), "RK", rc(9)],
+                [("JK", 64 * c, 64 * c + 64), ("AC", 12 + c, 13 + c)], scale=cnM, bias=T.RK[:, 16 * c + 15:16 * c + 16],
+                func=F.Sign, acc=T.AC[:, 12 + c:13 + c])
+        tt(sm(9), T.RK[:, 15:C:16], sm(8), A.add, ["RK", rs(8)], [rs(9)])
+        cut("v")
+        for s in (1, 2):
+            o0 = XB0[s] + 64 * s
+            unwrap(T.RX[:, 64 * s - 64:64 * s], T.XS[:, o0:o0 + 64], 64, [("XS", o0, o0 + 64)], [("RX", 64 * s - 64, 64 * s)])
+        cut("v")
+        for c in range(12):
+            ts(T.CMP[:, 64 * c:64 * c + 64], live(c // 4), cM, T.sm[:, 108 + c:109 + c], A.mult, A.is_lt,
+               [rlive(c // 4), rs(9), rc(8)], [("CMP", 64 * c, 64 * c + 64)])
+        cut("v")
+        ts(T.LY[:], T.RX[:, 15:128:16], cim, 0.25, A.mult, A.add, ["RX", rc(6)], ["LY"])
+        scan(T.CNT[:, 0:768], T.m64[:], T.CMP[:, 0:768], 0.0, A.mult, A.add, ["m64", ("CMP", 0, 768)], [("CNT", 0, 768)])
+        cut("v")
+        ts(T.LR2[:], T.AC[:, 12:24], 0.5, 32.75, A.mult, A.add, [("AC", 12, 24)], ["LR2"])
+        cut("v")
+        cp(T.LE[:], T.CNT[:, 63:768:64], [("CNT", 0, 768)], ["LE"])
+        act(T.G[:, 0:64], T.IO[:, 0:72].indirect(T.LR2[:, 0:4]), ["IO", "LR2"], [("G", 0, 64)], scale=W64[0],
+            bias=-33.0 * W64[0])
+        act(T.U1[:], T.IO[:, 0:72].indirect(T.LR2[:, 4:8]), ["IO", "LR2"], ["U1"], scale=W64[1])
+        cut("s")
+        for b in range(2, 4):
+            act(T.Tp[:, C * b:C * b + C], bank(4 + b), [("ps", 4 + b, 5 + b)], [("Tp", b, b + 1)])
+        for s in (1, 2, 0):
+            out, ro = (T.E[:, 0:64], ("E", 0, 64)) if s == 0 else (T.EP[:, 64 * s - 64:64 * s], ("EP", 64 * s - 64, 64 * s))
+            tt(out, T.TE[:, 72 * s:72 * s + 72].indirect(T.LE[:, 4 * s:4 * s + 4]), T.tie[:, 64 * s:64 * s + 64], A.add,
+               ["TE", "LE", "tie"], [ro])
+        cut("v")
+        tt(T.G[:, 64:128], T.G[:, 0:64].indirect(T.LY[:, 0:4]), T.U1[:], A.add, [("G", 0, 64), "LY", "U1"], [("G", 64, 128)])
+        cut("v")
+        tt(T.E[:, 64:128], T.G[:, 0:64].indirect(T.LY[:, 0:4]), T.EP[:, 0:64], A.add, [("G", 0, 64), "LY", "EP"],
+           [("E", 64, 128)])
+        tt(T.E[:, 128:C], T.G[:, 0:128].indirect(T.LY[:, 4:8]), T.EP[:, 64:128], A.add, ["G", "LY", "EP"], [("E", 128, C)])
+        cut("v")
+        ts(sm(6), T.AC[:, 12:24], -0.5, -31.5, A.mult, A.add, [("AC", 12, 24)], [rs(6)])
+        unwrap(T.RE[:], T.E[:], C, ["E"], ["RE"])
+        cut("v")
+        tt(sm(7), sm(6), T.CNT[:, 63:768:64], A.add, [rs(6), ("CNT", 0, 768)], [rs(7)])
+        count_all(lambda c: T.RE[:, 16 * c + 15:16 * c + 16], "RE", 24)
+        cp(T.LP[:, 0:NV], T.CNT[:, C - 1:NV * C:C], [("CNT", 0, NV * C)], [("LP", 0, NV)])
+        ts(T.LP[:, NV:12], T.AC[:, 24 + NV:36], -0.5, 95.75, A.mult, A.add, [("AC", 24, 36)], [("LP", NV, 12)])
+        if t == 1:
+            act(T.PR[:], T.MOD[:].indirect(T.LS[:, 0:12]), ["MOD", ("LS", 0, 12)], ["PR"])
+            cut("s")
+        cp(T.O[:].indirect(T.LP[:]), T.IO[:, 0:C], ["IO", "LP"], ["O"])
+        cut("v")
+        cp(T.LV[:, 0:8 * NV:8], T.CNT[:, C - 1:NV * C:C], [("CNT", 0, NV * C)], ["LVp"])
+        unwrap(T.RAW[:], T.O[:], C, ["O"], ["RAW"])
+        cut("v")
+        if t == 0:
+            ts(T.w64m[:], T.w64m[:], cM, None, A.mult, None, ["w64m", rc(8)], ["w64m"])
+            ts(T.tiem[:], T.c16m[:], cq, cM, A.add, A.mult, ["c16m", rc(0), rc(8)], ["tiem"])
+            cut("v")
+        ts(T[ol][:], T.RAW[:, 15:C:16], cim, 0.25, A.mult, A.add, ["RAW", rc(6)], [ol])
+        send(peer, T[lo][:], T[ol][:], "al%d" % t, [ol])
+        arrival(peer, "al%d" % t, 1, [lo])
+        if t == 1:
+            dma("y", "dop", T.op[:], T.PR[0:128:16, :], ["PR"], [])
+        tt(sm(8), sm(7), T.w64m[:], A.mult, [rs(7), "w64m"], [rs(8)])
+        tt(sm(10), T.RE[:, 15:C:16], T.tiem[:], A.add, ["RE", "tiem"], [rs(10)])
+        ts(T.LV[:, 8 * NV:96:8], T.AC[:, 24 + NV:36], -0.5, 95.5, A.mult, A.add, [("AC", 24, 36)], ["LVq"])
+        tt(sm(11), sm(10), sm(8), A.subtract, [rs(10), rs(8)], [rs(11)])
+        count_all(lambda c: T.sm[:, 132 + c:133 + c], rs(11), 36)
+        ts(T.LV[:, 96:96 + 8 * NV:8], T.CNT[:, C - 1:NV * C:C], -1.0, None, A.add, None, [("CNT", 0, NV * C)], ["LVe"])
+        ts(T.LV[:, 96 + 8 * NV:C:8], T.AC[:, 36 + NV:48], -0.5, 95.0, A.mult, A.add, [("AC", 36, 48)], ["LVf"])
+        cut("v")
+        for b in (2, 3):
+            act(T[Bt][:, b:768:4], T.Tp[:, C * b:C * b + C].indirect(T[lo][:]), [("Tp", b, b + 1), lo], [Bt + "b%d" % b])
+        tt(sm(12), T.LV[:, 96:C:8], T.LV[:, 0:96:8], A.subtract, ["LVp", "LVq", "LVe", "LVf"], [rs(12)])
+        for b in (0, 1):
+            cp(T[Bt][:, b:768:4], T.Tp[:, C * b:C * b + C].indirect(T[lo][:]), [("Tp", b, b + 1), lo], [Bt + "b%d" % b])
+        quant(T[qf][:], T[sf][:], T[Bt][:], [Bt + "b%d" % b for b in range(4)], [qf])
+        for b in range(4):
+            mm(4 + b, T.qw[:, 128 * b:128 * b + 128], T.sw[:, 128 * b:128 * b + 128], T[qf][:], T[sf][:], ["qw", "sw", qf])
+            cut("t")
+        cut("v")
+        for m in range(1, 8):
+            ts(T.LV[:, m:96:8], sm(12), 2.0 ** m - 1.0, 193.0 - 2.0 ** (m - 1), A.is_gt, A.mult, [rs(12)], ["LV%d" % m])
+            ts(T.LV[:, 96 + m:C:8], sm(12), 2.0 ** m - 1.0, 193.0 - 2.0 ** m, A.is_gt, A.mult, [rs(12)], ["LU%d" % m])
+        cut("v")
+        for b in range(4):
+            act(T.TAB[:, TW * b:TW * b + C], bank(4 + b), [("ps", 4 + b, 5 + b)], [("TAB", TW * b, TW * b + C)], scale=0.03125)
+            cut("s")
+        off = [193 * k - 2 ** k + 1 for k in range(9)]
+
+        def level(b, k):
+            n, h, a, o = 193 - 2 ** k, 2 ** (k - 1), TW * b + off[k - 1], TW * b + off[k]
+            scan(T.TAB[:, o:o + n], T.TAB[:, a:a + n], T.TAB[:, a + h:a + h + n], 1e29, A.min, A.max,
+                 [("TAB", a, a + h + n)], [("TAB", o, o + n)])
+            cut("v")
+
+        def win(b):
+            return T.TAB[:, TW * b:TW * b + off[8]], ("TAB", TW * b, TW * b + off[8])
+
+        Xn = "X%d" % (t + 1)
+        for pair in ((0, 1), (2, 3)):
+            for k in range(1, 8):
+                for b in pair:
+                    level(b, k)
+                if pair[0] == 0 and k == 1:
+                    scan(T.LW[:], T.m8[:], T.LV[:], 0.0, A.mult, A.add,
+                         ["m8", "LVp", "LVq", "LVe", "LVf"] + ["LV%d" % m for m in range(1, 8)] + ["LU%d" % m for m in range(1, 8)],
+                         ["LW"])
+                    cut("v")
+                if pair[0] == 0 and k == 2:
+                    cp(T.LL[:], T.LW[:, 7:C:8], ["LW"], ["LL"])
+                    cut("v")
+            for b in pair:
+                w, rw = win(b)
+                act(T.G1[:, C * b:C * b + C], w.indirect(T.LL[:, 0:12]), [rw, "LL"], [("G1", b, b + 1)])
+                cut("s")
+        for b in range(4):
+            w, rw = win(b)
+            tt(T.MX[:, C * b:C * b + C], w.indirect(T.LL[:, 12:24]), T.G1[:, C * b:C * b + C], A.max,
+               [rw, "LL", ("G1", b, b + 1)], [("MX", b, b + 1)])
+            cut("v")
+            if b > 0:
+                tt(T[Xn][:, b - 1:768:4], T.MX[:, C * b - C:C * b], bank(b - 1), A.add, [("MX", b - 1, b), ("ps", b - 1, b)],
+                   [Xn + "b%d" % (b - 1)])
+                cut("v")
+        tt(T[Xn][:, 3:768:4], T.MX[:, 3 * C:4 * C], bank(3), A.add, [("MX", 3, 4), ("ps", 3, 4)], [Xn + "b3"])
+
+    quant(T.qx2[:], T.sx2[:], T.X2[:], ["X2b%d" % b for b in range(4)], ["qx2"])
+    mm(4, T.qv[:], T.sv[:], T.qx2[:], T.sx2[:], ["qv", "qx2"])
+    dma("s", "doc", T.oc[:], T.qx2[:].bitcast(dt.uint8), ["qx2"], [])
+    for k, e in enumerate(("y", "s", "y", "s")):
+        dma(e, "ds%d" % k, T.osc[4 * k:4 * k + 4, :], T.sx2[32 * k:32 * k + 4, :], ["qx2"], [])
+    cp(T.Y[:], bank(4), [("ps", 4, 5)], ["Y"])
+    dma("y", "dy", T.y[:], T.Y[:], ["Y"], [])
+    g.wait_ge(T.sem.ls, sent[0])
+    for sem in SEMAPHORES:
+        if sem in last and not last[sem]["waited"]:
+            Q["g" if sem in DMAS else "t"].wait_ge(T.sem[sem], last[sem]["n"])

@@ -10,7 +10,7 @@ W64 = [278920.0, 4290.0, 65.0]
 KB0 = [0, 64, 192]
 XB0 = [0, 0, 128]
 TW = 1296
-NV = 5
+NV = 6
 X4, U8, U16, F32, B16, I32 = "float8_e4m3fn_x4", "uint8", "uint16", "float32", "bfloat16", "int32"
 
 SCRATCH = {}
@@ -24,15 +24,16 @@ for _n, _w, _d in [
     ("qw", 512, X4), ("sw", 512, U8), ("Z", 528, B16), ("qe", 512, X4), ("se", 512, U8),
     ("Tp", 768, B16), ("TB", 384, B16), ("RB", 384, B16), ("cm", 384, B16),
     ("pi", 4, I32), ("col", 16, F32), ("pat", 48, F32), ("tmp", 128, F32), ("c16", 12, F32), ("c16m", 12, F32),
-    ("cj", 12, F32), ("thr", 12, F32), ("w16m", 12, F32), ("w64m", 12, F32), ("tiem", 12, F32),
-    ("IO", 384, F32), ("MOD", 384, F32), ("ext", C, F32), ("ones", 768, B16), ("m16", C, B16), ("m64", 768, B16),
+    ("cj", 12, F32), ("thr", 12, F32), ("thc", 12, F32), ("wm", 24, F32), ("tiem", 12, F32),
+    ("PP", 36, F32), ("PM", 36, F32), ("PS", 36, F32),
+    ("IO", 384, F32), ("MOD", 384, F32), ("ext", C, F32), ("ones", 256, B16), ("m16", C, B16), ("m64", 256, B16),
     ("m8", C, F32), ("w16", C, F32), ("tie", C, F32), ("TE", 216, F32),
     ("PA", 384, F32), ("PB", 384, F32), ("V0", 384, F32), ("VA", 384, F32), ("VB", 384, F32),
     ("V0D", C, F32), ("VD", C, F32),
     ("RAW", C, F32), ("RAW2", C, F32), ("RK", C, F32), ("RE", C, F32), ("RX", 128, F32),
     ("sm", 192, F32), ("LS", 48, U16), ("LX", 24, U16), ("LR", 12, U16), ("LR2", 12, U16), ("LE", 12, U16),
     ("LY", 8, U16), ("LP", 12, U16), ("LL", 24, U16),
-    ("CMP", 960, B16), ("CNT", 960, B16), ("JK", 1344, B16), ("AC", 48, F32),
+    ("CMP", 1152, B16), ("CNT", 1152, B16), ("JK", 1344, B16), ("AC", 48, F32),
     ("U", C, F32), ("KB", 384, F32), ("XS", 320, F32), ("G", 128, F32), ("U1", 64, F32), ("EP", 128, F32),
     ("E", C, F32), ("O", C, F32), ("LV", C, F32), ("LW", C, F32), ("PR", C, F32),
     ("TAB", 4 * TW, F32), ("G1", 768, F32), ("MX", 768, F32), ("Y", C, F32),
@@ -41,7 +42,7 @@ for _n, _w, _d in [
 SCRATCH["BT"] = ("sbuf", [128, 12, 32], B16)
 SCRATCH["ps"] = ("psum", [128, 4096], F32)
 
-POOL = {"v": 40, "s": 30, "t": 10, "g": 10}
+POOL = {"v": 60, "s": 40, "t": 10, "g": 10}
 DMAS = ["dx", "du", "dv", "dwc", "dws", "dop", "doc", "ds0", "ds1", "ds2", "ds3", "dy"]
 SEMAPHORES = [e + str(i) for e in POOL for i in range(POOL[e])] + DMAS + ["ax0", "ax1", "al0", "al1", "ls"]
 
@@ -184,6 +185,8 @@ def rank_program(g, core, T, topo):
     col = lambda i: T.col[:, i:i + 1]
     cq, ch, cnh, c1q, cq1, ccj, cim, cmt, cM, cnM, cbm = [col(i) for i in range(11)]
     rc = lambda i: ("col", i, i + 1)
+    sm = lambda k: T.sm[:, 12 * k:12 * k + 12]
+    rs = lambda k: ("sm", 12 * k, 12 * k + 12)
 
     dma("y", "dx", T.X0[:], T.x[:], [], ["X0"])
     dma("s", "du", T.ut[:], T.u[:], [], ["ut"])
@@ -197,84 +200,108 @@ def rank_program(g, core, T, topo):
     cut("g")
     iota("IO", [[1, 384]], 0)
     cut("g")
-    ms(T.ones[:, 0:C], 1.0, [("ones", 0, C)])
+    ms(T.ones[:], 1.0, ["ones"])
     ms(T.Z[:], 0.0, ["Z"])
     cut("v")
-    for lo, hi, c in ((0, 16, 1.0), (16, 17, 0.0), (17, 24, 0.5), (24, 25, BIG), (25, 48, 1.0)):
-        ms(T.pat[:, lo:hi], c, [("pat", lo, hi)])
-    ms(T.tmp[:, 96:112], 0.5, [("tmp", 96, 112)])
-    ms(T.tmp[:, 112:128], 0.0, [("tmp", 112, 128)])
-    op("g", lambda: g.affine_select(T.Z[:, 3:515:4], T.ones[:, 0:128], [[-1, 128]], A.is_equal, 0.0, 0, 1),
-       [("ones", 0, C)], ["Z"])
     ts(T.pi[:, 2:3], T.pi[:, 0:1], 15, None, A.bitwise_and, None, [("pi", 0, 1)], [("pi", 2, 3)])
     ts(T.pi[:, 3:4], T.pi[:, 0:1], 4, 1, A.arith_shift_right, A.bitwise_and, [("pi", 0, 1)], [("pi", 3, 4)])
-    scan(T.V0[:, 0:16], T.tmp[:, 96:112], T.tmp[:, 112:128], 65536.0, A.mult, A.add, [("tmp", 96, 128)], [("V0", 0, 16)])
+    cut("v")
+    ms(T.tmp[:, 96:112], 0.5, [("tmp", 96, 112)])
+    ms(T.tmp[:, 112:128], 0.0, [("tmp", 112, 128)])
+    for lo, hi, c in ((0, 16, 1.0), (16, 17, 0.0)):
+        ms(T.pat[:, lo:hi], c, [("pat", lo, hi)])
+    cut("v")
     cp(T.col[:, 0:2], T.pi[:, 2:4], [("pi", 2, 4)], [("col", 0, 2)])
+    cut("v")
+    for lo, hi, c in ((17, 24, 0.5), (24, 25, BIG), (25, 48, 1.0)):
+        ms(T.pat[:, lo:hi], c, [("pat", lo, hi)])
+    cut("v")
+    op("g", lambda: g.affine_select(T.Z[:, 3:515:4], T.ones[:, 0:128], [[-1, 128]], A.is_equal, 0.0, 0, 1),
+       ["ones"], ["Z"])
+    scan(T.V0[:, 0:16], T.tmp[:, 96:112], T.tmp[:, 112:128], 65536.0, A.mult, A.add, [("tmp", 96, 128)], [("V0", 0, 16)])
     ts(cnh, ch, -1.0, 1.0, A.mult, A.add, [rc(1)], [rc(2)])
     ts(c1q, cq, -1.0, 1.0, A.mult, A.add, [rc(0)], [rc(3)])
-    ts(cq1, cq, 1.0, None, A.add, None, [rc(0)], [rc(4)])
     ts(ccj, ch, 1.0 / BIG, 0.5, A.max, A.mult, [rc(1)], [rc(5)])
+    ts(cq1, cq, 1.0, None, A.add, None, [rc(0)], [rc(4)])
+    cut("v")
     ts(cim, cq, 15.0, 1.0 / BIG, A.is_equal, A.max, [rc(0)], [rc(6)])
     ts(cmt, cq, 15.0, BIG, A.not_equal, A.mult, [rc(0)], [rc(7)])
     ts(T.tmp[:, 0:32], T.pat[:, 0:32], ch, None, A.mult, None, ["pat", rc(1)], [("tmp", 0, 32)])
+    cut("v")
     ts(T.tmp[:, 32:64], T.pat[:, 16:48], cnh, None, A.mult, None, ["pat", rc(2)], [("tmp", 32, 64)])
     ts(T.cj[:], T.c16[:], cq, ccj, A.add, A.mult, ["c16", rc(0), rc(5)], ["cj"])
-    ts(T.thr[:], T.c16[:], c1q, None, A.max, None, ["c16", rc(3)], ["thr"])
-    ts(cM, cmt, 1.0, None, A.max, None, [rc(7)], [rc(8)])
-    ts(cnM, cmt, 1.0, -1.0, A.max, A.mult, [rc(7)], [rc(9)])
+    ts(T.thr[:], T.c16[:], c1q, -0.002, A.max, A.add, ["c16", rc(3)], ["thr"])
+    cut("v")
     ts(T.tmp[:, 64:80], T.IO[:, 0:16], cq, None, A.not_equal, None, ["IO", rc(0)], [("tmp", 64, 80)])
     ts(T.tmp[:, 80:96], T.IO[:, 0:16], cq1, BIG, A.is_equal, A.mult, ["IO", rc(4)], [("tmp", 80, 96)])
+    ts(cM, cmt, 1.0, None, A.max, None, [rc(7)], [rc(8)])
+    ts(cnM, cmt, 1.0, -1.0, A.max, A.mult, [rc(7)], [rc(9)])
+    cut("v")
     tt(T.cm[:, 0:32], T.tmp[:, 0:32], T.tmp[:, 32:64], A.add, [("tmp", 0, 64)], [("cm", 0, 32)])
+    ts(sm(0), T.cj[:], 2.0 ** -70, None, A.max, None, ["cj"], [rs(0)])
+    cut("v")
+    ms(T.PM[:, 0:36:3], 0.0, ["PM0"])
+    ms(T.PM[:, 1:36:3], 1.0, ["PM1"])
+    ms(T.PM[:, 2:36:3], float(C), ["PM2"])
+    ms(T.PP[:, 0:36:3], -0.498046875 / C, ["PP0"])
+    cut("v")
     tt(T.ext[:, 0:16], T.tmp[:, 64:80], T.tmp[:, 80:96], A.add, [("tmp", 64, 96)], [("ext", 0, 16)])
+    op("v", lambda: g.vector.reciprocal(sm(1), sm(0)), [rs(0)], [rs(1)])
+    cut("v")
     quant(T.qu[:], T.su[:], T.ut[:], ["ut"], ["qu"])
     for n in ("V0", "VA", "VB"):
         act(T[n][:, C:384], T.IO[:, 0:C], ["IO"], [(n, C, 384)], scale=0.0)
     for n in ("PA", "PB"):
         act(T[n][:, C:384], T.IO[:, C:384], ["IO"], [(n, C, 384)])
-    for n, w in (("cm", 32), ("ext", 16), ("V0", 16)):
+    for n, w in (("cm", 32), ("V0", 16), ("ext", 16)):
         act(T[n][:, w:2 * w], T[n][:, 0:w], [(n, 0, w)], [(n, w, 2 * w)])
-    for n, w in (("cm", 32), ("ext", 16), ("V0", 16)):
+        cut("s")
+    for n, w in (("cm", 32), ("V0", 16), ("ext", 16)):
         act(T[n][:, 2 * w:4 * w], T[n][:, 0:2 * w], [(n, 0, 2 * w)], [(n, 2 * w, 4 * w)])
-    for n, w in (("cm", 32), ("ext", 16), ("V0", 16)):
+        cut("s")
+    for n, w in (("cm", 32), ("V0", 16), ("ext", 16)):
         act(T[n][:, 4 * w:8 * w], T[n][:, 0:4 * w], [(n, 0, 4 * w)], [(n, 4 * w, 8 * w)])
         act(T[n][:, 8 * w:12 * w], T[n][:, 0:4 * w], [(n, 0, 4 * w)], [(n, 8 * w, 12 * w)])
-    cut("s")
+        cut("s")
 
     def late_vector():
+        cut("v")
+        tt(T.thc[:], T.thr[:], sm(1), A.mult, ["thr", rs(1)], ["thc"])
         for b in range(4):
             quant(T.qe[:, 128 * b:128 * b + 128], T.se[:, 128 * b:128 * b + 128], T.Z[:, 3 - b:515 - b], ["Z"],
                   [("qe", b, b + 1)])
 
     def late_scalar():
-        act(T.ones[:, C:576], T.IO[:], ["IO"], [("ones", C, 576)], scale=0.0, bias=1.0)
-        act(T.ones[:, 576:768], T.IO[:, 0:C], ["IO"], [("ones", 576, 768)], scale=0.0, bias=1.0)
-        for k in range(4):
-            act(T.w16[:, 16 * k:16 * k + 16], T.ones[:, 0:16], [("ones", 0, C)], [("w16", 16 * k, 16 * k + 16)], scale=W16[k])
         act(T.V0D[:], T.V0[:, 0:C], [("V0", 0, C)], ["V0D"])
+        cut("s")
+        for k in range(4):
+            act(T.w16[:, 16 * k:16 * k + 16], T.ones[:, 0:16], ["ones"], [("w16", 16 * k, 16 * k + 16)], scale=W16[k])
         act(T.KB[:, 64:128], T.IO[:, 0:64], ["IO"], [("KB", 64, 128)], scale=0.0)
         act(T.KB[:, C:320], T.IO[:, 0:128], ["IO"], [("KB", C, 320)], scale=0.0)
-        act(T.XS[:, 0:64], T.IO[:, 0:64], ["IO"], [("XS", 0, 64)])
-        act(T.XS[:, 128:256], T.IO[:, 0:128], ["IO"], [("XS", 128, 256)])
+        cut("s")
 
     def late_scalar2(k):
         if k == 0:
+            for s in range(3):
+                act(T.wm[:, 12 + 4 * s:16 + 4 * s], T.ones[:, 0:4], ["ones"], ["wm%d" % (1 + s)], scale=W64[s])
             for s in (1, 2):
                 act(T.w16[:, 64 * s:64 * s + 64], T.w16[:, 0:64], [("w16", 0, 64)], [("w16", 64 * s, 64 * s + 64)])
         elif k == 1:
+            act(T.wm[:, 0:12], T.w16[:, 0:C:16], ["w16"], ["wm0"])
+            act(T.XS[:, 0:64], T.IO[:, 0:64], ["IO"], [("XS", 0, 64)])
+            act(T.XS[:, 128:256], T.IO[:, 0:128], ["IO"], [("XS", 128, 256)])
+        else:
             for s in range(3):
                 act(T.TE[:, 72 * s:72 * s + 72], T.IO[:, 0:72], ["IO"], [("TE", 72 * s, 72 * s + 72)], scale=W64[s],
                     bias=W64[s] * (-32.0 if s == 0 else 1.0))
-        else:
-            for s in range(3):
-                act(T.w64m[:, 4 * s:4 * s + 4], T.ones[:, 0:4], [("ones", 0, C)], [("w64m", 4 * s, 4 * s + 4)],
-                    scale=W64[s])
+        cut("s")
 
     def late_gpsimd():
         iota("c16m", [[0, 3], [16, 4]], 1)
         cut("g")
         mask("m16", C, 16)
         cut("g")
-        mask("m64", 768, 64)
+        mask("m64", 256, 64)
         cut("g")
         iota("tie", [[0, 3], [-1, 64]], -33)
         cut("g")
@@ -289,6 +316,7 @@ def rank_program(g, core, T, topo):
             k = c - NV
             act(T.JK[:, C * k:C * k + C], T.E[:], ["E", rraw, rc(9)], [("JK", C * k, C * k + C), ("AC", a0 + c, a0 + c + 1)],
                 scale=cnM, bias=raw(c), func=F.Sign, acc=T.AC[:, a0 + c:a0 + c + 1])
+        cut("s")
         for c in range(NV):
             ts(T.CMP[:, C * c:C * c + C], T.E[:], cM, raw(c), A.mult, A.is_gt, ["E", rraw, rc(8)], [("CMP", C * c, C * c + C)])
             if c % 2 == 1:
@@ -296,10 +324,8 @@ def rank_program(g, core, T, topo):
         cut("v")
         for c in range(NV):
             scan(T.CNT[:, C * c:C * c + C], T.ones[:, 0:C], T.CMP[:, C * c:C * c + C], 0.0, A.mult, A.add,
-                 [("ones", 0, C), ("CMP", C * c, C * c + C)], [("CNT", C * c, C * c + C)])
-
-    sm = lambda k: T.sm[:, 12 * k:12 * k + 12]
-    rs = lambda k: ("sm", 12 * k, 12 * k + 12)
+                 ["ones", ("CMP", C * c, C * c + C)], [("CNT", C * c, C * c + C)])
+        cut("v")
 
     for t in range(2):
         peer = T.cores[rank ^ (1 << t)]
@@ -323,12 +349,10 @@ def rank_program(g, core, T, topo):
         cut("t")
         op("v", lambda: g.vector.transpose(T.TB[:], T.BT[:]), ["BT"], ["TB"])
         scan(T.RB[:], T.cm[:], T.TB[:], 0.0, A.mult, A.add, ["cm", "TB"], ["RB"])
-        tt(sm(0), T.RB[:, 23:384:32], T.cj[:], A.mult, ["RB", "cj"], [rs(0)])
-        tt(sm(1), sm(0), T.thr[:], A.is_lt, [rs(0), "thr"], [rs(1)])
-        ts(sm(2), sm(0), -0.498046875, MAGIC, A.add, A.add, [rs(0)], [rs(2)])
-        ts(sm(3), sm(1), float(C), -MAGIC, A.mult, A.add, [rs(1)], [rs(3)])
-        tt(sm(4), sm(3), sm(2), A.add, [rs(2), rs(3)], [rs(4)])
-        cp(T.LS[:, 0:12], sm(4), [rs(4)], [("LS", 0, 12)])
+        tt(T.PP[:, 1:36:3], T.RB[:, 23:384:32], T.thc[:], A.is_lt, ["RB", "thc"], ["PP1"])
+        tt(T.PP[:, 2:36:3], T.RB[:, 23:384:32], T.cj[:], A.mult, ["RB", "cj"], ["PP2"])
+        scan(T.PS[:], T.PM[:], T.PP[:], 0.0, A.mult, A.add, ["PM0", "PM1", "PM2", "PP0", "PP1", "PP2"], ["PS"])
+        ts(T.LS[:, 0:12], T.PS[:, 2:36:3], MAGIC, -MAGIC, A.add, A.add, ["PS"], [("LS", 0, 12)])
         act(T.PA[:, 0:C], T.IO[:].indirect(T.LS[:, 0:12]), ["IO", ("LS", 0, 12)], [("PA", 0, C)])
         pn, vn = ["PA", "PB", "PA", "PB", "PA"], ["V0", "VA", "VB", "VA", "VB"]
         for r in range(4):
@@ -340,7 +364,11 @@ def rank_program(g, core, T, topo):
             cut("v")
             if r == 0 and t == 0:
                 scan(T.tmp[:, 0:16], T.ext[:, 0:16], T.V0[:, 0:16], 0.0, A.mult, A.add, ["ext", "V0"], [("tmp", 0, 16)])
+                ts(cbm, cM, -0.5, None, A.mult, None, [rc(8)], [rc(10)])
                 quant(T.qv[:], T.sv[:], T.vt[:], ["vt"], ["qv"])
+            if r == 2 and t == 0:
+                ts(T.wm[:], T.wm[:], cM, None, A.mult, None, [rc(8)], ["wm"] + ["wm%d" % k for k in range(4)])
+                ts(T.tiem[:], T.c16m[:], cq, cM, A.add, A.mult, ["c16m", rc(0), rc(8)], ["tiem"])
             if r < 3:
                 act(T.VD[:], T[vn[r + 1]][:, 0:C], [(vn[r + 1], 0, C)], ["VD"])
                 cut("s")
@@ -352,130 +380,190 @@ def rank_program(g, core, T, topo):
         for b in range(4):
             mm(4 + b, T.qe[:, 128 * b:128 * b + 128], T.se[:, 128 * b:128 * b + 128], T[lq][:], T[lp][:], [("qe", b, b + 1), lq])
             cut("t")
-        unwrap(T.RAW2[:], T.VB[:, 0:C], C, [("VB", 0, C)], ["RAW2"])
-        for c in range(12):
-            act(T.JK[:, 16 * c:16 * c + 16], T.VB[:, 16 * c:16 * c + 16], [("VB", 0, C), "RAW2", rc(9)],
-                [("JK", 16 * c, 16 * c + 16), ("AC", c, c + 1)], scale=cnM, bias=T.RAW2[:, 16 * c + 15:16 * c + 16],
-                func=F.Sign, acc=T.AC[:, c:c + 1])
-        ts(sm(5), T.RAW2[:, 15:C:16], T.tmp[:, 15:16], None, A.add, None, ["RAW2", ("tmp", 0, 16)], [rs(5)])
+        blk = lambda c: T.VB[:, 16 * c:16 * c + 16]
+        rvb = ("VB", 0, C)
+
+        def sign16(c, bias, rb):
+            act(T.JK[:, 16 * c:16 * c + 16], blk(c), [rvb, rb, rc(9)], [("JK", 16 * c, 16 * c + 16), ("AC", c, c + 1)],
+                scale=cnM, bias=bias, func=F.Sign, acc=T.AC[:, c:c + 1])
+
+        def enter16(cs):
+            for c in cs:
+                ts(T.CMP[:, 96 + 16 * c:112 + 16 * c], blk(c), cM, T.sm[:, 60 + c:61 + c], A.mult, A.is_lt,
+                   [rvb, rs(5), rc(8)], [("CMP", 96 + 16 * c, 112 + 16 * c)])
+            cut("v")
+
+        unwrap(T.RAW2[:], T.VB[:, 0:C], C, [rvb], ["RAW2"])
         cut("v")
         unwrap(T.RAW[:], T.PA[:, 0:C], C, [("PA", 0, C)], ["RAW"])
         cut("v")
-        for c in range(12):
-            ts(T.CMP[:, 16 * c:16 * c + 16], T.VB[:, 16 * c:16 * c + 16], cM, T.sm[:, 60 + c:61 + c], A.mult, A.is_lt,
-               [("VB", 0, C), rs(5), rc(8)], [("CMP", 16 * c, 16 * c + 16)])
+        for c in range(6):
+            sign16(c, T.RAW2[:, 16 * c + 15:16 * c + 16], "RAW2")
+        cut("s")
+        ts(sm(5), T.RAW2[:, 15:C:16], T.tmp[:, 15:16], cbm, A.add, A.add, ["RAW2", ("tmp", 0, 16), rc(10)], [rs(5)])
         cut("v")
+        for c in range(6, 12):
+            ts(T.CMP[:, 16 * c - 96:16 * c - 80], blk(c), cM, T.RAW2[:, 16 * c + 15:16 * c + 16], A.mult, A.is_le,
+               [rvb, "RAW2", rc(8)], [("CMP", 16 * c - 96, 16 * c - 80)])
+        cut("v")
+        for c in range(6, 12):
+            sign16(c, T.sm[:, 60 + c:61 + c], rs(5))
+        cut("s")
         ts(T.LX[:, 0:24:2], T.RAW[:, 15:C:16], cim, 0.25 - C, A.mult, A.add, ["RAW", rc(6)], ["LX"])
-        scan(T.CNT[:, 0:C], T.m16[:], T.CMP[:, 0:C], 0.0, A.mult, A.add, ["m16", ("CMP", 0, C)], [("CNT", 0, C)])
-        if t == 0:
-            ts(T.w16m[:], T.w16[:, 0:C:16], cM, None, A.mult, None, ["w16", rc(8)], ["w16m"])
         cut("v")
-        ts(T.LR[:], T.AC[:, 0:12], 0.5, 8.75, A.mult, A.add, [("AC", 0, 12)], ["LR"])
+        enter16((0, 1))
+        scan(T.CNT[:, 0:96], T.m16[:, 0:96], T.CMP[:, 0:96], 0.0, A.mult, A.add, ["m16", ("CMP", 0, 96)], [("CNT", 0, 96)])
+        cut("v")
+        enter16((2, 3))
+        ts(T.LR[:, 0:6], T.AC[:, 0:6], 0.5, 8.75, A.mult, A.add, [("AC", 0, 6)], [("LR", 0, 6)])
+        cp(T.LR[:, 6:12], T.CNT[:, 15:96:16], [("CNT", 0, 96)], [("LR", 6, 12)])
+        cut("v")
+        enter16((4, 5))
+        tt(T.U[:], T.IO[:, 0:24].indirect(T.LR[:]), T.w16[:], A.mult, ["IO", "LR", "w16"], ["U"])
+        cut("v")
         for s in range(3):
             o0 = KB0[s] + 64 * s
             ts(T.KB[:, o0:o0 + 16], T.IO[:, 0:24].indirect(T.LR[:, 4 * s:4 * s + 1]), W16[0], None, A.mult, None,
                ["IO", "LR"], [("KB", o0, o0 + 16)])
-        tt(T.U[:], T.IO[:, 0:24].indirect(T.LR[:]), T.w16[:], A.mult, ["IO", "LR", "w16"], ["U"])
+            cut("v")
+        scan(T.CNT[:, 96:C], T.m16[:, 0:96], T.CMP[:, 96:C], 0.0, A.mult, A.add, ["m16", ("CMP", 96, C)], [("CNT", 96, C)])
+        cut("v")
         for be in range(4):
             for s in (1, 2):
                 c = 4 * s + be
                 o0 = XB0[s] + 16 * c
                 act(T.XS[:, o0:o0 + 16], T.XS[:, XB0[s]:o0].indirect(T.LX[:, 2 * c:2 * c + 1]), [("XS", XB0[s], o0), "LX"],
                     [("XS", o0, o0 + 16)])
-        for b in range(2):
-            act(T.Tp[:, C * b:C * b + C], bank(4 + b), [("ps", 4 + b, 5 + b)], [("Tp", b, b + 1)])
+            cut("s")
+            if be < 2:
+                act(T.Tp[:, C * be:C * be + C], bank(4 + be), [("ps", 4 + be, 5 + be)], [("Tp", be, be + 1)])
+                cut("s")
         for be in range(1, 4):
             for s in range(3):
                 c = 4 * s + be
                 o0 = KB0[s] + 16 * c
                 tt(T.KB[:, o0:o0 + 16], T.KB[:, KB0[s]:o0].indirect(T.LX[:, 2 * c:2 * c + 1]), T.U[:, 16 * c:16 * c + 16],
                    A.add, [("KB", KB0[s], o0), "LX", "U"], [("KB", o0, o0 + 16)])
-            cut("v")
+                cut("v")
             if be == 1:
-                ts(sm(6), T.AC[:, 0:12], -0.5, -7.5, A.mult, A.add, [("AC", 0, 12)], [rs(6)])
+                ts(sm(6), T.LR[:], -1.0, 1.0, A.mult, A.add, ["LR"], [rs(6)])
+                cp(T.sm[:, 156:162], T.CNT[:, 111:C:16], [("CNT", 96, C)], [("sm", 156, 162)])
+                ts(T.sm[:, 162:168], T.AC[:, 6:12], 0.5, 8.0, A.mult, A.add, [("AC", 6, 12)], [("sm", 162, 168)])
             elif be == 2:
-                tt(sm(7), sm(6), T.CNT[:, 15:C:16], A.add, [rs(6), ("CNT", 0, C)], [rs(7)])
+                tt(sm(7), sm(6), sm(13), A.add, [rs(6), rs(13)], [rs(7)])
             else:
-                tt(sm(8), sm(7), T.w16m[:], A.mult, [rs(7), "w16m"], [rs(8)])
+                tt(sm(8), sm(7), T.wm[:, 0:12], A.mult, [rs(7), "wm"], [rs(8)])
             cut("v")
         live = lambda s: T.KB[:, KB0[s] + 64 * s:KB0[s] + 64 * s + 64]
         rlive = lambda s: ("KB", KB0[s] + 64 * s, KB0[s] + 64 * s + 64)
         for s in range(3):
             unwrap(T.RK[:, 64 * s:64 * s + 64], live(s), 64, [rlive(s)], [("RK", 64 * s, 64 * s + 64)])
-        for c in range(12):
-            act(T.JK[:, 64 * c:64 * c + 64], live(c // 4), [rlive(c // 4), "RK", rc(9)],
-                [("JK", 64 * c, 64 * c + 64), ("AC", 12 + c, 13 + c)], scale=cnM, bias=T.RK[:, 16 * c + 15:16 * c + 16],
-                func=F.Sign, acc=T.AC[:, 12 + c:13 + c])
-        tt(sm(9), T.RK[:, 15:C:16], sm(8), A.add, ["RK", rs(8)], [rs(9)])
-        cut("v")
+            cut("v")
+
+        def sign64(cs):
+            for c in cs:
+                s = c // 4
+                act(T.JK[:, 64 * c:64 * c + 64], live(s), [rlive(s), ("RK", 64 * s, 64 * s + 64), rc(9)],
+                    [("JK", 64 * c, 64 * c + 64), ("AC", 12 + c, 13 + c)], scale=cnM, bias=T.RK[:, 16 * c + 15:16 * c + 16],
+                    func=F.Sign, acc=T.AC[:, 12 + c:13 + c])
+            cut("s")
+
+        sign64(range(8))
         for s in (1, 2):
             o0 = XB0[s] + 64 * s
             unwrap(T.RX[:, 64 * s - 64:64 * s], T.XS[:, o0:o0 + 64], 64, [("XS", o0, o0 + 64)], [("RX", 64 * s - 64, 64 * s)])
         cut("v")
-        for c in range(12):
-            ts(T.CMP[:, 64 * c:64 * c + 64], live(c // 4), cM, T.sm[:, 108 + c:109 + c], A.mult, A.is_lt,
-               [rlive(c // 4), rs(9), rc(8)], [("CMP", 64 * c, 64 * c + 64)])
+        tt(sm(9), T.RK[:, 15:C:16], sm(8), A.add, ["RK", rs(8)], [rs(9)])
         cut("v")
         ts(T.LY[:], T.RX[:, 15:128:16], cim, 0.25, A.mult, A.add, ["RX", rc(6)], ["LY"])
-        scan(T.CNT[:, 0:768], T.m64[:], T.CMP[:, 0:768], 0.0, A.mult, A.add, ["m64", ("CMP", 0, 768)], [("CNT", 0, 768)])
         cut("v")
-        ts(T.LR2[:], T.AC[:, 12:24], 0.5, 32.75, A.mult, A.add, [("AC", 12, 24)], ["LR2"])
+        for s in (1, 2, 0):
+            for c in range(4 * s, 4 * s + 4):
+                ts(T.CMP[:, 64 * c:64 * c + 64], live(s), cM, T.sm[:, 108 + c:109 + c], A.mult, A.is_lt,
+                   [rlive(s), rs(9), rc(8)], [("CMP", 64 * c, 64 * c + 64)])
+            cut("v")
+        for s in (1, 2, 0):
+            lo_, hi_ = 256 * s, 256 * s + 256
+            if s == 0:
+                ts(T.LR2[:, 0:8], T.AC[:, 12:20], 0.5, 32.75, A.mult, A.add, [("AC", 12, 20)], ["LR2"])
+                cut("v")
+            scan(T.CNT[:, lo_:hi_], T.m64[:], T.CMP[:, lo_:hi_], 0.0, A.mult, A.add, ["m64", ("CMP", lo_, hi_)],
+                 [("CNT", lo_, hi_)])
+            cut("v")
+        cp(T.LE[:, 4:12], T.CNT[:, 319:768:64], [("CNT", 256, 768)], [("LE", 1, 3)])
         cut("v")
-        cp(T.LE[:], T.CNT[:, 63:768:64], [("CNT", 0, 768)], ["LE"])
+        cp(T.LE[:, 0:4], T.CNT[:, 63:256:64], [("CNT", 0, 256)], [("LE", 0, 1)])
+        cut("v")
+        cp(sm(13), T.CNT[:, 63:768:64], [("CNT", 0, 768)], [rs(13)])
+        cut("v")
         act(T.G[:, 0:64], T.IO[:, 0:72].indirect(T.LR2[:, 0:4]), ["IO", "LR2"], [("G", 0, 64)], scale=W64[0],
             bias=-33.0 * W64[0])
         act(T.U1[:], T.IO[:, 0:72].indirect(T.LR2[:, 4:8]), ["IO", "LR2"], ["U1"], scale=W64[1])
         cut("s")
+        sign64(range(8, 12))
         for b in range(2, 4):
             act(T.Tp[:, C * b:C * b + C], bank(4 + b), [("ps", 4 + b, 5 + b)], [("Tp", b, b + 1)])
-        for s in (1, 2, 0):
+        cut("s")
+
+        def enter64(s):
             out, ro = (T.E[:, 0:64], ("E", 0, 64)) if s == 0 else (T.EP[:, 64 * s - 64:64 * s], ("EP", 64 * s - 64, 64 * s))
             tt(out, T.TE[:, 72 * s:72 * s + 72].indirect(T.LE[:, 4 * s:4 * s + 4]), T.tie[:, 64 * s:64 * s + 64], A.add,
-               ["TE", "LE", "tie"], [ro])
-        cut("v")
+               ["TE", ("LE", s, s + 1), "tie"], [ro])
+            cut("v")
+
+        enter64(1)
+        enter64(2)
         tt(T.G[:, 64:128], T.G[:, 0:64].indirect(T.LY[:, 0:4]), T.U1[:], A.add, [("G", 0, 64), "LY", "U1"], [("G", 64, 128)])
         cut("v")
-        tt(T.E[:, 64:128], T.G[:, 0:64].indirect(T.LY[:, 0:4]), T.EP[:, 0:64], A.add, [("G", 0, 64), "LY", "EP"],
+        enter64(0)
+        tt(T.E[:, 64:128], T.G[:, 0:64].indirect(T.LY[:, 0:4]), T.EP[:, 0:64], A.add, [("G", 0, 64), "LY", ("EP", 0, 64)],
            [("E", 64, 128)])
+        cut("v")
         tt(T.E[:, 128:C], T.G[:, 0:128].indirect(T.LY[:, 4:8]), T.EP[:, 64:128], A.add, ["G", "LY", "EP"], [("E", 128, C)])
         cut("v")
-        ts(sm(6), T.AC[:, 12:24], -0.5, -31.5, A.mult, A.add, [("AC", 12, 24)], [rs(6)])
-        unwrap(T.RE[:], T.E[:], C, ["E"], ["RE"])
+        unwrap(T.RE[:, 0:128], T.E[:, 0:128], 128, [("E", 0, 128)], [("RE", 0, 128)])
         cut("v")
-        tt(sm(7), sm(6), T.CNT[:, 63:768:64], A.add, [rs(6), ("CNT", 0, 768)], [rs(7)])
+        unwrap(T.RE[:, 128:C], T.E[:, 128:C], 64, [("E", 128, C)], [("RE", 128, C)])
+        cut("v")
         count_all(lambda c: T.RE[:, 16 * c + 15:16 * c + 16], "RE", 24)
-        cp(T.LP[:, 0:NV], T.CNT[:, C - 1:NV * C:C], [("CNT", 0, NV * C)], [("LP", 0, NV)])
+        ts(sm(6), T.AC[:, 12:24], -0.5, -31.5, A.mult, A.add, [("AC", 12, 24)], [rs(6)])
+        tt(sm(10), T.RE[:, 15:C:16], T.tiem[:], A.add, ["RE", "tiem"], [rs(10)])
+        cut("v")
         ts(T.LP[:, NV:12], T.AC[:, 24 + NV:36], -0.5, 95.75, A.mult, A.add, [("AC", 24, 36)], [("LP", NV, 12)])
+        cp(T.LP[:, 0:NV], T.CNT[:, C - 1:NV * C:C], [("CNT", 0, NV * C)], [("LP", 0, NV)])
+        cut("v")
+        tt(sm(7), sm(6), sm(13), A.add, [rs(6), rs(13)], [rs(7)])
+        cp(T.LV[:, 0:8 * NV:8], T.CNT[:, C - 1:NV * C:C], [("CNT", 0, NV * C)], ["LVp"])
+        ts(T.LV[:, 8 * NV:96:8], T.AC[:, 24 + NV:36], -0.5, 95.5, A.mult, A.add, [("AC", 24, 36)], ["LVq"])
+        cut("v")
         if t == 1:
             act(T.PR[:], T.MOD[:].indirect(T.LS[:, 0:12]), ["MOD", ("LS", 0, 12)], ["PR"])
             cut("s")
         cp(T.O[:].indirect(T.LP[:]), T.IO[:, 0:C], ["IO", "LP"], ["O"])
         cut("v")
-        cp(T.LV[:, 0:8 * NV:8], T.CNT[:, C - 1:NV * C:C], [("CNT", 0, NV * C)], ["LVp"])
+        tt(sm(8), sm(7), T.wm[:, 12:24], A.mult, [rs(7), "wm"], [rs(8)])
+        cut("v")
         unwrap(T.RAW[:], T.O[:], C, ["O"], ["RAW"])
         cut("v")
-        if t == 0:
-            ts(T.w64m[:], T.w64m[:], cM, None, A.mult, None, ["w64m", rc(8)], ["w64m"])
-            ts(T.tiem[:], T.c16m[:], cq, cM, A.add, A.mult, ["c16m", rc(0), rc(8)], ["tiem"])
-            cut("v")
+        tt(sm(11), sm(10), sm(8), A.subtract, [rs(10), rs(8)], [rs(11)])
+        cut("v")
         ts(T[ol][:], T.RAW[:, 15:C:16], cim, 0.25, A.mult, A.add, ["RAW", rc(6)], [ol])
         send(peer, T[lo][:], T[ol][:], "al%d" % t, [ol])
         arrival(peer, "al%d" % t, 1, [lo])
         if t == 1:
             dma("y", "dop", T.op[:], T.PR[0:128:16, :], ["PR"], [])
-        tt(sm(8), sm(7), T.w64m[:], A.mult, [rs(7), "w64m"], [rs(8)])
-        tt(sm(10), T.RE[:, 15:C:16], T.tiem[:], A.add, ["RE", "tiem"], [rs(10)])
-        ts(T.LV[:, 8 * NV:96:8], T.AC[:, 24 + NV:36], -0.5, 95.5, A.mult, A.add, [("AC", 24, 36)], ["LVq"])
-        tt(sm(11), sm(10), sm(8), A.subtract, [rs(10), rs(8)], [rs(11)])
+        cut("v")
         count_all(lambda c: T.sm[:, 132 + c:133 + c], rs(11), 36)
-        ts(T.LV[:, 96:96 + 8 * NV:8], T.CNT[:, C - 1:NV * C:C], -1.0, None, A.add, None, [("CNT", 0, NV * C)], ["LVe"])
         ts(T.LV[:, 96 + 8 * NV:C:8], T.AC[:, 36 + NV:48], -0.5, 95.0, A.mult, A.add, [("AC", 36, 48)], ["LVf"])
+        ts(T.LV[:, 96:96 + 8 * NV:8], T.CNT[:, C - 1:NV * C:C], -1.0, None, A.add, None, [("CNT", 0, NV * C)], ["LVe"])
         cut("v")
         for b in (2, 3):
             act(T[Bt][:, b:768:4], T.Tp[:, C * b:C * b + C].indirect(T[lo][:]), [("Tp", b, b + 1), lo], [Bt + "b%d" % b])
-        tt(sm(12), T.LV[:, 96:C:8], T.LV[:, 0:96:8], A.subtract, ["LVp", "LVq", "LVe", "LVf"], [rs(12)])
         for b in (0, 1):
             cp(T[Bt][:, b:768:4], T.Tp[:, C * b:C * b + C].indirect(T[lo][:]), [("Tp", b, b + 1), lo], [Bt + "b%d" % b])
+        cut("v")
+        tt(sm(12), T.LV[:, 96:C:8], T.LV[:, 0:96:8], A.subtract, ["LVp", "LVq", "LVe", "LVf"], [rs(12)])
+        cut("v")
         quant(T[qf][:], T[sf][:], T[Bt][:], [Bt + "b%d" % b for b in range(4)], [qf])
         for b in range(4):
             mm(4 + b, T.qw[:, 128 * b:128 * b + 128], T.sw[:, 128 * b:128 * b + 128], T[qf][:], T[sf][:], ["qw", "sw", qf])
@@ -500,32 +588,43 @@ def rank_program(g, core, T, topo):
             return T.TAB[:, TW * b:TW * b + off[8]], ("TAB", TW * b, TW * b + off[8])
 
         Xn = "X%d" % (t + 1)
-        for pair in ((0, 1), (2, 3)):
-            for k in range(1, 8):
-                for b in pair:
-                    level(b, k)
-                if pair[0] == 0 and k == 1:
-                    scan(T.LW[:], T.m8[:], T.LV[:], 0.0, A.mult, A.add,
-                         ["m8", "LVp", "LVq", "LVe", "LVf"] + ["LV%d" % m for m in range(1, 8)] + ["LU%d" % m for m in range(1, 8)],
-                         ["LW"])
-                    cut("v")
-                if pair[0] == 0 and k == 2:
-                    cp(T.LL[:], T.LW[:, 7:C:8], ["LW"], ["LL"])
-                    cut("v")
-            for b in pair:
-                w, rw = win(b)
-                act(T.G1[:, C * b:C * b + C], w.indirect(T.LL[:, 0:12]), [rw, "LL"], [("G1", b, b + 1)])
-                cut("s")
-        for b in range(4):
+
+        def pick(b):
             w, rw = win(b)
             tt(T.MX[:, C * b:C * b + C], w.indirect(T.LL[:, 12:24]), T.G1[:, C * b:C * b + C], A.max,
                [rw, "LL", ("G1", b, b + 1)], [("MX", b, b + 1)])
             cut("v")
-            if b > 0:
-                tt(T[Xn][:, b - 1:768:4], T.MX[:, C * b - C:C * b], bank(b - 1), A.add, [("MX", b - 1, b), ("ps", b - 1, b)],
-                   [Xn + "b%d" % (b - 1)])
+
+        def plus(b):
+            tt(T[Xn][:, b:768:4], T.MX[:, C * b:C * b + C], bank(b), A.add, [("MX", b, b + 1), ("ps", b, b + 1)],
+               [Xn + "b%d" % b])
+            cut("v")
+
+        for i in range(1, 11):
+            if i == 10:
+                pick(0)
+            for b in range(4):
+                if 1 <= i - b <= 7:
+                    level(b, i - b)
+                if i - b == 7:
+                    w, rw = win(b)
+                    act(T.G1[:, C * b:C * b + C], w.indirect(T.LL[:, 0:12]), [rw, "LL"], [("G1", b, b + 1)])
+                    cut("s")
+            if i == 1:
+                scan(T.LW[:], T.m8[:], T.LV[:], 0.0, A.mult, A.add,
+                     ["m8", "LVp", "LVq", "LVe", "LVf"] + ["LV%d" % m for m in range(1, 8)] + ["LU%d" % m for m in range(1, 8)],
+                     ["LW"])
                 cut("v")
-        tt(T[Xn][:, 3:768:4], T.MX[:, 3 * C:4 * C], bank(3), A.add, [("MX", 3, 4), ("ps", 3, 4)], [Xn + "b3"])
+            if i == 2:
+                cp(T.LL[:], T.LW[:, 7:C:8], ["LW"], ["LL"])
+                cut("v")
+        pick(1)
+        plus(0)
+        pick(2)
+        plus(1)
+        pick(3)
+        plus(2)
+        plus(3)
 
     quant(T.qx2[:], T.sx2[:], T.X2[:], ["X2b%d" % b for b in range(4)], ["qx2"])
     mm(4, T.qv[:], T.sv[:], T.qx2[:], T.sx2[:], ["qv", "qx2"])

@@ -3,12 +3,14 @@ from concourse.mybir import dt, AluOpType, ActivationFunctionType
 A = AluOpType
 F = ActivationFunctionType
 C = 192
+H = 96
 BIG = 2.0 ** 60
 MAGIC = 12582912.0
 W16 = [4913.0, 289.0, 17.0, 1.0]
 W64 = [278920.0, 4290.0, 65.0]
 KB0 = [0, 64, 192]
 XB0 = [0, 0, 128]
+HB = [0, 192, 480]
 TW = 1296
 NV = 6
 X4, U8, U16, F32, B16, I32 = "float8_e4m3fn_x4", "uint8", "uint16", "float32", "bfloat16", "int32"
@@ -22,16 +24,16 @@ for _n, _w, _d in [
     ("Bt0", 768, B16), ("Bt1", 768, B16), ("qf0", C, X4), ("qf1", C, X4), ("sf0", C, U8), ("sf1", C, U8),
     ("ut", 512, B16), ("vt", 512, B16), ("qu", 128, X4), ("su", 128, U8), ("qv", 128, X4), ("sv", 128, U8),
     ("qw", 512, X4), ("sw", 512, U8), ("Z", 528, B16), ("qe", 512, X4), ("se", 512, U8),
-    ("Tp", 768, B16), ("TB", 384, B16), ("RB", 384, B16), ("cm", 384, B16),
+    ("Tp", 768, B16), ("TB", 384, B16), ("RB", 384, B16), ("cm", C, B16),
     ("pi", 4, I32), ("col", 16, F32), ("pat", 48, F32), ("tmp", 128, F32), ("c16", 12, F32), ("c16m", 12, F32),
     ("cj", 12, F32), ("thr", 12, F32), ("thc", 12, F32), ("wm", 24, F32), ("tiem", 12, F32),
     ("PP", 36, F32), ("PM", 36, F32), ("PS", 36, F32),
-    ("IO", 384, F32), ("MOD", 384, F32), ("ext", C, F32), ("ones", 256, B16), ("m16", C, B16), ("m64", 256, B16),
+    ("IO", 288, F32), ("MOD", 480, F32), ("ext", C, F32), ("ones", 256, B16), ("m16", H, B16), ("m64", 256, B16),
     ("m8", C, F32), ("w16", C, F32), ("tie", C, F32), ("TE", 216, F32),
-    ("PA", 384, F32), ("PB", 384, F32), ("V0", 384, F32), ("VA", 384, F32), ("VB", 384, F32),
-    ("V0D", C, F32), ("VD", C, F32),
+    ("PA", 480, F32), ("PB", 480, F32), ("V0", 480, F32), ("VA", 480, F32), ("VB", 480, F32),
+    ("V0D", H, F32), ("VD", C, F32),
     ("RAW", C, F32), ("RAW2", C, F32), ("RK", C, F32), ("RE", C, F32), ("RX", 128, F32),
-    ("sm", 192, F32), ("LS", 48, U16), ("LX", 24, U16), ("LR", 12, U16), ("LR2", 12, U16), ("LE", 12, U16),
+    ("sm", 192, F32), ("LS", 24, U16), ("LX", 24, U16), ("LR", 12, U16), ("LR2", 12, U16), ("LE", 12, U16),
     ("LY", 8, U16), ("LP", 12, U16), ("LL", 24, U16),
     ("CMP", 1152, B16), ("CNT", 1152, B16), ("JK", 1344, B16), ("AC", 48, F32),
     ("U", C, F32), ("KB", 384, F32), ("XS", 320, F32), ("G", 128, F32), ("U1", 64, F32), ("EP", 128, F32),
@@ -42,7 +44,7 @@ for _n, _w, _d in [
 SCRATCH["BT"] = ("sbuf", [128, 12, 32], B16)
 SCRATCH["ps"] = ("psum", [128, 4096], F32)
 
-POOL = {"v": 60, "s": 40, "t": 10, "g": 10}
+POOL = {"v": 60, "s": 40, "t": 10, "g": 12}
 DMAS = ["dx", "du", "dv", "dwc", "dws", "dop", "doc", "ds0", "ds1", "ds2", "ds3", "dy"]
 SEMAPHORES = [e + str(i) for e in POOL for i in range(POOL[e])] + DMAS + ["ax0", "ax1", "al0", "al1", "ls"]
 
@@ -159,8 +161,9 @@ def rank_program(g, core, T, topo):
         op("t", lambda: g.tensor.matmul_mx(T.ps[:, 512 * bank:512 * bank + C], lq, lsc, rq, rs, True, True),
            reads, [("ps", bank, bank + 1)])
 
-    def iota(name, pattern, base):
-        op("g", lambda: g.iota(T[name][:], pattern, base, 0, allow_small_or_imprecise_dtypes=True), [], [name])
+    def iota(name, lo, hi, pattern, base):
+        op("g", lambda: g.iota(T[name][:, lo:hi], pattern, base, 0, allow_small_or_imprecise_dtypes=True), [],
+           [(name, lo, hi)])
 
     def mask(name, n, period):
         op("g", lambda: g.affine_select(T[name][:], T.ones[:, 0:n], [[0, n // period], [1, period]], A.not_equal,
@@ -196,9 +199,9 @@ def rank_program(g, core, T, topo):
 
     op("g", lambda: g.iota(T.pi[:, 0:1], [[0, 1]], 0, 1), [], [("pi", 0, 1)])
     cut("g")
-    iota("c16", [[16, 12]], 0)
+    iota("c16", 0, 12, [[16, 12]], 0)
     cut("g")
-    iota("IO", [[1, 384]], 0)
+    iota("IO", 0, 288, [[1, 288]], 0)
     cut("g")
     ms(T.ones[:], 1.0, ["ones"])
     ms(T.Z[:], 0.0, ["Z"])
@@ -242,71 +245,89 @@ def rank_program(g, core, T, topo):
     cut("v")
     ms(T.PM[:, 0:36:3], 0.0, ["PM0"])
     ms(T.PM[:, 1:36:3], 1.0, ["PM1"])
-    ms(T.PM[:, 2:36:3], float(C), ["PM2"])
-    ms(T.PP[:, 0:36:3], -0.498046875 / C, ["PP0"])
     cut("v")
     tt(T.ext[:, 0:16], T.tmp[:, 64:80], T.tmp[:, 80:96], A.add, [("tmp", 64, 96)], [("ext", 0, 16)])
     op("v", lambda: g.vector.reciprocal(sm(1), sm(0)), [rs(0)], [rs(1)])
     cut("v")
     quant(T.qu[:], T.su[:], T.ut[:], ["ut"], ["qu"])
     for n in ("V0", "VA", "VB"):
-        act(T[n][:, C:384], T.IO[:, 0:C], ["IO"], [(n, C, 384)], scale=0.0)
-    for n in ("PA", "PB"):
-        act(T[n][:, C:384], T.IO[:, C:384], ["IO"], [(n, C, 384)])
+        act(T[n][:, H:C], T.IO[:, 0:H], ["IO"], [(n, H, C)], scale=0.0)
+        act(T[n][:, 288:480], T.IO[:, 0:C], ["IO"], [(n, 288, 480)], scale=0.0)
     for n, w in (("cm", 32), ("V0", 16), ("ext", 16)):
         act(T[n][:, w:2 * w], T[n][:, 0:w], [(n, 0, w)], [(n, w, 2 * w)])
         cut("s")
     for n, w in (("cm", 32), ("V0", 16), ("ext", 16)):
-        act(T[n][:, 2 * w:4 * w], T[n][:, 0:2 * w], [(n, 0, 2 * w)], [(n, 2 * w, 4 * w)])
+        for k in (2, 4):
+            act(T[n][:, k * w:(k + 2) * w], T[n][:, 0:2 * w], [(n, 0, 2 * w)], [(n, k * w, (k + 2) * w)])
         cut("s")
-    for n, w in (("cm", 32), ("V0", 16), ("ext", 16)):
-        act(T[n][:, 4 * w:8 * w], T[n][:, 0:4 * w], [(n, 0, 4 * w)], [(n, 4 * w, 8 * w)])
-        act(T[n][:, 8 * w:12 * w], T[n][:, 0:4 * w], [(n, 0, 4 * w)], [(n, 8 * w, 12 * w)])
-        cut("s")
+    for n in ("PA", "PB"):
+        act(T[n][:, H:C], T.IO[:, H:C], ["IO"], [(n, H, C)])
+        act(T[n][:, 288:480], T.IO[:, H:288], ["IO"], [(n, 288, 480)])
+    cut("s")
+    act(T.V0[:, C:288], T.V0[:, 0:H], [("V0", 0, H)], [("V0", C, 288)])
+    act(T.V0D[:], T.V0[:, 0:H], [("V0", 0, H)], ["V0D"])
+    act(T.ext[:, H:C], T.ext[:, 0:H], [("ext", 0, H)], [("ext", H, C)])
+    cut("s")
 
     def late_vector():
         cut("v")
         tt(T.thc[:], T.thr[:], sm(1), A.mult, ["thr", rs(1)], ["thc"])
-        for b in range(4):
-            quant(T.qe[:, 128 * b:128 * b + 128], T.se[:, 128 * b:128 * b + 128], T.Z[:, 3 - b:515 - b], ["Z"],
-                  [("qe", b, b + 1)])
+        ms(T.PM[:, 2:18:3], float(H), ["PM2"])
+        ms(T.PM[:, 20:36:3], float(C), ["PM3"])
+        ms(T.PP[:, 0:18:3], -0.498046875 / H, ["PP0"])
+        ms(T.PP[:, 18:36:3], -(H + 0.498046875) / C, ["PP3"])
+        cut("v")
+
+    def late_vector2(k):
+        if k < 2:
+            for b in (2 * k, 2 * k + 1):
+                quant(T.qe[:, 128 * b:128 * b + 128], T.se[:, 128 * b:128 * b + 128], T.Z[:, 3 - b:515 - b], ["Z"],
+                      [("qe", b, b + 1)])
+        elif k == 2:
+            scan(T.tmp[:, 0:16], T.ext[:, 0:16], T.V0D[:, 0:16], 0.0, A.mult, A.add, ["ext", "V0D"], [("tmp", 0, 16)])
+            ts(cbm, cM, -0.5, None, A.mult, None, [rc(8)], [rc(10)])
+        else:
+            ts(T.wm[:], T.wm[:], cM, None, A.mult, None, [rc(8)], ["wm"] + ["wm%d" % i for i in range(7)])
+            ts(T.tiem[:], T.c16m[:], cq, cM, A.add, A.mult, ["c16m", rc(0), rc(8)], ["tiem"])
+        cut("v")
 
     def late_scalar():
-        act(T.V0D[:], T.V0[:, 0:C], [("V0", 0, C)], ["V0D"])
-        cut("s")
         for k in range(4):
             act(T.w16[:, 16 * k:16 * k + 16], T.ones[:, 0:16], ["ones"], [("w16", 16 * k, 16 * k + 16)], scale=W16[k])
+            act(T.wm[:, k:12:4], T.ones[:, 0:3], ["ones"], ["wm%d" % (3 + k)], scale=W16[k])
+        for s in range(3):
+            act(T.wm[:, 12 + 4 * s:16 + 4 * s], T.ones[:, 0:4], ["ones"], ["wm%d" % s], scale=W64[s])
+        cut("s")
+
+    def late_scalar2():
+        for s in (1, 2):
+            act(T.w16[:, 64 * s:64 * s + 64], T.w16[:, 0:64], [("w16", 0, 64)], [("w16", 64 * s, 64 * s + 64)])
         act(T.KB[:, 64:128], T.IO[:, 0:64], ["IO"], [("KB", 64, 128)], scale=0.0)
         act(T.KB[:, C:320], T.IO[:, 0:128], ["IO"], [("KB", C, 320)], scale=0.0)
         cut("s")
 
-    def late_scalar2(k):
-        if k == 0:
-            for s in range(3):
-                act(T.wm[:, 12 + 4 * s:16 + 4 * s], T.ones[:, 0:4], ["ones"], ["wm%d" % (1 + s)], scale=W64[s])
-            for s in (1, 2):
-                act(T.w16[:, 64 * s:64 * s + 64], T.w16[:, 0:64], [("w16", 0, 64)], [("w16", 64 * s, 64 * s + 64)])
-        elif k == 1:
-            act(T.wm[:, 0:12], T.w16[:, 0:C:16], ["w16"], ["wm0"])
-            act(T.XS[:, 0:64], T.IO[:, 0:64], ["IO"], [("XS", 0, 64)])
-            act(T.XS[:, 128:256], T.IO[:, 0:128], ["IO"], [("XS", 128, 256)])
-        else:
-            for s in range(3):
-                act(T.TE[:, 72 * s:72 * s + 72], T.IO[:, 0:72], ["IO"], [("TE", 72 * s, 72 * s + 72)], scale=W64[s],
-                    bias=W64[s] * (-32.0 if s == 0 else 1.0))
+    def late_scalar3():
+        for s in range(3):
+            act(T.TE[:, 72 * s:72 * s + 72], T.IO[:, 0:72], ["IO"], [("TE", 72 * s, 72 * s + 72)], scale=W64[s],
+                bias=W64[s] * (-32.0 if s == 0 else 1.0))
         cut("s")
 
     def late_gpsimd():
-        iota("c16m", [[0, 3], [16, 4]], 1)
+        iota("c16m", 0, 12, [[0, 3], [16, 4]], 1)
         cut("g")
-        mask("m16", C, 16)
+        mask("m16", H, 16)
+        cut("g")
+        iota("XS", 0, 64, [[1, 64]], 0)
+        iota("XS", 128, 256, [[1, 128]], 0)
         cut("g")
         mask("m64", 256, 64)
         cut("g")
-        iota("tie", [[0, 3], [-1, 64]], -33)
+        iota("tie", 0, C, [[0, 3], [-1, 64]], -33)
         cut("g")
         mask("m8", C, 8)
-        iota("MOD", [[0, 2], [1, C]], 0)
+        iota("MOD", 0, C, [[0, 2], [1, H]], 0)
+        iota("MOD", C, 288, [[1, H]], H)
+        iota("MOD", 288, 480, [[1, C]], 0)
 
     def unwrap(out, row, n, reads, writes):
         scan(out, T.ext[:, 0:n], row, 0.0, A.mult, A.add, ["ext"] + reads, writes)
@@ -314,11 +335,11 @@ def rank_program(g, core, T, topo):
     def count_all(raw, rraw, a0):
         for c in range(NV, 12):
             k = c - NV
-            act(T.JK[:, C * k:C * k + C], T.E[:], ["E", rraw, rc(9)], [("JK", C * k, C * k + C), ("AC", a0 + c, a0 + c + 1)],
+            act(T.JK[:, C * k:C * k + C], T.E[:], ["E", rraw(c), rc(9)], [("JK", C * k, C * k + C), ("AC", a0 + c, a0 + c + 1)],
                 scale=cnM, bias=raw(c), func=F.Sign, acc=T.AC[:, a0 + c:a0 + c + 1])
         cut("s")
         for c in range(NV):
-            ts(T.CMP[:, C * c:C * c + C], T.E[:], cM, raw(c), A.mult, A.is_gt, ["E", rraw, rc(8)], [("CMP", C * c, C * c + C)])
+            ts(T.CMP[:, C * c:C * c + C], T.E[:], cM, raw(c), A.mult, A.is_gt, ["E", rraw(c), rc(8)], [("CMP", C * c, C * c + C)])
             if c % 2 == 1:
                 cut("v")
         cut("v")
@@ -326,6 +347,11 @@ def rank_program(g, core, T, topo):
             scan(T.CNT[:, C * c:C * c + C], T.ones[:, 0:C], T.CMP[:, C * c:C * c + C], 0.0, A.mult, A.add,
                  ["ones", ("CMP", C * c, C * c + C)], [("CNT", C * c, C * c + C)])
         cut("v")
+
+    hw = lambda n, h: T[n][:, HB[h]:HB[h + 1]]
+    hl = lambda n, h: T[n][:, HB[h]:HB[h] + H]
+    rw_ = lambda n, h: (n, HB[h], HB[h + 1])
+    rl_ = lambda n, h: (n, HB[h], HB[h] + H)
 
     for t in range(2):
         peer = T.cores[rank ^ (1 << t)]
@@ -342,91 +368,126 @@ def rank_program(g, core, T, topo):
             late_vector()
             late_scalar()
             late_gpsimd()
-        for k in range(2):
-            ts(T.BT[:, :, 16 * k:16 * k + 16], bank(4), 0.0, None, A.is_gt, None, [("ps", 4, 5)], [("BT", k, k + 1)])
-        for b in range(4):
-            mm(b, T.qe[:, 128 * b:128 * b + 128], T.se[:, 128 * b:128 * b + 128], T[qx][:], T[sx][:], [("qe", b, b + 1), qx])
-        cut("t")
-        op("v", lambda: g.vector.transpose(T.TB[:], T.BT[:]), ["BT"], ["TB"])
-        scan(T.RB[:], T.cm[:], T.TB[:], 0.0, A.mult, A.add, ["cm", "TB"], ["RB"])
-        tt(T.PP[:, 1:36:3], T.RB[:, 23:384:32], T.thc[:], A.is_lt, ["RB", "thc"], ["PP1"])
-        tt(T.PP[:, 2:36:3], T.RB[:, 23:384:32], T.cj[:], A.mult, ["RB", "cj"], ["PP2"])
-        scan(T.PS[:], T.PM[:], T.PP[:], 0.0, A.mult, A.add, ["PM0", "PM1", "PM2", "PP0", "PP1", "PP2"], ["PS"])
-        ts(T.LS[:, 0:12], T.PS[:, 2:36:3], MAGIC, -MAGIC, A.add, A.add, ["PS"], [("LS", 0, 12)])
-        act(T.PA[:, 0:C], T.IO[:].indirect(T.LS[:, 0:12]), ["IO", ("LS", 0, 12)], [("PA", 0, C)])
-        pn, vn = ["PA", "PB", "PA", "PB", "PA"], ["V0", "VA", "VB", "VA", "VB"]
-        for r in range(4):
-            L, rl = T.LS[:, 12 * r:12 * r + 12], ("LS", 12 * r, 12 * r + 12)
-            own = "V0D" if r == 0 else "VD"
-            act(T[pn[r + 1]][:, 0:C], T[pn[r]][:].indirect(L), [pn[r], rl], [(pn[r + 1], 0, C)])
-            cut("s")
-            tt(T[vn[r + 1]][:, 0:C], T[vn[r]][:].indirect(L), T[own][:], A.add, [vn[r], own, rl], [(vn[r + 1], 0, C)])
+        for h in range(2):
+            for k in range(2):
+                ts(T.BT[:, 6 * h:6 * h + 6, 16 * k:16 * k + 16], T.ps[:, 2048 + H * h:2048 + H * h + H], 0.0, None, A.is_gt,
+                   None, [("ps", 4, 5)], [("BT", 2 * h + k, 2 * h + k + 1)])
             cut("v")
-            if r == 0 and t == 0:
-                scan(T.tmp[:, 0:16], T.ext[:, 0:16], T.V0[:, 0:16], 0.0, A.mult, A.add, ["ext", "V0"], [("tmp", 0, 16)])
-                ts(cbm, cM, -0.5, None, A.mult, None, [rc(8)], [rc(10)])
-                quant(T.qv[:], T.sv[:], T.vt[:], ["vt"], ["qv"])
-            if r == 2 and t == 0:
-                ts(T.wm[:], T.wm[:], cM, None, A.mult, None, [rc(8)], ["wm"] + ["wm%d" % k for k in range(4)])
-                ts(T.tiem[:], T.c16m[:], cq, cM, A.add, A.mult, ["c16m", rc(0), rc(8)], ["tiem"])
-            if r < 3:
-                act(T.VD[:], T[vn[r + 1]][:, 0:C], [(vn[r + 1], 0, C)], ["VD"])
+        for h in range(2):
+            op("v", lambda: g.vector.transpose(T.TB[:, C * h:C * h + C], T.BT[:, 6 * h:6 * h + 6, :]),
+               [("BT", 2 * h, 2 * h + 2)], [("TB", h, h + 1)])
+            cut("v")
+        for h in range(2):
+            scan(T.RB[:, C * h:C * h + C], T.cm[:], T.TB[:, C * h:C * h + C], 0.0, A.mult, A.add, ["cm", ("TB", h, h + 1)],
+                 [("RB", h, h + 1)])
+            cut("v")
+        for h in range(2):
+            rb = T.RB[:, C * h + 23:C * h + C:32]
+            tt(T.PP[:, 18 * h + 1:18 * h + 18:3], rb, T.thc[:, 6 * h:6 * h + 6], A.is_lt, [("RB", h, h + 1), "thc"],
+               [("PP1", h, h + 1)])
+            tt(T.PP[:, 18 * h + 2:18 * h + 18:3], rb, T.cj[:, 6 * h:6 * h + 6], A.mult, [("RB", h, h + 1), "cj"],
+               [("PP2", h, h + 1)])
+            cut("v")
+        for h in range(2):
+            scan(T.PS[:, 18 * h:18 * h + 18], T.PM[:, 18 * h:18 * h + 18], T.PP[:, 18 * h:18 * h + 18], 0.0, A.mult, A.add,
+                 ["PM0", "PM1", "PM2", "PM3", "PP0", "PP3", ("PP1", h, h + 1), ("PP2", h, h + 1)], [("PS", h, h + 1)])
+            cut("v")
+        for h in range(2):
+            ts(T.LS[:, 6 * h:6 * h + 6], T.PS[:, 18 * h + 2:18 * h + 18:3], MAGIC, -MAGIC, A.add, A.add, [("PS", h, h + 1)],
+               [("LS", 6 * h, 6 * h + 6)])
+            cut("v")
+        for h in range(2):
+            act(hl("PA", h), T.IO[:, 0:HB[h + 1] - HB[h]].indirect(T.LS[:, 6 * h:6 * h + 6]), ["IO", ("LS", 6 * h, 6 * h + 6)],
+                [rl_("PA", h)])
+            cut("s")
+        pn, vn = ["PA", "PB", "PA", "PB", "PA", "PB", "PA"], ["V0", "VA", "VB", "VA", "VB", "VA", "VB"]
+        for r in range(6):
+            for h in range(2):
+                l0 = 12 * (r // 3) + 6 * h
+                L, rl = T.LS[:, l0:l0 + 6], ("LS", l0, l0 + 6)
+                own, ro = (T.V0D[:], "V0D") if r < 3 else (T.VD[:, H * h:H * h + H], ("VD", h, h + 1))
+                act(hl(pn[r + 1], h), hw(pn[r], h).indirect(L), [rw_(pn[r], h), rl], [rl_(pn[r + 1], h)])
                 cut("s")
+                tt(hl(vn[r + 1], h), hw(vn[r], h).indirect(L), own, A.add, [rw_(vn[r], h), ro, rl], [rl_(vn[r + 1], h)])
+                cut("v")
+            if r == 2:
                 if t == 0:
-                    late_scalar2(r)
-                unwrap(T.RAW[:], T[pn[r + 1]][:, 0:C], C, [(pn[r + 1], 0, C)], ["RAW"])
-                ts(T.LS[:, 12 * r + 12:12 * r + 24], T.RAW[:, 15:C:16], cim, 0.25, A.mult, A.add, ["RAW", rc(6)],
-                   [("LS", 12 * r + 12, 12 * r + 24)])
+                    late_vector2(0)
+                    late_scalar2()
+                for h in range(2):
+                    cp(T.VD[:, H * h:H * h + H], hl("VA", h), [rl_("VA", h)], [("VD", h, h + 1)])
+                    cut("v")
+                for h in range(2):
+                    unwrap(T.RAW[:, H * h:H * h + H], hl("PB", h), H, [rl_("PB", h)], [("RAW", H * h, H * h + H)])
+                    cut("v")
+                if t == 0:
+                    late_vector2(2)
+                for h in range(2):
+                    ts(T.LS[:, 12 + 6 * h:18 + 6 * h], T.RAW[:, H * h + 15:H * h + H:16], cim, 0.25, A.mult, A.add,
+                       [("RAW", H * h, H * h + H), rc(6)], [("LS", 12 + 6 * h, 18 + 6 * h)])
+                    cut("v")
+                if t == 0:
+                    late_vector2(1)
         for b in range(4):
             mm(4 + b, T.qe[:, 128 * b:128 * b + 128], T.se[:, 128 * b:128 * b + 128], T[lq][:], T[lp][:], [("qe", b, b + 1), lq])
             cut("t")
-        blk = lambda c: T.VB[:, 16 * c:16 * c + 16]
-        rvb = ("VB", 0, C)
+        for b in range(4):
+            mm(b, T.qe[:, 128 * b:128 * b + 128], T.se[:, 128 * b:128 * b + 128], T[qx][:], T[sx][:], [("qe", b, b + 1), qx])
+        cut("t")
+        blk = lambda c: T.VB[:, HB[c // 6] + 16 * (c % 6):HB[c // 6] + 16 * (c % 6) + 16]
+        rvb = lambda c: rl_("VB", c // 6)
+        rr2 = lambda c: ("RAW2", H * (c // 6), H * (c // 6) + H)
 
         def sign16(c, bias, rb):
-            act(T.JK[:, 16 * c:16 * c + 16], blk(c), [rvb, rb, rc(9)], [("JK", 16 * c, 16 * c + 16), ("AC", c, c + 1)],
+            act(T.JK[:, 16 * c:16 * c + 16], blk(c), [rvb(c), rb, rc(9)], [("JK", 16 * c, 16 * c + 16), ("AC", c, c + 1)],
                 scale=cnM, bias=bias, func=F.Sign, acc=T.AC[:, c:c + 1])
 
         def enter16(cs):
             for c in cs:
                 ts(T.CMP[:, 96 + 16 * c:112 + 16 * c], blk(c), cM, T.sm[:, 60 + c:61 + c], A.mult, A.is_lt,
-                   [rvb, rs(5), rc(8)], [("CMP", 96 + 16 * c, 112 + 16 * c)])
+                   [rvb(c), rs(5), rc(8)], [("CMP", 96 + 16 * c, 112 + 16 * c)])
             cut("v")
 
-        unwrap(T.RAW2[:], T.VB[:, 0:C], C, [rvb], ["RAW2"])
-        cut("v")
-        unwrap(T.RAW[:], T.PA[:, 0:C], C, [("PA", 0, C)], ["RAW"])
+        for h in range(2):
+            unwrap(T.RAW2[:, H * h:H * h + H], hl("VB", h), H, [rl_("VB", h)], [("RAW2", H * h, H * h + H)])
+            cut("v")
+        for h in range(2):
+            unwrap(T.RAW[:, H * h:H * h + H], hl("PA", h), H, [rl_("PA", h)], [("RAW", H * h, H * h + H)])
         cut("v")
         for c in range(6):
-            sign16(c, T.RAW2[:, 16 * c + 15:16 * c + 16], "RAW2")
+            sign16(c, T.RAW2[:, 16 * c + 15:16 * c + 16], rr2(c))
         cut("s")
         ts(sm(5), T.RAW2[:, 15:C:16], T.tmp[:, 15:16], cbm, A.add, A.add, ["RAW2", ("tmp", 0, 16), rc(10)], [rs(5)])
         cut("v")
         for c in range(6, 12):
             ts(T.CMP[:, 16 * c - 96:16 * c - 80], blk(c), cM, T.RAW2[:, 16 * c + 15:16 * c + 16], A.mult, A.is_le,
-               [rvb, "RAW2", rc(8)], [("CMP", 16 * c - 96, 16 * c - 80)])
+               [rvb(c), rr2(c), rc(8)], [("CMP", 16 * c - 96, 16 * c - 80)])
         cut("v")
         for c in range(6, 12):
             sign16(c, T.sm[:, 60 + c:61 + c], rs(5))
         cut("s")
-        ts(T.LX[:, 0:24:2], T.RAW[:, 15:C:16], cim, 0.25 - C, A.mult, A.add, ["RAW", rc(6)], ["LX"])
+        ts(T.LX[:, 0:24:2], T.RAW[:, 15:C:16], cim, 0.25 - H, A.mult, A.add, ["RAW", rc(6)], ["LX"])
         cut("v")
         enter16((0, 1))
-        scan(T.CNT[:, 0:96], T.m16[:, 0:96], T.CMP[:, 0:96], 0.0, A.mult, A.add, ["m16", ("CMP", 0, 96)], [("CNT", 0, 96)])
-        cut("v")
-        enter16((2, 3))
         ts(T.LR[:, 0:6], T.AC[:, 0:6], 0.5, 8.75, A.mult, A.add, [("AC", 0, 6)], [("LR", 0, 6)])
+        cut("v")
+        scan(T.CNT[:, 0:96], T.m16[:], T.CMP[:, 0:96], 0.0, A.mult, A.add, ["m16", ("CMP", 0, 96)], [("CNT", 0, 96)])
+        cut("v")
+        enter16((2, 3, 4))
         cp(T.LR[:, 6:12], T.CNT[:, 15:96:16], [("CNT", 0, 96)], [("LR", 6, 12)])
         cut("v")
-        enter16((4, 5))
-        tt(T.U[:], T.IO[:, 0:24].indirect(T.LR[:]), T.w16[:], A.mult, ["IO", "LR", "w16"], ["U"])
-        cut("v")
+        enter16((5,))
         for s in range(3):
             o0 = KB0[s] + 64 * s
             ts(T.KB[:, o0:o0 + 16], T.IO[:, 0:24].indirect(T.LR[:, 4 * s:4 * s + 1]), W16[0], None, A.mult, None,
-               ["IO", "LR"], [("KB", o0, o0 + 16)])
+               ["IO", ("LR", 4 * s, 4 * s + 1)], [("KB", o0, o0 + 16)])
             cut("v")
-        scan(T.CNT[:, 96:C], T.m16[:, 0:96], T.CMP[:, 96:C], 0.0, A.mult, A.add, ["m16", ("CMP", 96, C)], [("CNT", 96, C)])
+        tt(T.U[:], T.IO[:, 0:24].indirect(T.LR[:]), T.w16[:], A.mult, ["IO", "LR", "w16"], ["U"])
+        cut("v")
+        scan(T.CNT[:, 96:C], T.m16[:], T.CMP[:, 96:C], 0.0, A.mult, A.add, ["m16", ("CMP", 96, C)], [("CNT", 96, C)])
+        ts(sm(6), T.LR[:], -1.0, 1.0, A.mult, A.add, ["LR"], [rs(6)])
+        if t == 0:
+            late_vector2(3)
         cut("v")
         for be in range(4):
             for s in (1, 2):
@@ -438,6 +499,8 @@ def rank_program(g, core, T, topo):
             if be < 2:
                 act(T.Tp[:, C * be:C * be + C], bank(4 + be), [("ps", 4 + be, 5 + be)], [("Tp", be, be + 1)])
                 cut("s")
+            elif be == 2 and t == 0:
+                late_scalar3()
         for be in range(1, 4):
             for s in range(3):
                 c = 4 * s + be
@@ -446,7 +509,6 @@ def rank_program(g, core, T, topo):
                    A.add, [("KB", KB0[s], o0), "LX", "U"], [("KB", o0, o0 + 16)])
                 cut("v")
             if be == 1:
-                ts(sm(6), T.LR[:], -1.0, 1.0, A.mult, A.add, ["LR"], [rs(6)])
                 cp(T.sm[:, 156:162], T.CNT[:, 111:C:16], [("CNT", 96, C)], [("sm", 156, 162)])
                 ts(T.sm[:, 162:168], T.AC[:, 6:12], 0.5, 8.0, A.mult, A.add, [("AC", 6, 12)], [("sm", 162, 168)])
             elif be == 2:
@@ -492,9 +554,10 @@ def rank_program(g, core, T, topo):
             cut("v")
         cp(T.LE[:, 4:12], T.CNT[:, 319:768:64], [("CNT", 256, 768)], [("LE", 1, 3)])
         cut("v")
-        cp(T.LE[:, 0:4], T.CNT[:, 63:256:64], [("CNT", 0, 256)], [("LE", 0, 1)])
+        cp(T.sm[:, 160:168], T.CNT[:, 319:768:64], [("CNT", 256, 768)], [("sm", 160, 168)])
         cut("v")
-        cp(sm(13), T.CNT[:, 63:768:64], [("CNT", 0, 768)], [rs(13)])
+        cp(T.LE[:, 0:4], T.CNT[:, 63:256:64], [("CNT", 0, 256)], [("LE", 0, 1)])
+        cp(T.sm[:, 156:160], T.CNT[:, 63:256:64], [("CNT", 0, 256)], [("sm", 156, 160)])
         cut("v")
         act(T.G[:, 0:64], T.IO[:, 0:72].indirect(T.LR2[:, 0:4]), ["IO", "LR2"], [("G", 0, 64)], scale=W64[0],
             bias=-33.0 * W64[0])
@@ -515,29 +578,31 @@ def rank_program(g, core, T, topo):
         enter64(2)
         tt(T.G[:, 64:128], T.G[:, 0:64].indirect(T.LY[:, 0:4]), T.U1[:], A.add, [("G", 0, 64), "LY", "U1"], [("G", 64, 128)])
         cut("v")
-        enter64(0)
         tt(T.E[:, 64:128], T.G[:, 0:64].indirect(T.LY[:, 0:4]), T.EP[:, 0:64], A.add, [("G", 0, 64), "LY", ("EP", 0, 64)],
            [("E", 64, 128)])
         cut("v")
+        enter64(0)
         tt(T.E[:, 128:C], T.G[:, 0:128].indirect(T.LY[:, 4:8]), T.EP[:, 64:128], A.add, ["G", "LY", "EP"], [("E", 128, C)])
         cut("v")
         unwrap(T.RE[:, 0:128], T.E[:, 0:128], 128, [("E", 0, 128)], [("RE", 0, 128)])
         cut("v")
         unwrap(T.RE[:, 128:C], T.E[:, 128:C], 64, [("E", 128, C)], [("RE", 128, C)])
         cut("v")
-        count_all(lambda c: T.RE[:, 16 * c + 15:16 * c + 16], "RE", 24)
+        count_all(lambda c: T.RE[:, 16 * c + 15:16 * c + 16], lambda c: ("RE", 16 * c, 16 * c + 16), 24)
         ts(sm(6), T.AC[:, 12:24], -0.5, -31.5, A.mult, A.add, [("AC", 12, 24)], [rs(6)])
         tt(sm(10), T.RE[:, 15:C:16], T.tiem[:], A.add, ["RE", "tiem"], [rs(10)])
         cut("v")
-        ts(T.LP[:, NV:12], T.AC[:, 24 + NV:36], -0.5, 95.75, A.mult, A.add, [("AC", 24, 36)], [("LP", NV, 12)])
         cp(T.LP[:, 0:NV], T.CNT[:, C - 1:NV * C:C], [("CNT", 0, NV * C)], [("LP", 0, NV)])
+        ts(T.LP[:, NV:12], T.AC[:, 24 + NV:36], -0.5, 95.75, A.mult, A.add, [("AC", 24, 36)], [("LP", NV, 12)])
         cut("v")
         tt(sm(7), sm(6), sm(13), A.add, [rs(6), rs(13)], [rs(7)])
         cp(T.LV[:, 0:8 * NV:8], T.CNT[:, C - 1:NV * C:C], [("CNT", 0, NV * C)], ["LVp"])
         ts(T.LV[:, 8 * NV:96:8], T.AC[:, 24 + NV:36], -0.5, 95.5, A.mult, A.add, [("AC", 24, 36)], ["LVq"])
         cut("v")
         if t == 1:
-            act(T.PR[:], T.MOD[:].indirect(T.LS[:, 0:12]), ["MOD", ("LS", 0, 12)], ["PR"])
+            for h in range(2):
+                act(T.PR[:, H * h:H * h + H], hw("MOD", h).indirect(T.LS[:, 6 * h:6 * h + 6]), ["MOD", ("LS", 0, 12)],
+                    [("PR", h, h + 1)])
             cut("s")
         cp(T.O[:].indirect(T.LP[:]), T.IO[:, 0:C], ["IO", "LP"], ["O"])
         cut("v")
@@ -553,27 +618,40 @@ def rank_program(g, core, T, topo):
         if t == 1:
             dma("y", "dop", T.op[:], T.PR[0:128:16, :], ["PR"], [])
         cut("v")
-        count_all(lambda c: T.sm[:, 132 + c:133 + c], rs(11), 36)
-        ts(T.LV[:, 96 + 8 * NV:C:8], T.AC[:, 36 + NV:48], -0.5, 95.0, A.mult, A.add, [("AC", 36, 48)], ["LVf"])
+        count_all(lambda c: T.sm[:, 132 + c:133 + c], lambda c: rs(11), 36)
+        if t == 0:
+            quant(T.qv[:], T.sv[:], T.vt[:], ["vt"], ["qv"])
+            cut("v")
         ts(T.LV[:, 96:96 + 8 * NV:8], T.CNT[:, C - 1:NV * C:C], -1.0, None, A.add, None, [("CNT", 0, NV * C)], ["LVe"])
+        ts(T.LV[:, 96 + 8 * NV:C:8], T.AC[:, 36 + NV:48], -0.5, 95.0, A.mult, A.add, [("AC", 36, 48)], ["LVf"])
+        tt(sm(12), T.LV[:, 96:C:8], T.LV[:, 0:96:8], A.subtract, ["LVp", "LVq", "LVe", "LVf"], [rs(12)])
+        cut("v")
+        for m in range(1, 8):
+            ts(T.LV[:, m:96:8], sm(12), 2.0 ** m - 1.0, 193.0 - 2.0 ** (m - 1), A.is_gt, A.mult, [rs(12)], ["LV%d" % m])
         cut("v")
         for b in (2, 3):
             act(T[Bt][:, b:768:4], T.Tp[:, C * b:C * b + C].indirect(T[lo][:]), [("Tp", b, b + 1), lo], [Bt + "b%d" % b])
         for b in (0, 1):
             cp(T[Bt][:, b:768:4], T.Tp[:, C * b:C * b + C].indirect(T[lo][:]), [("Tp", b, b + 1), lo], [Bt + "b%d" % b])
         cut("v")
-        tt(sm(12), T.LV[:, 96:C:8], T.LV[:, 0:96:8], A.subtract, ["LVp", "LVq", "LVe", "LVf"], [rs(12)])
-        cut("v")
-        quant(T[qf][:], T[sf][:], T[Bt][:], [Bt + "b%d" % b for b in range(4)], [qf])
-        for b in range(4):
-            mm(4 + b, T.qw[:, 128 * b:128 * b + 128], T.sw[:, 128 * b:128 * b + 128], T[qf][:], T[sf][:], ["qw", "sw", qf])
-            cut("t")
-        cut("v")
         for m in range(1, 8):
-            ts(T.LV[:, m:96:8], sm(12), 2.0 ** m - 1.0, 193.0 - 2.0 ** (m - 1), A.is_gt, A.mult, [rs(12)], ["LV%d" % m])
+            if m == 4:
+                cut("v")
+                quant(T[qf][:], T[sf][:], T[Bt][:], [Bt + "b%d" % b for b in range(4)], [qf])
+                for b in range(4):
+                    mm(4 + b, T.qw[:, 128 * b:128 * b + 128], T.sw[:, 128 * b:128 * b + 128], T[qf][:], T[sf][:],
+                       ["qw", "sw", qf])
+                    cut("t")
+                cut("v")
             ts(T.LV[:, 96 + m:C:8], sm(12), 2.0 ** m - 1.0, 193.0 - 2.0 ** m, A.is_gt, A.mult, [rs(12)], ["LU%d" % m])
+        scan(T.LW[:], T.m8[:], T.LV[:], 0.0, A.mult, A.add,
+             ["m8", "LVp", "LVq", "LVe", "LVf"] + ["LV%d" % m for m in range(1, 8)] + ["LU%d" % m for m in range(1, 8)], ["LW"])
         cut("v")
-        for b in range(4):
+        ts(T.TAB[:, 0:C], bank(4), 0.03125, None, A.mult, None, [("ps", 4, 5)], [("TAB", 0, C)])
+        cut("v")
+        cp(T.LL[:], T.LW[:, 7:C:8], ["LW"], ["LL"])
+        cut("v")
+        for b in range(1, 4):
             act(T.TAB[:, TW * b:TW * b + C], bank(4 + b), [("ps", 4 + b, 5 + b)], [("TAB", TW * b, TW * b + C)], scale=0.03125)
             cut("s")
         off = [193 * k - 2 ** k + 1 for k in range(9)]
@@ -600,29 +678,24 @@ def rank_program(g, core, T, topo):
                [Xn + "b%d" % b])
             cut("v")
 
-        for i in range(1, 11):
-            if i == 10:
-                pick(0)
-            for b in range(4):
-                if 1 <= i - b <= 7:
-                    level(b, i - b)
-                if i - b == 7:
-                    w, rw = win(b)
-                    act(T.G1[:, C * b:C * b + C], w.indirect(T.LL[:, 0:12]), [rw, "LL"], [("G1", b, b + 1)])
-                    cut("s")
-            if i == 1:
-                scan(T.LW[:], T.m8[:], T.LV[:], 0.0, A.mult, A.add,
-                     ["m8", "LVp", "LVq", "LVe", "LVf"] + ["LV%d" % m for m in range(1, 8)] + ["LU%d" % m for m in range(1, 8)],
-                     ["LW"])
-                cut("v")
-            if i == 2:
-                cp(T.LL[:], T.LW[:, 7:C:8], ["LW"], ["LL"])
-                cut("v")
+        order = [(0, 1), (1, 1), (0, 2), (2, 1), (1, 2), (0, 3), (3, 1), (2, 2), (1, 3), (0, 4), (3, 2), (2, 3), (1, 4), (0, 5),
+                 (3, 3), (2, 4), (1, 5), (0, 6), (3, 4), (2, 5), (1, 6), (0, 7), (3, 5), (2, 6), (1, 7), (3, 6), (2, 7)]
+        for b, k in order:
+            level(b, k)
+            if k == 7:
+                w, rw = win(b)
+                act(T.G1[:, C * b:C * b + C], w.indirect(T.LL[:, 0:12]), [rw, "LL"], [("G1", b, b + 1)])
+                cut("s")
+        pick(0)
+        level(3, 7)
+        w, rw = win(3)
+        act(T.G1[:, 3 * C:4 * C], w.indirect(T.LL[:, 0:12]), [rw, "LL"], [("G1", 3, 4)])
+        cut("s")
         pick(1)
         plus(0)
         pick(2)
-        plus(1)
         pick(3)
+        plus(1)
         plus(2)
         plus(3)
 

@@ -12,8 +12,12 @@ KB0 = [0, 64, 192]
 XB0 = [0, 0, 128]
 HB = [0, 192, 480]
 TW = 1296
-NV = 6
-X4, U8, U16, F32, B16, I32 = "float8_e4m3fn_x4", "uint8", "uint16", "float32", "bfloat16", "int32"
+NE = 3
+OFF = [193 * k - 2 ** k + 1 for k in range(9)]
+LAG = [0.0, 0.5, 1.6, 2.7]
+PICK = [8.9, 9.65, 10.5, 11.5]
+PLUS = [10.6, 11.4, 11.6, 12.0]
+X4, U8, U16, F32, B16 = "float8_e4m3fn_x4", "uint8", "uint16", "float32", "bfloat16"
 
 SCRATCH = {}
 for _n, _w, _d in [
@@ -24,27 +28,29 @@ for _n, _w, _d in [
     ("Bt0", 768, B16), ("Bt1", 768, B16), ("qf0", C, X4), ("qf1", C, X4), ("sf0", C, U8), ("sf1", C, U8),
     ("ut", 512, B16), ("vt", 512, B16), ("qu", 128, X4), ("su", 128, U8), ("qv", 128, X4), ("sv", 128, U8),
     ("qw", 512, X4), ("sw", 512, U8), ("Z", 528, B16), ("qe", 512, X4), ("se", 512, U8),
-    ("Tp", 768, B16), ("TB", 384, B16), ("RB", 384, B16), ("cm", C, B16),
-    ("pi", 4, I32), ("col", 16, F32), ("pat", 48, F32), ("tmp", 128, F32), ("c16", 12, F32), ("c16m", 12, F32),
-    ("cj", 12, F32), ("thr", 12, F32), ("thc", 12, F32), ("wm", 24, F32), ("tiem", 12, F32),
-    ("PP", 36, F32), ("PM", 36, F32), ("PS", 36, F32),
-    ("IO", 288, F32), ("MOD", 480, F32), ("ext", C, F32), ("ones", 256, B16), ("m16", H, B16), ("m64", 256, B16),
-    ("m8", C, F32), ("w16", C, F32), ("tie", C, F32), ("TE", 216, F32),
-    ("PA", 480, F32), ("PB", 480, F32), ("V0", 480, F32), ("VA", 480, F32), ("VB", 480, F32),
-    ("V0D", H, F32), ("VD", C, F32),
-    ("RAW", C, F32), ("RAW2", C, F32), ("RK", C, F32), ("RE", C, F32), ("RX", 128, F32),
-    ("sm", 192, F32), ("LS", 24, U16), ("LX", 24, U16), ("LR", 12, U16), ("LR2", 12, U16), ("LE", 12, U16),
-    ("LY", 8, U16), ("LP", 12, U16), ("LL", 24, U16),
-    ("CMP", 1152, B16), ("CNT", 1152, B16), ("JK", 1344, B16), ("AC", 48, F32),
-    ("U", C, F32), ("KB", 384, F32), ("XS", 320, F32), ("G", 128, F32), ("U1", 64, F32), ("EP", 128, F32),
-    ("E", C, F32), ("O", C, F32), ("LV", C, F32), ("LW", C, F32), ("PR", C, F32),
+    ("Tp", 768, B16), ("TB", 384, B16), ("RB", 384, B16), ("cf", 384, B16),
+    ("PT", 224, F32), ("PC", 224, F32), ("col", 16, F32), ("tmp", 64, F32), ("c16", 12, F32), ("c16f", 12, F32),
+    ("wm", 12, F32), ("wsh", 12, F32), ("wf", C, F32), ("IO", 288, F32), ("IOb", C, B16), ("MOD", 480, F32), ("ext", C, B16), ("ones", 256, B16),
+    ("m16", C, B16), ("m64", 256, B16), ("exa", 64, F32), ("RA", 128, F32), ("tie", C, F32), ("TE", 216, F32), ("D1", 16, F32),
+    ("TH", H, F32), ("RL", H, F32), ("RR", H, F32), ("FL", H, F32), ("SL", C, F32),
+    ("PA", 480, F32), ("PB", 480, F32), ("V0", 480, F32), ("VA", 480, F32), ("VB", 480, F32), ("VD", C, F32),
+    ("K16", C, F32), ("KS", C, F32), ("RAW", C, F32), ("RAW2", C, F32), ("RK", C, F32), ("RE", C, F32),
+    ("RX", 128, F32), ("RG", 128, F32), ("sm", 192, F32),
+    ("LS", 24, U16), ("LX", 24, U16), ("LR", 12, U16), ("LR2", 8, U16), ("LE", 12, U16), ("LY", 8, U16),
+    ("LP", 12, U16), ("LL", 24, U16), ("L15", 6, U16), ("L8", 6, U16),
+    ("CMP", 960, B16), ("CNT", 960, B16), ("C16", C, B16), ("N16", C, B16), ("N64", 512, B16),
+    ("JK", 1344, B16), ("AC", 48, F32),
+    ("U", C, F32), ("KB", 384, F32), ("XS", 320, F32), ("GE", 320, F32), ("UE", C, F32),
+    ("O", C, B16), ("RO", C, B16), ("PR", C, F32),
     ("TAB", 4 * TW, F32), ("G1", 768, F32), ("MX", 768, F32), ("Y", C, F32),
 ]:
     SCRATCH[_n] = ("sbuf", [128, _w], _d)
 SCRATCH["BT"] = ("sbuf", [128, 12, 32], B16)
+SCRATCH["cm"] = ("sbuf", [128, 12, 32], B16)
+SCRATCH["w16"] = ("sbuf", [128, 12, 16], F32)
 SCRATCH["ps"] = ("psum", [128, 4096], F32)
 
-POOL = {"v": 60, "s": 40, "t": 10, "g": 12}
+POOL = {"v": 64, "s": 44, "t": 10, "g": 12}
 DMAS = ["dx", "du", "dv", "dwc", "dws", "dop", "doc", "ds0", "ds1", "ds2", "ds3", "dy"]
 SEMAPHORES = [e + str(i) for e in POOL for i in range(POOL[e])] + DMAS + ["ax0", "ax1", "al0", "al1", "ls"]
 
@@ -57,9 +63,30 @@ def rank_program(g, core, T, topo):
     known = {e: set() for e in Q}
     cur = {e: None for e in Q}
     nxt = {e: 0 for e in Q}
+    joined = [False]
     last = {}
     batches = []
     hist = {}
+
+    def R(n, a=0, b=None, s=1):
+        b = SCRATCH[n][1][1] if b is None else b
+        return (T[n][:, a:b:s] if s != 1 else T[n][:, a:b], [(n, frozenset(range(a, b, s)))])
+
+    def R3(n, a, b, c, d):
+        w = SCRATCH[n][1][2]
+        return (T[n][:, a:b, c:d], [(n, frozenset(i * w + j for i in range(a, b) for j in range(c, d)))])
+
+    def bank(b, lo=0, hi=C):
+        return (T.ps[:, 512 * b + lo:512 * b + hi], [("ps", frozenset([b]))])
+
+    def ind(win, off):
+        return (win[0].indirect(off[0]), win[1] + off[1])
+
+    def ap(x):
+        return x[0] if isinstance(x, tuple) else x
+
+    def regs(*xs):
+        return [r for x in xs if isinstance(x, tuple) for r in x[1]]
 
     def new_batch(e, sem, base):
         b = {"id": len(batches), "e": e, "sem": sem, "n": base, "known": set(known[e]) if e else set(), "waited": False}
@@ -78,31 +105,23 @@ def rank_program(g, core, T, topo):
         known[e].update(b["known"])
         cur[e] = None
 
-    def cut(e):
-        cur[e] = None
-
-    def reg(r):
-        return (r, 0, 1 << 20) if isinstance(r, str) else r
-
     def depend(e, reads, writes):
         deps = {}
         for w, rs in ((False, reads), (True, writes)):
-            for r in rs:
-                n, lo, hi = reg(r)
-                for (l2, h2, w2, b) in hist.get(n, []):
-                    if l2 < hi and lo < h2 and (w or w2 or (n == "ps" and b["e"] != e)):
+            for n, cols in rs:
+                for (c2, w2, b) in hist.get(n, []):
+                    if (w or w2 or (n == "ps" and b["e"] != e)) and not cols.isdisjoint(c2):
                         deps[b["id"]] = b
         for i in sorted(deps, reverse=True):
             wait(e, deps[i])
 
     def note(b, reads, writes):
         for w, rs in ((False, reads), (True, writes)):
-            for r in rs:
-                n, lo, hi = reg(r)
+            for n, cols in rs:
                 h = hist.setdefault(n, [])
                 if w:
-                    h[:] = [x for x in h if not (lo <= x[0] and x[1] <= hi)]
-                h.append((lo, hi, w, b))
+                    h[:] = [x for x in h if not x[0] <= cols]
+                h.append((cols, w, b))
 
     def op(e, fn, reads, writes):
         depend(e, reads, writes)
@@ -118,594 +137,445 @@ def rank_program(g, core, T, topo):
         fn().then_inc(T.sem[b["sem"]], 1)
         b["n"] += 1
         note(b, reads, writes)
+        if not joined[0]:
+            cur[e] = None
 
-    def dma(e, sem, out, in_, reads, writes):
-        depend(e, reads, writes)
-        Q[e].dma_start(out, in_).then_inc(T.sem[sem], 16)
-        b = new_batch(e, sem, 16)
-        note(b, reads, writes)
+    def together(calls):
+        joined[0] = True
+        for c in calls:
+            c()
+        joined[0] = False
+        for e in cur:
+            cur[e] = None
 
-    def ts(out, in0, s1, s2, o0, o1, reads, writes):
+    def dma(e, sem, out, in_):
+        depend(e, regs(in_), regs(out))
+        Q[e].dma_start(ap(out), ap(in_)).then_inc(T.sem[sem], 16)
+        note(new_batch(e, sem, 16), regs(in_), regs(out))
+
+    def ts(out, in0, s1, o0, s2=None, o1=None):
         if o1 is None:
-            op("v", lambda: g.vector.tensor_scalar(out, in0, s1, None, o0), reads, writes)
+            op("v", lambda: g.vector.tensor_scalar(out[0], in0[0], ap(s1), None, o0), regs(in0, s1), out[1])
         else:
-            op("v", lambda: g.vector.tensor_scalar(out, in0, s1, s2, o0, o1), reads, writes)
+            op("v", lambda: g.vector.tensor_scalar(out[0], in0[0], ap(s1), ap(s2), o0, o1), regs(in0, s1, s2), out[1])
 
-    def tt(out, in0, in1, o, reads, writes):
-        op("v", lambda: g.vector.tensor_tensor(out, in0, in1, o), reads, writes)
+    def tt(out, in0, in1, o):
+        op("v", lambda: g.vector.tensor_tensor(out[0], in0[0], in1[0], o), regs(in0, in1), out[1])
 
-    def scan(out, d0, d1, init, o0, o1, reads, writes):
-        op("v", lambda: g.vector.tensor_tensor_scan(out, d0, d1, init, o0, o1), reads, writes)
+    def scan(out, d0, d1, o0=A.mult, o1=A.add, init=0.0):
+        op("v", lambda: g.vector.tensor_tensor_scan(out[0], d0[0], d1[0], init, o0, o1), regs(d0, d1), out[1])
 
-    def cp(out, in_, reads, writes):
-        op("v", lambda: g.vector.tensor_copy(out, in_), reads, writes)
+    def cp(out, in_):
+        op("v", lambda: g.vector.tensor_copy(out[0], in_[0]), in_[1], out[1])
 
-    def ms(ap, c, writes):
-        op("v", lambda: g.vector.memset(ap, c), [], writes)
+    def ms(out, c):
+        op("v", lambda: g.vector.memset(out[0], c), [], out[1])
 
-    def act(out, in_, reads, writes, scale=None, bias=None, func=None, acc=None):
+    def act(out, in_, scale=None, bias=None, func=None, acc=None):
         kw = {}
         if scale is not None:
-            kw["scale"] = scale
+            kw["scale"] = ap(scale)
         if bias is not None:
-            kw["bias"] = bias
+            kw["bias"] = ap(bias)
         if acc is not None:
-            kw["accum_out"] = acc
+            kw["accum_out"] = acc[0]
         fu = func if func is not None else (F.Identity if bias is not None else F.Copy)
-        op("s", lambda: g.scalar.activation(out, in_, fu, **kw), reads, writes)
+        op("s", lambda: g.scalar.activation(out[0], in_[0], fu, **kw), regs(in_, scale, bias), regs(out, acc))
 
-    def quant(q, s, x, reads, writes):
-        op("v", lambda: g.vector.quantize_mx(q, s, x), reads, writes)
+    def quant(q, s, x):
+        op("v", lambda: g.vector.quantize_mx(q[0], s[0], x[0]), x[1], regs(q, s))
 
-    def mm(bank, lq, lsc, rq, rs, reads):
-        op("t", lambda: g.tensor.matmul_mx(T.ps[:, 512 * bank:512 * bank + C], lq, lsc, rq, rs, True, True),
-           reads, [("ps", bank, bank + 1)])
+    def mm(b, lq, ls, rq, rs):
+        op("t", lambda: g.tensor.matmul_mx(bank(b)[0], lq[0], ls[0], rq[0], rs[0], True, True), regs(lq, ls, rq, rs),
+           bank(b)[1])
 
-    def iota(name, lo, hi, pattern, base):
-        op("g", lambda: g.iota(T[name][:, lo:hi], pattern, base, 0, allow_small_or_imprecise_dtypes=True), [],
-           [(name, lo, hi)])
+    def iota(out, pattern, base):
+        op("g", lambda: g.iota(out[0], pattern, base, 0, allow_small_or_imprecise_dtypes=True), [], out[1])
 
     def mask(name, n, period):
         op("g", lambda: g.affine_select(T[name][:], T.ones[:, 0:n], [[0, n // period], [1, period]], A.not_equal,
-                                        0.0, 0, 0), ["ones"], [name])
+                                        0.0, 0, 0), R("ones")[1], R(name)[1])
 
     sent = [0]
 
-    def send(peer, dst, src, sem, reads):
-        depend("g", reads, [])
+    def u8(x):
+        return (x[0].bitcast(dt.uint8), x[1])
+
+    def send(peer, dst, src, sem):
+        depend("g", src[1], [])
         rid, pid, _ = topo.addr(peer)
-        g.remote_dma(dst, src, T.sem[sem], T.sem.ls, pid, rid, topo.mask(core, peer))
-        n = len(topo.engines(core, peer))
-        sent[0] += n
-        cut("g")
+        g.remote_dma(dst[0], src[0], T.sem[sem], T.sem.ls, pid, rid, topo.mask(core, peer))
+        sent[0] += len(topo.engines(core, peer))
 
-    def arrival(peer, sem, calls, writes):
-        note(new_batch(None, sem, calls * len(topo.engines(peer, core))), [], writes)
+    def arrival(peer, sem, calls, *lands):
+        note(new_batch(None, sem, calls * len(topo.engines(peer, core))), [], regs(*lands))
 
-    def bank(b):
-        return T.ps[:, 512 * b:512 * b + C]
+    def fill(out, n, c):
+        act(out, R("ones", 0, n), scale=c)
 
-    col = lambda i: T.col[:, i:i + 1]
-    cq, ch, cnh, c1q, cq1, ccj, cim, cmt, cM, cnM, cbm = [col(i) for i in range(11)]
-    rc = lambda i: ("col", i, i + 1)
-    sm = lambda k: T.sm[:, 12 * k:12 * k + 12]
-    rs = lambda k: ("sm", 12 * k, 12 * k + 12)
+    cw, cthr, cq, ch, cM, cim, cown = [R("PC", 32 * i, 32 * i + 1) for i in range(7)]
+    cj, cjq, cA, cB, c16B, cH0, cnM, cnMe, cE, cq1, c8, cS = [R("col", i, i + 1) for i in range(12)]
+    sm = lambda k, a=0, b=12: R("sm", 16 * k + a, 16 * k + b)
 
-    dma("y", "dx", T.X0[:], T.x[:], [], ["X0"])
-    dma("s", "du", T.ut[:], T.u[:], [], ["ut"])
-    dma("y", "dwc", T.qw[:].bitcast(dt.uint8), T.wc[:], [], ["qw"])
-    dma("y", "dws", T.sw[:], T.ws[:], [], ["sw"])
-    dma("y", "dv", T.vt[:], T.v[:], [], ["vt"])
+    dma("y", "dx", R("X0"), T.x[:])
+    dma("s", "du", R("ut"), T.u[:])
+    dma("y", "dwc", u8(R("qw")), T.wc[:])
+    dma("y", "dws", R("sw"), T.ws[:])
+    dma("y", "dv", R("vt"), T.v[:])
 
-    op("g", lambda: g.iota(T.pi[:, 0:1], [[0, 1]], 0, 1), [], [("pi", 0, 1)])
-    cut("g")
-    iota("c16", 0, 12, [[16, 12]], 0)
-    cut("g")
-    iota("IO", 0, 288, [[1, 288]], 0)
-    cut("g")
-    ms(T.ones[:], 1.0, ["ones"])
-    ms(T.Z[:], 0.0, ["Z"])
-    cut("v")
-    ts(T.pi[:, 2:3], T.pi[:, 0:1], 15, None, A.bitwise_and, None, [("pi", 0, 1)], [("pi", 2, 3)])
-    ts(T.pi[:, 3:4], T.pi[:, 0:1], 4, 1, A.arith_shift_right, A.bitwise_and, [("pi", 0, 1)], [("pi", 3, 4)])
-    cut("v")
-    ms(T.tmp[:, 96:112], 0.5, [("tmp", 96, 112)])
-    ms(T.tmp[:, 112:128], 0.0, [("tmp", 112, 128)])
-    for lo, hi, c in ((0, 16, 1.0), (16, 17, 0.0)):
-        ms(T.pat[:, lo:hi], c, [("pat", lo, hi)])
-    cut("v")
-    cp(T.col[:, 0:2], T.pi[:, 2:4], [("pi", 2, 4)], [("col", 0, 2)])
-    cut("v")
-    for lo, hi, c in ((17, 24, 0.5), (24, 25, BIG), (25, 48, 1.0)):
-        ms(T.pat[:, lo:hi], c, [("pat", lo, hi)])
-    cut("v")
+    iota(R("PT", 64, 96), [[0, 2], [1, 16]], 0)
+    iota(R("PT", 96, 128), [[1, 2], [0, 16]], 0)
+    iota(R("c16"), [[16, 12]], 0)
+    iota(R("IO"), [[1, 288]], 0)
+    ms(R("ones"), 1.0)
+    together([lambda: ms(R("PT", 0, 32), 0.0), lambda: ms(R("PT", 32, 64), -1e29), lambda: ms(R("PT", 128, 160), BIG),
+              lambda: ms(R("PT", 160, 192), 1.0 / BIG), lambda: ms(R("tmp", 0, 16), 0.5), lambda: ms(R("Z"), 0.0)])
+    together([lambda: fill(R("PT", 0, 8), 8, 1.0), lambda: fill(R("PT", 16, 24), 8, 1.0),
+              lambda: fill(R("PT", 24, 25), 1, -0.498046875), lambda: fill(R("PT", 25, 29, 3), 2, MAGIC),
+              lambda: fill(R("PT", 26, 30, 3), 2, -MAGIC), lambda: fill(R("PT", 27, 28), 1, 1.25),
+              lambda: fill(R("PT", 32, 40), 8, 0.0), lambda: fill(R("PT", 48, 56), 8, 0.0),
+              lambda: fill(R("PT", 143, 192, 16), 4, 1.0)])
+
+    def zero_window(n):
+        together([lambda a=a, b=b: ms(R(n, a, b), 0.0) for a, b in ((H, C), (288, 480))])
+
+    zero_window("VA")
+    together([lambda k=k: scan(R("PT", 192 + 16 * k, 208 + 16 * k), R("tmp", 0, 16), R("Z", 0, 16), init=65536.0)
+              for k in range(2)])
+    ms(R3("cm", 0, 12, 0, 32), 1.0)
+    ts(R("c16f"), R("c16"), -0.5, A.add)
+    zero_window("VB")
+    op("v", lambda: g.vector.transpose(T.PC[:], T.PT[:]), R("PT")[1], R("PC")[1])
+    op("v", lambda: g.vector.reciprocal(sm(1)[0], T.c16f[:]), R("c16f")[1], sm(1)[1])
     op("g", lambda: g.affine_select(T.Z[:, 3:515:4], T.ones[:, 0:128], [[-1, 128]], A.is_equal, 0.0, 0, 1),
-       ["ones"], ["Z"])
-    scan(T.V0[:, 0:16], T.tmp[:, 96:112], T.tmp[:, 112:128], 65536.0, A.mult, A.add, [("tmp", 96, 128)], [("V0", 0, 16)])
-    ts(cnh, ch, -1.0, 1.0, A.mult, A.add, [rc(1)], [rc(2)])
-    ts(c1q, cq, -1.0, 1.0, A.mult, A.add, [rc(0)], [rc(3)])
-    ts(ccj, ch, 1.0 / BIG, 0.5, A.max, A.mult, [rc(1)], [rc(5)])
-    ts(cq1, cq, 1.0, None, A.add, None, [rc(0)], [rc(4)])
-    cut("v")
-    ts(cim, cq, 15.0, 1.0 / BIG, A.is_equal, A.max, [rc(0)], [rc(6)])
-    ts(cmt, cq, 15.0, BIG, A.not_equal, A.mult, [rc(0)], [rc(7)])
-    ts(T.tmp[:, 0:32], T.pat[:, 0:32], ch, None, A.mult, None, ["pat", rc(1)], [("tmp", 0, 32)])
-    cut("v")
-    ts(T.tmp[:, 32:64], T.pat[:, 16:48], cnh, None, A.mult, None, ["pat", rc(2)], [("tmp", 32, 64)])
-    ts(T.cj[:], T.c16[:], cq, ccj, A.add, A.mult, ["c16", rc(0), rc(5)], ["cj"])
-    ts(T.thr[:], T.c16[:], c1q, -0.002, A.max, A.add, ["c16", rc(3)], ["thr"])
-    cut("v")
-    ts(T.tmp[:, 64:80], T.IO[:, 0:16], cq, None, A.not_equal, None, ["IO", rc(0)], [("tmp", 64, 80)])
-    ts(T.tmp[:, 80:96], T.IO[:, 0:16], cq1, BIG, A.is_equal, A.mult, ["IO", rc(4)], [("tmp", 80, 96)])
-    ts(cM, cmt, 1.0, None, A.max, None, [rc(7)], [rc(8)])
-    ts(cnM, cmt, 1.0, -1.0, A.max, A.mult, [rc(7)], [rc(9)])
-    cut("v")
-    tt(T.cm[:, 0:32], T.tmp[:, 0:32], T.tmp[:, 32:64], A.add, [("tmp", 0, 64)], [("cm", 0, 32)])
-    ts(sm(0), T.cj[:], 2.0 ** -70, None, A.max, None, ["cj"], [rs(0)])
-    cut("v")
-    ms(T.PM[:, 0:36:3], 0.0, ["PM0"])
-    ms(T.PM[:, 1:36:3], 1.0, ["PM1"])
-    cut("v")
-    tt(T.ext[:, 0:16], T.tmp[:, 64:80], T.tmp[:, 80:96], A.add, [("tmp", 64, 96)], [("ext", 0, 16)])
-    op("v", lambda: g.vector.reciprocal(sm(1), sm(0)), [rs(0)], [rs(1)])
-    cut("v")
-    quant(T.qu[:], T.su[:], T.ut[:], ["ut"], ["qu"])
-    for n in ("V0", "VA", "VB"):
-        act(T[n][:, H:C], T.IO[:, 0:H], ["IO"], [(n, H, C)], scale=0.0)
-        act(T[n][:, 288:480], T.IO[:, 0:C], ["IO"], [(n, 288, 480)], scale=0.0)
-    for n, w in (("cm", 32), ("V0", 16), ("ext", 16)):
-        act(T[n][:, w:2 * w], T[n][:, 0:w], [(n, 0, w)], [(n, w, 2 * w)])
-        cut("s")
-    for n, w in (("cm", 32), ("V0", 16), ("ext", 16)):
-        for k in (2, 4):
-            act(T[n][:, k * w:(k + 2) * w], T[n][:, 0:2 * w], [(n, 0, 2 * w)], [(n, k * w, (k + 2) * w)])
-        cut("s")
-    for n in ("PA", "PB"):
-        act(T[n][:, H:C], T.IO[:, H:C], ["IO"], [(n, H, C)])
-        act(T[n][:, 288:480], T.IO[:, H:288], ["IO"], [(n, 288, 480)])
-    cut("s")
-    act(T.V0[:, C:288], T.V0[:, 0:H], [("V0", 0, H)], [("V0", C, 288)])
-    act(T.V0D[:], T.V0[:, 0:H], [("V0", 0, H)], ["V0D"])
-    act(T.ext[:, H:C], T.ext[:, 0:H], [("ext", 0, H)], [("ext", H, C)])
-    cut("s")
+       R("ones")[1], R("Z")[1])
+    together([lambda: act(cj, ch, scale=0.5, bias=0.5 / BIG), lambda: act(cA, ch, scale=0.5, bias=0.5),
+              lambda: act(cB, ch, scale=-0.5, bias=1.0), lambda: act(c16B, ch, scale=-BIG, bias=BIG)])
+    together([lambda: ts(cH0, cq, 0.0, A.is_equal, float(H), A.mult), lambda: ts(cq1, cq, 1.0, A.add),
+              lambda: ts(R("tmp", 16, 32), R("IO", 0, 16), cq, A.not_equal)])
+    act(cjq, cq, scale=cj)
+    cmc = lambda a, b, lo=0, hi=12: R3("cm", lo, hi, a, b)
+    together([lambda: act(cmc(0, 1), R("ones", 0, 12), scale=ch), lambda: act(cmc(1, 8), R("ones", 0, 84), scale=cA),
+              lambda: act(cmc(16, 17), R("ones", 0, 12), scale=c16B), lambda: act(cmc(17, 24), R("ones", 0, 84), scale=cB),
+              lambda: act(cmc(24, 25), R("c16"), scale=cj, bias=cjq), lambda: act(cmc(27, 28), sm(1), scale=-0.75),
+              lambda: act(cmc(30, 31, 0, 1), R("ones", 0, 1), scale=cH0), lambda: fill(cmc(30, 31, 1, 6), 5, float(H)),
+              lambda: fill(cmc(30, 31, 6, 12), 6, float(C))])
+    ts(R("tmp", 32, 48), R("IO", 0, 16), cq1, A.is_equal, BIG, A.mult)
+    quant(R("qu"), R("su"), R("ut"))
 
-    def late_vector():
-        cut("v")
-        tt(T.thc[:], T.thr[:], sm(1), A.mult, ["thr", rs(1)], ["thc"])
-        ms(T.PM[:, 2:18:3], float(H), ["PM2"])
-        ms(T.PM[:, 20:36:3], float(C), ["PM3"])
-        ms(T.PP[:, 0:18:3], -0.498046875 / H, ["PP0"])
-        ms(T.PP[:, 18:36:3], -(H + 0.498046875) / C, ["PP3"])
-        cut("v")
+    def after_scores_vector():
+        tt(R("ext", 0, 16), R("tmp", 16, 32), R("tmp", 32, 48), A.add)
+        rank_constants()
 
-    def late_vector2(k):
-        if k < 2:
-            for b in (2 * k, 2 * k + 1):
-                quant(T.qe[:, 128 * b:128 * b + 128], T.se[:, 128 * b:128 * b + 128], T.Z[:, 3 - b:515 - b], ["Z"],
-                      [("qe", b, b + 1)])
-        elif k == 2:
-            scan(T.tmp[:, 0:16], T.ext[:, 0:16], T.V0D[:, 0:16], 0.0, A.mult, A.add, ["ext", "V0D"], [("tmp", 0, 16)])
-            ts(cbm, cM, -0.5, None, A.mult, None, [rc(8)], [rc(10)])
-        else:
-            ts(T.wm[:], T.wm[:], cM, None, A.mult, None, [rc(8)], ["wm"] + ["wm%d" % i for i in range(7)])
-            ts(T.tiem[:], T.c16m[:], cq, cM, A.add, A.mult, ["c16m", rc(0), rc(8)], ["tiem"])
-        cut("v")
+    def after_scores_scalar():
+        act(R("V0", 0, 32), R("PT", 192, 224))
+        act(R("PA", H, C), R("IO", H, C))
+        act(R("PA", 288, 480), R("IO", H, 288))
+        for h in range(2):
+            act(R("cf", C * h, C * h + C), R3("cm", 6 * h, 6 * h + 6, 0, 32))
+        together([lambda k=k: act(R("V0", 32 * k, 32 * k + 32), R("V0", 0, 32)) for k in (1, 2, 6, 7, 8)] +
+                 [lambda: fill(R("V0", H, C), H, 0.0), lambda: fill(R("V0", 288, 480), C, 0.0)])
+        together([lambda a=a, b=b, c=c: act(R("PB", a, b), R("IO", c, c + b - a)) for a, b, c in ((H, C, H), (288, 480, H))])
 
-    def late_scalar():
-        for k in range(4):
-            act(T.w16[:, 16 * k:16 * k + 16], T.ones[:, 0:16], ["ones"], [("w16", 16 * k, 16 * k + 16)], scale=W16[k])
-            act(T.wm[:, k:12:4], T.ones[:, 0:3], ["ones"], ["wm%d" % (3 + k)], scale=W16[k])
-        for s in range(3):
-            act(T.wm[:, 12 + 4 * s:16 + 4 * s], T.ones[:, 0:4], ["ones"], ["wm%d" % s], scale=W64[s])
-        cut("s")
-
-    def late_scalar2():
-        for s in (1, 2):
-            act(T.w16[:, 64 * s:64 * s + 64], T.w16[:, 0:64], [("w16", 0, 64)], [("w16", 64 * s, 64 * s + 64)])
-        act(T.KB[:, 64:128], T.IO[:, 0:64], ["IO"], [("KB", 64, 128)], scale=0.0)
-        act(T.KB[:, C:320], T.IO[:, 0:128], ["IO"], [("KB", C, 320)], scale=0.0)
-        cut("s")
-
-    def late_scalar3():
-        for s in range(3):
-            act(T.TE[:, 72 * s:72 * s + 72], T.IO[:, 0:72], ["IO"], [("TE", 72 * s, 72 * s + 72)], scale=W64[s],
-                bias=W64[s] * (-32.0 if s == 0 else 1.0))
-        cut("s")
+    def spread_ext():
+        together([lambda k=k: act(R("ext", 16 * k, 16 * k + 16), R("ext", 0, 16)) for k in range(1, 6)])
 
     def late_gpsimd():
-        iota("c16m", 0, 12, [[0, 3], [16, 4]], 1)
-        cut("g")
-        mask("m16", H, 16)
-        cut("g")
-        iota("XS", 0, 64, [[1, 64]], 0)
-        iota("XS", 128, 256, [[1, 128]], 0)
-        cut("g")
+        mask("m16", C, 16)
+        iota(R("D1"), [[1, 16]], 1)
+        iota(R("XS", 0, 64), [[1, 64]], 0)
+        iota(R("XS", 128, 256), [[1, 128]], 0)
         mask("m64", 256, 64)
-        cut("g")
-        iota("tie", 0, C, [[0, 3], [-1, 64]], -33)
-        cut("g")
-        mask("m8", C, 8)
-        iota("MOD", 0, C, [[0, 2], [1, H]], 0)
-        iota("MOD", C, 288, [[1, H]], H)
-        iota("MOD", 288, 480, [[1, C]], 0)
+        iota(R("tie"), [[0, 3], [-1, 64]], -33)
+        iota(R("IOb"), [[1, C]], 0)
+        iota(R("MOD", 0, C), [[0, 2], [1, H]], 0)
+        iota(R("MOD", C, 288), [[1, H]], H)
+        iota(R("MOD", 288, 480), [[1, C]], 0)
 
-    def unwrap(out, row, n, reads, writes):
-        scan(out, T.ext[:, 0:n], row, 0.0, A.mult, A.add, ["ext"] + reads, writes)
+    def rank_constants():
+        together([lambda: ts(R("L15"), R("c16", 0, 6), 15.25, A.add), lambda: ts(c8, cq, 7.5, A.is_gt, 0.25, A.add),
+                  lambda: ts(cE, cown, -0.5, A.add, cM, A.mult)])
 
-    def count_all(raw, rraw, a0):
-        for c in range(NV, 12):
-            k = c - NV
-            act(T.JK[:, C * k:C * k + C], T.E[:], ["E", rraw(c), rc(9)], [("JK", C * k, C * k + C), ("AC", a0 + c, a0 + c + 1)],
-                scale=cnM, bias=raw(c), func=F.Sign, acc=T.AC[:, a0 + c:a0 + c + 1])
-        cut("s")
-        for c in range(NV):
-            ts(T.CMP[:, C * c:C * c + C], T.E[:], cM, raw(c), A.mult, A.is_gt, ["E", rraw(c), rc(8)], [("CMP", C * c, C * c + C)])
-            if c % 2 == 1:
-                cut("v")
-        cut("v")
-        for c in range(NV):
-            scan(T.CNT[:, C * c:C * c + C], T.ones[:, 0:C], T.CMP[:, C * c:C * c + C], 0.0, A.mult, A.add,
-                 ["ones", ("CMP", C * c, C * c + C)], [("CNT", C * c, C * c + C)])
-        cut("v")
+    def hold_constants():
+        ts(R("tmp"), R("ext", 0, 64), 1.0 + 2.0 ** -10, A.min, -1.0, A.add)
+        ts(cS, cM, -1.0, A.add, 2.0 ** 20, A.min)
+        ts(R("L8"), R("c16", 0, 6), 0.125, A.mult, c8, A.add)
 
-    hw = lambda n, h: T[n][:, HB[h]:HB[h + 1]]
-    hl = lambda n, h: T[n][:, HB[h]:HB[h] + H]
-    rw_ = lambda n, h: (n, HB[h], HB[h + 1])
-    rl_ = lambda n, h: (n, HB[h], HB[h] + H)
+    def rank_constants_scalar():
+        w16 = lambda k: (T.w16[:, k:12:4, :], [("w16", frozenset(16 * c + i for c in range(k, 12, 4) for i in range(16)))])
+        together([lambda: act(cnM, cM, scale=-1.0), lambda: act(cnMe, cM, scale=-(1.0 + 2.0 ** -22)),
+                  lambda: act(R("ext", H, C), R("ext", 0, H))] + [lambda k=k: fill(w16(k), 48, W16[k]) for k in range(4)] +
+                 [lambda: fill(R("KB", 64, 128), 64, 0.0), lambda: fill(R("KB", C, 320), 128, 0.0)])
+
+    def segment_constants_scalar():
+        together([lambda k=k: fill(R("wm", k, 12, 4), 3, -0.5 * W16[k]) for k in range(4)] +
+                 [lambda: act(R("exa"), R("tmp"), scale=2.0 ** 30), lambda: act(R("wf"), R3("w16", 0, 12, 0, 16))])
+
+    def key_constants_scalar():
+        together([lambda s=s: act(R("TE", 72 * s, 72 * s + 72), R("IO", 0, 72), scale=W64[s],
+                                  bias=W64[s] * (-32.0 if s == 0 else 1.0)) for s in range(3)])
+
+    def pick_constants_scalar():
+        wl = [193.0 - 2.0 ** m for m in range(7)] + [1.0]
+        wr = [193.0 - 2.0 ** (m + 1) for m in range(7)] + [1.0]
+        together([lambda m=m: fill(R("TH", m, H, 8), 12, 2.0 ** (m + 1) if m < 7 else 1e9) for m in range(8)] +
+                 [lambda m=m, n=n, w=w: fill(R(n, m, H, 8), 12, w[m - 1] / w[m] if m else 0.0)
+                  for n, w in (("RL", wl), ("RR", wr)) for m in range(8)])
+
+    def unwrap(out, row, n):
+        scan(out, R("ext", 0, n), row)
+
+    def signs(c0, cols, row, thr, scale, a0):
+        n = len(row(cols[0])[1][0][1])
+        together([lambda c=c: act(R("JK", n * (c - c0), n * (c - c0) + n), row(c), scale=scale, bias=thr(c), func=F.Sign,
+                                  acc=R("AC", a0 + c, a0 + c + 1)) for c in cols])
+
+    hw = lambda n, h: R(n, HB[h], HB[h + 1])
+    hl = lambda n, h: R(n, HB[h], HB[h] + H)
+    half = lambda n, h, w=H, o=0: R(n, o + w * h, o + w * h + w)
 
     for t in range(2):
+        first = t == 0
         peer = T.cores[rank ^ (1 << t)]
-        X, qx, sx = "X%d" % t, "qx%d" % t, "sx%d" % t
-        lq, lp, ol, lo, Bt, qf, sf = ["%s%d" % (n, t) for n in ("lq", "lp", "ol", "lo", "Bt", "qf", "sf")]
-        xr = [X] if t == 0 else [X + "b%d" % b for b in range(4)]
-        quant(T[qx][:], T[sx][:], T[X][:], xr, [qx])
-        mm(4, T.qu[:], T.su[:], T[qx][:], T[sx][:], ["qu", qx])
-        cut("t")
-        send(peer, T[lq][:].bitcast(dt.uint8), T[qx][:].bitcast(dt.uint8), "ax%d" % t, [qx])
-        send(peer, T[lp][:], T[sx][:], "ax%d" % t, [qx])
-        arrival(peer, "ax%d" % t, 2, [lq])
-        if t == 0:
-            late_vector()
-            late_scalar()
+        X, qx, sx = R("X%d" % t), R("qx%d" % t), R("sx%d" % t)
+        lq, lp, ol, lo, qf, sf = [R("%s%d" % (n, t)) for n in ("lq", "lp", "ol", "lo", "qf", "sf")]
+        Bt, Xn = "Bt%d" % t, "X%d" % (t + 1)
+        quant(qx, sx, X)
+        mm(4, R("qu"), R("su"), qx, sx)
+        send(peer, u8(lq), u8(qx), "ax%d" % t)
+        send(peer, lp, sx, "ax%d" % t)
+        arrival(peer, "ax%d" % t, 2, lq, lp)
+        if first:
+            after_scores_vector()
+            after_scores_scalar()
+            spread_ext()
             late_gpsimd()
         for h in range(2):
-            for k in range(2):
-                ts(T.BT[:, 6 * h:6 * h + 6, 16 * k:16 * k + 16], T.ps[:, 2048 + H * h:2048 + H * h + H], 0.0, None, A.is_gt,
-                   None, [("ps", 4, 5)], [("BT", 2 * h + k, 2 * h + k + 1)])
-            cut("v")
+            together([lambda k=k: ts(R3("BT", 6 * h, 6 * h + 6, 16 * k, 16 * k + 16), bank(4, H * h, H * h + H), cthr, A.is_gt,
+                                     cw, A.mult) for k in range(2)])
         for h in range(2):
-            op("v", lambda: g.vector.transpose(T.TB[:, C * h:C * h + C], T.BT[:, 6 * h:6 * h + 6, :]),
-               [("BT", 2 * h, 2 * h + 2)], [("TB", h, h + 1)])
-            cut("v")
+            o, i = half("TB", h, C), R3("BT", 6 * h, 6 * h + 6, 0, 32)
+            op("v", lambda: g.vector.transpose(o[0], i[0]), i[1], o[1])
         for h in range(2):
-            scan(T.RB[:, C * h:C * h + C], T.cm[:], T.TB[:, C * h:C * h + C], 0.0, A.mult, A.add, ["cm", ("TB", h, h + 1)],
-                 [("RB", h, h + 1)])
-            cut("v")
+            scan(half("RB", h, C), half("cf", h, C), half("TB", h, C))
         for h in range(2):
-            rb = T.RB[:, C * h + 23:C * h + C:32]
-            tt(T.PP[:, 18 * h + 1:18 * h + 18:3], rb, T.thc[:, 6 * h:6 * h + 6], A.is_lt, [("RB", h, h + 1), "thc"],
-               [("PP1", h, h + 1)])
-            tt(T.PP[:, 18 * h + 2:18 * h + 18:3], rb, T.cj[:, 6 * h:6 * h + 6], A.mult, [("RB", h, h + 1), "cj"],
-               [("PP2", h, h + 1)])
-            cut("v")
+            tt(sm(0, 6 * h, 6 * h + 6), R("RB", C * h + 26, C * h + C, 32), R("RB", C * h + 30, C * h + C, 32), A.add)
         for h in range(2):
-            scan(T.PS[:, 18 * h:18 * h + 18], T.PM[:, 18 * h:18 * h + 18], T.PP[:, 18 * h:18 * h + 18], 0.0, A.mult, A.add,
-                 ["PM0", "PM1", "PM2", "PM3", "PP0", "PP3", ("PP1", h, h + 1), ("PP2", h, h + 1)], [("PS", h, h + 1)])
-            cut("v")
+            ts(half("LS", h, 6), sm(0, 6 * h, 6 * h + 6), 0.25 - H * h, A.add)
         for h in range(2):
-            ts(T.LS[:, 6 * h:6 * h + 6], T.PS[:, 18 * h + 2:18 * h + 18:3], MAGIC, -MAGIC, A.add, A.add, [("PS", h, h + 1)],
-               [("LS", 6 * h, 6 * h + 6)])
-            cut("v")
-        for h in range(2):
-            act(hl("PA", h), T.IO[:, 0:HB[h + 1] - HB[h]].indirect(T.LS[:, 6 * h:6 * h + 6]), ["IO", ("LS", 6 * h, 6 * h + 6)],
-                [rl_("PA", h)])
-            cut("s")
-        pn, vn = ["PA", "PB", "PA", "PB", "PA", "PB", "PA"], ["V0", "VA", "VB", "VA", "VB", "VA", "VB"]
+            act(hl("PA", h), ind(R("IO", 0, HB[h + 1] - HB[h]), half("LS", h, 6)))
+        pn, vn = ["PA", "PB", "PA", "PB", "PA", "PB", "PA"], ["V0", "VA", "VB", "VA", "VB", "VA"]
         for r in range(6):
             for h in range(2):
-                l0 = 12 * (r // 3) + 6 * h
-                L, rl = T.LS[:, l0:l0 + 6], ("LS", l0, l0 + 6)
-                own, ro = (T.V0D[:], "V0D") if r < 3 else (T.VD[:, H * h:H * h + H], ("VD", h, h + 1))
-                act(hl(pn[r + 1], h), hw(pn[r], h).indirect(L), [rw_(pn[r], h), rl], [rl_(pn[r + 1], h)])
-                cut("s")
-                tt(hl(vn[r + 1], h), hw(vn[r], h).indirect(L), own, A.add, [rw_(vn[r], h), ro, rl], [rl_(vn[r + 1], h)])
-                cut("v")
+                L = half("LS", h, 6, 12 * (r // 3))
+                act(hl(pn[r + 1], h), ind(hw(pn[r], h), L))
+                tt(hl(vn[r + 1], h) if r < 5 else half("K16", h), ind(hw(vn[r], h), L),
+                   hl("V0", 1 - h) if r < 3 else half("VD", h), A.add)
             if r == 2:
-                if t == 0:
-                    late_vector2(0)
-                    late_scalar2()
                 for h in range(2):
-                    cp(T.VD[:, H * h:H * h + H], hl("VA", h), [rl_("VA", h)], [("VD", h, h + 1)])
-                    cut("v")
+                    cp(half("VD", h), hl("VA", h))
+                if first:
+                    rank_constants_scalar()
+                    together([lambda b=b: quant(R("qe", 128 * b, 128 * b + 128), R("se", 128 * b, 128 * b + 128),
+                                                R("Z", 3 - b, 515 - b)) for b in range(2)])
                 for h in range(2):
-                    unwrap(T.RAW[:, H * h:H * h + H], hl("PB", h), H, [rl_("PB", h)], [("RAW", H * h, H * h + H)])
-                    cut("v")
-                if t == 0:
-                    late_vector2(2)
+                    unwrap(half("RAW", h), hl("PB", h), H)
+                if first:
+                    together([lambda b=b: quant(R("qe", 128 * b, 128 * b + 128), R("se", 128 * b, 128 * b + 128),
+                                                R("Z", 3 - b, 515 - b)) for b in range(2, 4)])
                 for h in range(2):
-                    ts(T.LS[:, 12 + 6 * h:18 + 6 * h], T.RAW[:, H * h + 15:H * h + H:16], cim, 0.25, A.mult, A.add,
-                       [("RAW", H * h, H * h + H), rc(6)], [("LS", 12 + 6 * h, 18 + 6 * h)])
-                    cut("v")
-                if t == 0:
-                    late_vector2(1)
+                    ts(half("LS", h, 6, 12), R("RAW", H * h + 15, H * h + H, 16), cim, A.mult, 0.25, A.add)
         for b in range(4):
-            mm(4 + b, T.qe[:, 128 * b:128 * b + 128], T.se[:, 128 * b:128 * b + 128], T[lq][:], T[lp][:], [("qe", b, b + 1), lq])
-            cut("t")
-        for b in range(4):
-            mm(b, T.qe[:, 128 * b:128 * b + 128], T.se[:, 128 * b:128 * b + 128], T[qx][:], T[sx][:], [("qe", b, b + 1), qx])
-        cut("t")
-        blk = lambda c: T.VB[:, HB[c // 6] + 16 * (c % 6):HB[c // 6] + 16 * (c % 6) + 16]
-        rvb = lambda c: rl_("VB", c // 6)
-        rr2 = lambda c: ("RAW2", H * (c // 6), H * (c // 6) + H)
-
-        def sign16(c, bias, rb):
-            act(T.JK[:, 16 * c:16 * c + 16], blk(c), [rvb(c), rb, rc(9)], [("JK", 16 * c, 16 * c + 16), ("AC", c, c + 1)],
-                scale=cnM, bias=bias, func=F.Sign, acc=T.AC[:, c:c + 1])
-
-        def enter16(cs):
-            for c in cs:
-                ts(T.CMP[:, 96 + 16 * c:112 + 16 * c], blk(c), cM, T.sm[:, 60 + c:61 + c], A.mult, A.is_lt,
-                   [rvb(c), rs(5), rc(8)], [("CMP", 96 + 16 * c, 112 + 16 * c)])
-            cut("v")
-
+            mm(4 + b, R("qe", 128 * b, 128 * b + 128), R("se", 128 * b, 128 * b + 128), lq, lp)
+        together([lambda b=b: mm(b, R("qe", 128 * b, 128 * b + 128), R("se", 128 * b, 128 * b + 128), qx, sx) for b in range(4)])
         for h in range(2):
-            unwrap(T.RAW2[:, H * h:H * h + H], hl("VB", h), H, [rl_("VB", h)], [("RAW2", H * h, H * h + H)])
-            cut("v")
+            act(half("KS", h), half("K16", h), scale=cM)
         for h in range(2):
-            unwrap(T.RAW[:, H * h:H * h + H], hl("PA", h), H, [rl_("PA", h)], [("RAW", H * h, H * h + H)])
-        cut("v")
-        for c in range(6):
-            sign16(c, T.RAW2[:, 16 * c + 15:16 * c + 16], rr2(c))
-        cut("s")
-        ts(sm(5), T.RAW2[:, 15:C:16], T.tmp[:, 15:16], cbm, A.add, A.add, ["RAW2", ("tmp", 0, 16), rc(10)], [rs(5)])
-        cut("v")
-        for c in range(6, 12):
-            ts(T.CMP[:, 16 * c - 96:16 * c - 80], blk(c), cM, T.RAW2[:, 16 * c + 15:16 * c + 16], A.mult, A.is_le,
-               [rvb(c), rr2(c), rc(8)], [("CMP", 16 * c - 96, 16 * c - 80)])
-        cut("v")
-        for c in range(6, 12):
-            sign16(c, T.sm[:, 60 + c:61 + c], rs(5))
-        cut("s")
-        ts(T.LX[:, 0:24:2], T.RAW[:, 15:C:16], cim, 0.25 - H, A.mult, A.add, ["RAW", rc(6)], ["LX"])
-        cut("v")
-        enter16((0, 1))
-        ts(T.LR[:, 0:6], T.AC[:, 0:6], 0.5, 8.75, A.mult, A.add, [("AC", 0, 6)], [("LR", 0, 6)])
-        cut("v")
-        scan(T.CNT[:, 0:96], T.m16[:], T.CMP[:, 0:96], 0.0, A.mult, A.add, ["m16", ("CMP", 0, 96)], [("CNT", 0, 96)])
-        cut("v")
-        enter16((2, 3, 4))
-        cp(T.LR[:, 6:12], T.CNT[:, 15:96:16], [("CNT", 0, 96)], [("LR", 6, 12)])
-        cut("v")
-        enter16((5,))
-        for s in range(3):
-            o0 = KB0[s] + 64 * s
-            ts(T.KB[:, o0:o0 + 16], T.IO[:, 0:24].indirect(T.LR[:, 4 * s:4 * s + 1]), W16[0], None, A.mult, None,
-               ["IO", ("LR", 4 * s, 4 * s + 1)], [("KB", o0, o0 + 16)])
-            cut("v")
-        tt(T.U[:], T.IO[:, 0:24].indirect(T.LR[:]), T.w16[:], A.mult, ["IO", "LR", "w16"], ["U"])
-        cut("v")
-        scan(T.CNT[:, 96:C], T.m16[:], T.CMP[:, 96:C], 0.0, A.mult, A.add, ["m16", ("CMP", 96, C)], [("CNT", 96, C)])
-        ts(sm(6), T.LR[:], -1.0, 1.0, A.mult, A.add, ["LR"], [rs(6)])
-        if t == 0:
-            late_vector2(3)
-        cut("v")
-        for be in range(4):
+            unwrap(half("RAW2", h), half("K16", h), H)
+            if first and h == 0:
+                hold_constants()
+                segment_constants_scalar()
+        for h in range(2):
+            unwrap(half("RAW", h), hl("PA", h), H)
+            tt(half("C16", h), ind(half("RAW2", h), R("L15")), half("KS", h), A.is_gt)
+            ts(sm(2, 6 * h, 6 * h + 6), R("RAW2", H * h + 15, H * h + H, 16), cE, A.add)
+        scan(half("N16", 0), half("m16", 0), half("C16", 0))
+        ts(R("LX", 0, 24, 2), R("RAW", 15, C, 16), cim, A.mult, 0.25 - H, A.add)
+        scan(half("N16", 1), half("m16", 1), half("C16", 1))
+        for h in range(2):
+            cp(half("LR", h, 6), R("N16", H * h + 15, H * h + H, 16))
+        enter16 = lambda cols: signs(0, cols, lambda c: R("K16", 16 * c, 16 * c + 16), lambda c: sm(2, c, c + 1), cnM, 24)
+
+        def outside(be):
             for s in (1, 2):
                 c = 4 * s + be
                 o0 = XB0[s] + 16 * c
-                act(T.XS[:, o0:o0 + 16], T.XS[:, XB0[s]:o0].indirect(T.LX[:, 2 * c:2 * c + 1]), [("XS", XB0[s], o0), "LX"],
-                    [("XS", o0, o0 + 16)])
-            cut("s")
-            if be < 2:
-                act(T.Tp[:, C * be:C * be + C], bank(4 + be), [("ps", 4 + be, 5 + be)], [("Tp", be, be + 1)])
-                cut("s")
-            elif be == 2 and t == 0:
-                late_scalar3()
+                act(R("XS", o0, o0 + 16), ind(R("XS", XB0[s], o0), R("LX", 2 * c, 2 * c + 1)))
+
+        def unpack(b):
+            act(R("Tp", C * b, C * b + C), bank(4 + b))
+
+        enter16(list(range(6)))
+        enter16([6, 7, 8])
+        for s in range(3):
+            o0 = KB0[s] + 64 * s
+            act(R("KB", o0, o0 + 16), ind(R("D1"), R("LR", 4 * s, 4 * s + 1)), scale=W16[0])
+        for h in range(2):
+            tt(half("U", h), ind(R("D1"), half("LR", h, 6)), half("wf", h), A.mult)
+        tt(sm(11), R("N16", 15, C, 16), R("wf", 0, C, 16), A.mult)
+        outside(0)
+        enter16([9, 10, 11])
+        outside(1)
+        unpack(0)
+        outside(2)
+        unpack(1)
+        outside(3)
+        if first:
+            ts(R("wsh"), R("wm"), 16.0, A.mult, cS, A.add)
+            key_constants_scalar()
         for be in range(1, 4):
             for s in range(3):
                 c = 4 * s + be
                 o0 = KB0[s] + 16 * c
-                tt(T.KB[:, o0:o0 + 16], T.KB[:, KB0[s]:o0].indirect(T.LX[:, 2 * c:2 * c + 1]), T.U[:, 16 * c:16 * c + 16],
-                   A.add, [("KB", KB0[s], o0), "LX", "U"], [("KB", o0, o0 + 16)])
-                cut("v")
+                tt(R("KB", o0, o0 + 16), ind(R("KB", KB0[s], o0), R("LX", 2 * c, 2 * c + 1)), R("U", 16 * c, 16 * c + 16), A.add)
             if be == 1:
-                cp(T.sm[:, 156:162], T.CNT[:, 111:C:16], [("CNT", 96, C)], [("sm", 156, 162)])
-                ts(T.sm[:, 162:168], T.AC[:, 6:12], 0.5, 8.0, A.mult, A.add, [("AC", 6, 12)], [("sm", 162, 168)])
+                tt(sm(3), R("wsh"), sm(11), A.add)
             elif be == 2:
-                tt(sm(7), sm(6), sm(13), A.add, [rs(6), rs(13)], [rs(7)])
+                tt(sm(4), R("AC", 24, 36), R("wm"), A.mult)
             else:
-                tt(sm(8), sm(7), T.wm[:, 0:12], A.mult, [rs(7), "wm"], [rs(8)])
-            cut("v")
-        live = lambda s: T.KB[:, KB0[s] + 64 * s:KB0[s] + 64 * s + 64]
-        rlive = lambda s: ("KB", KB0[s] + 64 * s, KB0[s] + 64 * s + 64)
-        for s in range(3):
-            unwrap(T.RK[:, 64 * s:64 * s + 64], live(s), 64, [rlive(s)], [("RK", 64 * s, 64 * s + 64)])
-            cut("v")
-
-        def sign64(cs):
-            for c in cs:
-                s = c // 4
-                act(T.JK[:, 64 * c:64 * c + 64], live(s), [rlive(s), ("RK", 64 * s, 64 * s + 64), rc(9)],
-                    [("JK", 64 * c, 64 * c + 64), ("AC", 12 + c, 13 + c)], scale=cnM, bias=T.RK[:, 16 * c + 15:16 * c + 16],
-                    func=F.Sign, acc=T.AC[:, 12 + c:13 + c])
-            cut("s")
-
-        sign64(range(8))
+                tt(sm(5), sm(3), sm(4), A.add)
+        live = lambda s: R("KB", KB0[s] + 64 * s, KB0[s] + 64 * s + 64)
+        hold = lambda s: scan(R("RA", 64 * s - 64, 64 * s), R("exa"), live(s), A.add, A.max)
+        unwrap(R("RK", 0, 64), live(0), 64)
+        unwrap(R("RK", 64, 128), live(1), 64)
+        hold(1)
+        hold(2)
+        ts(sm(6, 0, 4), sm(5, 0, 4), cS, A.subtract, cnM, A.mult)
         for s in (1, 2):
             o0 = XB0[s] + 64 * s
-            unwrap(T.RX[:, 64 * s - 64:64 * s], T.XS[:, o0:o0 + 64], 64, [("XS", o0, o0 + 64)], [("RX", 64 * s - 64, 64 * s)])
-        cut("v")
-        tt(sm(9), T.RK[:, 15:C:16], sm(8), A.add, ["RK", rs(8)], [rs(9)])
-        cut("v")
-        ts(T.LY[:], T.RX[:, 15:128:16], cim, 0.25, A.mult, A.add, ["RX", rc(6)], ["LY"])
-        cut("v")
-        for s in (1, 2, 0):
-            for c in range(4 * s, 4 * s + 4):
-                ts(T.CMP[:, 64 * c:64 * c + 64], live(s), cM, T.sm[:, 108 + c:109 + c], A.mult, A.is_lt,
-                   [rlive(s), rs(9), rc(8)], [("CMP", 64 * c, 64 * c + 64)])
-            cut("v")
-        for s in (1, 2, 0):
-            lo_, hi_ = 256 * s, 256 * s + 256
-            if s == 0:
-                ts(T.LR2[:, 0:8], T.AC[:, 12:20], 0.5, 32.75, A.mult, A.add, [("AC", 12, 20)], ["LR2"])
-                cut("v")
-            scan(T.CNT[:, lo_:hi_], T.m64[:], T.CMP[:, lo_:hi_], 0.0, A.mult, A.add, ["m64", ("CMP", lo_, hi_)],
-                 [("CNT", lo_, hi_)])
-            cut("v")
-        cp(T.LE[:, 4:12], T.CNT[:, 319:768:64], [("CNT", 256, 768)], [("LE", 1, 3)])
-        cut("v")
-        cp(T.sm[:, 160:168], T.CNT[:, 319:768:64], [("CNT", 256, 768)], [("sm", 160, 168)])
-        cut("v")
-        cp(T.LE[:, 0:4], T.CNT[:, 63:256:64], [("CNT", 0, 256)], [("LE", 0, 1)])
-        cp(T.sm[:, 156:160], T.CNT[:, 63:256:64], [("CNT", 0, 256)], [("sm", 156, 160)])
-        cut("v")
-        act(T.G[:, 0:64], T.IO[:, 0:72].indirect(T.LR2[:, 0:4]), ["IO", "LR2"], [("G", 0, 64)], scale=W64[0],
-            bias=-33.0 * W64[0])
-        act(T.U1[:], T.IO[:, 0:72].indirect(T.LR2[:, 4:8]), ["IO", "LR2"], ["U1"], scale=W64[1])
-        cut("s")
-        sign64(range(8, 12))
-        for b in range(2, 4):
-            act(T.Tp[:, C * b:C * b + C], bank(4 + b), [("ps", 4 + b, 5 + b)], [("Tp", b, b + 1)])
-        cut("s")
+            unwrap(R("RX", 64 * s - 64, 64 * s), R("XS", o0, o0 + 64), 64)
+        rk = lambda c: R("RK", 16 * c + 15, 16 * c + 16)
+        for s in range(2):
+            signs(0, list(range(4 * s, 4 * s + 4)), lambda c: live(c // 4), rk, cnMe, 0)
 
-        def enter64(s):
-            out, ro = (T.E[:, 0:64], ("E", 0, 64)) if s == 0 else (T.EP[:, 64 * s - 64:64 * s], ("EP", 64 * s - 64, 64 * s))
-            tt(out, T.TE[:, 72 * s:72 * s + 72].indirect(T.LE[:, 4 * s:4 * s + 4]), T.tie[:, 64 * s:64 * s + 64], A.add,
-               ["TE", ("LE", s, s + 1), "tie"], [ro])
-            cut("v")
+        def below(s):
+            together([lambda c=c: ts(R("CMP", 64 * c - 256, 64 * c - C), live(s), sm(5, c, c + 1), A.add,
+                                     R("RA", 16 * c - 49, 16 * c - 48), A.is_lt) for c in range(4 * s, 4 * s + 4)])
 
-        enter64(1)
-        enter64(2)
-        tt(T.G[:, 64:128], T.G[:, 0:64].indirect(T.LY[:, 0:4]), T.U1[:], A.add, [("G", 0, 64), "LY", "U1"], [("G", 64, 128)])
-        cut("v")
-        tt(T.E[:, 64:128], T.G[:, 0:64].indirect(T.LY[:, 0:4]), T.EP[:, 0:64], A.add, [("G", 0, 64), "LY", ("EP", 0, 64)],
-           [("E", 64, 128)])
-        cut("v")
-        enter64(0)
-        tt(T.E[:, 128:C], T.G[:, 0:128].indirect(T.LY[:, 4:8]), T.EP[:, 64:128], A.add, ["G", "LY", "EP"], [("E", 128, C)])
-        cut("v")
-        unwrap(T.RE[:, 0:128], T.E[:, 0:128], 128, [("E", 0, 128)], [("RE", 0, 128)])
-        cut("v")
-        unwrap(T.RE[:, 128:C], T.E[:, 128:C], 64, [("E", 128, C)], [("RE", 128, C)])
-        cut("v")
-        count_all(lambda c: T.RE[:, 16 * c + 15:16 * c + 16], lambda c: ("RE", 16 * c, 16 * c + 16), 24)
-        ts(sm(6), T.AC[:, 12:24], -0.5, -31.5, A.mult, A.add, [("AC", 12, 24)], [rs(6)])
-        tt(sm(10), T.RE[:, 15:C:16], T.tiem[:], A.add, ["RE", "tiem"], [rs(10)])
-        cut("v")
-        cp(T.LP[:, 0:NV], T.CNT[:, C - 1:NV * C:C], [("CNT", 0, NV * C)], [("LP", 0, NV)])
-        ts(T.LP[:, NV:12], T.AC[:, 24 + NV:36], -0.5, 95.75, A.mult, A.add, [("AC", 24, 36)], [("LP", NV, 12)])
-        cut("v")
-        tt(sm(7), sm(6), sm(13), A.add, [rs(6), rs(13)], [rs(7)])
-        cp(T.LV[:, 0:8 * NV:8], T.CNT[:, C - 1:NV * C:C], [("CNT", 0, NV * C)], ["LVp"])
-        ts(T.LV[:, 8 * NV:96:8], T.AC[:, 24 + NV:36], -0.5, 95.5, A.mult, A.add, [("AC", 24, 36)], ["LVq"])
-        cut("v")
-        if t == 1:
-            for h in range(2):
-                act(T.PR[:, H * h:H * h + H], hw("MOD", h).indirect(T.LS[:, 6 * h:6 * h + 6]), ["MOD", ("LS", 0, 12)],
-                    [("PR", h, h + 1)])
-            cut("s")
-        cp(T.O[:].indirect(T.LP[:]), T.IO[:, 0:C], ["IO", "LP"], ["O"])
-        cut("v")
-        tt(sm(8), sm(7), T.wm[:, 12:24], A.mult, [rs(7), "wm"], [rs(8)])
-        cut("v")
-        unwrap(T.RAW[:], T.O[:], C, ["O"], ["RAW"])
-        cut("v")
-        tt(sm(11), sm(10), sm(8), A.subtract, [rs(10), rs(8)], [rs(11)])
-        cut("v")
-        ts(T[ol][:], T.RAW[:, 15:C:16], cim, 0.25, A.mult, A.add, ["RAW", rc(6)], [ol])
-        send(peer, T[lo][:], T[ol][:], "al%d" % t, [ol])
-        arrival(peer, "al%d" % t, 1, [lo])
-        if t == 1:
-            dma("y", "dop", T.op[:], T.PR[0:128:16, :], ["PR"], [])
-        cut("v")
-        count_all(lambda c: T.sm[:, 132 + c:133 + c], lambda c: rs(11), 36)
-        if t == 0:
-            quant(T.qv[:], T.sv[:], T.vt[:], ["vt"], ["qv"])
-            cut("v")
-        ts(T.LV[:, 96:96 + 8 * NV:8], T.CNT[:, C - 1:NV * C:C], -1.0, None, A.add, None, [("CNT", 0, NV * C)], ["LVe"])
-        ts(T.LV[:, 96 + 8 * NV:C:8], T.AC[:, 36 + NV:48], -0.5, 95.0, A.mult, A.add, [("AC", 36, 48)], ["LVf"])
-        tt(sm(12), T.LV[:, 96:C:8], T.LV[:, 0:96:8], A.subtract, ["LVp", "LVq", "LVe", "LVf"], [rs(12)])
-        cut("v")
-        for m in range(1, 8):
-            ts(T.LV[:, m:96:8], sm(12), 2.0 ** m - 1.0, 193.0 - 2.0 ** (m - 1), A.is_gt, A.mult, [rs(12)], ["LV%d" % m])
-        cut("v")
-        for b in (2, 3):
-            act(T[Bt][:, b:768:4], T.Tp[:, C * b:C * b + C].indirect(T[lo][:]), [("Tp", b, b + 1), lo], [Bt + "b%d" % b])
-        for b in (0, 1):
-            cp(T[Bt][:, b:768:4], T.Tp[:, C * b:C * b + C].indirect(T[lo][:]), [("Tp", b, b + 1), lo], [Bt + "b%d" % b])
-        cut("v")
-        for m in range(1, 8):
-            if m == 4:
-                cut("v")
-                quant(T[qf][:], T[sf][:], T[Bt][:], [Bt + "b%d" % b for b in range(4)], [qf])
-                for b in range(4):
-                    mm(4 + b, T.qw[:, 128 * b:128 * b + 128], T.sw[:, 128 * b:128 * b + 128], T[qf][:], T[sf][:],
-                       ["qw", "sw", qf])
-                    cut("t")
-                cut("v")
-            ts(T.LV[:, 96 + m:C:8], sm(12), 2.0 ** m - 1.0, 193.0 - 2.0 ** m, A.is_gt, A.mult, [rs(12)], ["LU%d" % m])
-        scan(T.LW[:], T.m8[:], T.LV[:], 0.0, A.mult, A.add,
-             ["m8", "LVp", "LVq", "LVe", "LVf"] + ["LV%d" % m for m in range(1, 8)] + ["LU%d" % m for m in range(1, 8)], ["LW"])
-        cut("v")
-        ts(T.TAB[:, 0:C], bank(4), 0.03125, None, A.mult, None, [("ps", 4, 5)], [("TAB", 0, C)])
-        cut("v")
-        cp(T.LL[:], T.LW[:, 7:C:8], ["LW"], ["LL"])
-        cut("v")
+        below(1)
+        tt(sm(4, 0, 4), R("RK", 15, 64, 16), sm(6, 0, 4), A.add)
+        below(2)
+        ts(R("LR2", 0, 4), R("AC", 0, 4), 0.5, A.mult, 32.25, A.add)
+        signs(-8, [0, 1, 2, 3], lambda c: live(0), lambda c: sm(4, c, c + 1), cnMe, 12)
+        scan(half("N64", 0, 256), R("m64"), half("CMP", 0, 256))
+        ts(R("LY"), R("RX", 15, 128, 16), cim, A.mult, 0.25, A.add)
+        unwrap(R("RK", 128, C), live(2), 64)
+        ts(R("LR2", 4, 8), R("AC", 4, 8), 0.5, A.mult, 32.25, A.add)
+        act(R("GE", 0, 64), ind(R("IO", 0, 72), R("LR2", 0, 4)), scale=W64[0], bias=-32.0 * W64[0])
+        act(R("UE", 0, 64), ind(R("IO", 0, 72), R("LR2", 4, 8)), scale=W64[1], bias=W64[1])
+        scan(half("N64", 1, 256), R("m64"), half("CMP", 1, 256))
+        cp(R("LE", 4, 8), R("N64", 63, 256, 64))
+        ts(R("LE", 0, 4), R("AC", 12, 16), 0.5, A.mult, 32.25, A.add)
+        cp(R("LE", 8, 12), R("N64", 319, 512, 64))
+
+        def enter64(s, out):
+            tt(out, ind(R("TE", 72 * s, 72 * s + 72), R("LE", 4 * s, 4 * s + 4)), R("tie", 64 * s, 64 * s + 64), A.add)
+
+        signs(-4, [8, 9, 10, 11], lambda c: live(2), rk, cnMe, 0)
+        unpack(2)
+        unpack(3)
+        enter64(1, R("UE", 64, 128))
+        enter64(2, R("UE", 128, C))
+        tt(R("GE", 64, 128), ind(R("GE", 0, 64), R("LY", 0, 4)), R("UE", 0, 64), A.add)
+        enter64(0, R("GE", 256, 320))
+        ts(sm(6, 0, 4), R("AC", 8, 12), -0.5, A.mult, -32.0, A.add)
+        tt(R("GE", 128, 256), ind(R("GE", 0, 128), R("LY")), R("UE", 64, C), A.add)
+        unwrap(R("RE", 128, C), R("GE", 256, 320), 64)
+        unwrap(R("RG"), R("GE", 0, 128), 128)
+        tt(sm(7, 8, 12), sm(6, 0, 4), R("N64", 319, 512, 64), A.add)
+        unwrap(R("RE", 0, 128), R("GE", 128, 256), 128)
+        E = R("GE", 128, 320)
+        pos = lambda c: 16 * ((c - 4) % 12) + 15
+        ent = lambda c: R("RE", pos(c), pos(c) + 1)
+        above = lambda k, thr: ts(R("CMP", C * k, C * k + C), E, cM, A.mult, thr, A.is_gt)
+        total = lambda k: scan(R("CNT", C * k, C * k + C), R("ones", 0, C), R("CMP", C * k, C * k + C))
+        signs(1, [1, 2, 3], lambda c: E, ent, cnM, 24)
+        signs(1, [4, 5, 6, 7], lambda c: E, ent, cnM, 24)
+        for k, c in enumerate((0, 8, 9, 10, 11)):
+            above(k, ent(c))
+            if k == 2:
+                total(0)
+        total(1)
+        cp(R("LP", 0, 1), R("CNT", C - 1, C))
+        together([lambda k=k: total(k) for k in (2, 3, 4)])
+        together([lambda: ts(R("LP", 1, 8), R("AC", 25, 32), -0.5, A.mult, 95.75, A.add),
+                  lambda: cp(R("LP", 8, 12), R("CNT", 2 * C - 1, 5 * C, C))])
+        lea = lambda c: R("RG", 16 * c + 15, 16 * c + 16)
+        signs(NE, list(range(NE, 8)), lambda c: E, lea, cnM, 36)
+        op("v", lambda: g.vector.tensor_copy(T.O[:].indirect(T.LP[:]), T.IOb[:]), regs(R("IOb"), R("LP")), R("O")[1])
+        cp(sm(8), R("LP"))
+        ts(R("CMP", 0, C), E, cM, A.mult, lea(0), A.is_gt)
+        unwrap(R("RO"), R("O"), C)
+        ts(R("CMP", C, 2 * C), E, cM, A.mult, lea(1), A.is_gt)
+        ts(ol, R("RO", 15, C, 16), cim, A.mult, 0.25, A.add)
+        send(peer, lo, ol, "al%d" % t)
+        arrival(peer, "al%d" % t, 1, lo)
+        if first:
+            pick_constants_scalar()
+        else:
+            together([lambda h=h: act(half("PR", h), ind(hw("MOD", h), half("LS", h, 6))) for h in range(2)])
+            dma("y", "dop", T.op[:], (T.PR[0:128:16, :], R("PR")[1]))
+        for c in range(2, NE):
+            ts(R("CMP", C * c, C * c + C), E, cM, A.mult, lea(c), A.is_gt)
+        together([lambda c=c: scan(R("CNT", C * c, C * c + C), R("ones", 0, C), R("CMP", C * c, C * c + C)) for c in range(NE)])
+        ts(sm(9, NE, 8), R("AC", 36 + NE, 44), -0.5, A.mult, 96.0, A.add)
+        if first:
+            quant(R("qv"), R("sv"), R("vt"))
+        together([lambda: tt(sm(7, 0, NE), R("CNT", C - 1, NE * C, C), sm(8, 0, NE), A.subtract),
+                  lambda: tt(sm(7, NE, 8), sm(9, NE, 8), sm(8, NE, 8), A.subtract)])
+        tt(sm(10), sm(7), sm(8), A.add)
+        tt(R("FL"), ind(sm(7), R("L8")), R("TH"), A.is_ge)
+        together([lambda b=b: act(R(Bt, b, 768, 4), ind(R("Tp", C * b, C * b + C), lo)) for b in (2, 3)])
+        together([lambda b=b: cp(R(Bt, b, 768, 4), ind(R("Tp", C * b, C * b + C), lo)) for b in (0, 1)])
+        quant(qf, sf, R(Bt))
+        for b in range(4):
+            mm(4 + b, R("qw", 128 * b, 128 * b + 128), R("sw", 128 * b, 128 * b + 128), qf, sf)
+        together([lambda: scan(half("SL", 0), R("RL"), R("FL")), lambda: scan(half("SL", 1), R("RR"), R("FL"))])
+        ts(R("TAB", 0, C), bank(4), 0.03125, A.mult)
         for b in range(1, 4):
-            act(T.TAB[:, TW * b:TW * b + C], bank(4 + b), [("ps", 4 + b, 5 + b)], [("TAB", TW * b, TW * b + C)], scale=0.03125)
-            cut("s")
-        off = [193 * k - 2 ** k + 1 for k in range(9)]
+            act(R("TAB", TW * b, TW * b + C), bank(4 + b), scale=0.03125)
+        together([lambda: tt(sm(11), R("SL", 7, H, 8), sm(8), A.add), lambda: tt(sm(9), R("SL", H + 7, C, 8), sm(10), A.add)])
 
         def level(b, k):
-            n, h, a, o = 193 - 2 ** k, 2 ** (k - 1), TW * b + off[k - 1], TW * b + off[k]
-            scan(T.TAB[:, o:o + n], T.TAB[:, a:a + n], T.TAB[:, a + h:a + h + n], 1e29, A.min, A.max,
-                 [("TAB", a, a + h + n)], [("TAB", o, o + n)])
-            cut("v")
+            n, h, a, o = 193 - 2 ** k, 2 ** (k - 1), TW * b + OFF[k - 1], TW * b + OFF[k]
+            scan(R("TAB", o, o + n), R("TAB", a, a + n), R("TAB", a + h, a + h + n), A.min, A.max, 1e29)
 
-        def win(b):
-            return T.TAB[:, TW * b:TW * b + off[8]], ("TAB", TW * b, TW * b + off[8])
+        win = lambda b: R("TAB", TW * b, TW * b + OFF[8])
 
-        Xn = "X%d" % (t + 1)
+        def left(b):
+            act(R("G1", C * b, C * b + C), ind(win(b), R("LL", 0, 12)))
 
         def pick(b):
-            w, rw = win(b)
-            tt(T.MX[:, C * b:C * b + C], w.indirect(T.LL[:, 12:24]), T.G1[:, C * b:C * b + C], A.max,
-               [rw, "LL", ("G1", b, b + 1)], [("MX", b, b + 1)])
-            cut("v")
+            tt(R("MX", C * b, C * b + C), ind(win(b), R("LL", 12, 24)), R("G1", C * b, C * b + C), A.max)
 
         def plus(b):
-            tt(T[Xn][:, b:768:4], T.MX[:, C * b:C * b + C], bank(b), A.add, [("MX", b, b + 1), ("ps", b, b + 1)],
-               [Xn + "b%d" % b])
-            cut("v")
+            tt(R(Xn, b, 768, 4), R("MX", C * b, C * b + C), bank(b), A.add)
 
-        order = [(0, 1), (1, 1), (0, 2), (2, 1), (1, 2), (0, 3), (3, 1), (2, 2), (1, 3), (0, 4), (3, 2), (2, 3), (1, 4), (0, 5),
-                 (3, 3), (2, 4), (1, 5), (0, 6), (3, 4), (2, 5), (1, 6), (0, 7), (3, 5), (2, 6), (1, 7), (3, 6), (2, 7)]
-        for b, k in order:
-            level(b, k)
-            if k == 7:
-                w, rw = win(b)
-                act(T.G1[:, C * b:C * b + C], w.indirect(T.LL[:, 0:12]), [rw, "LL"], [("G1", b, b + 1)])
-                cut("s")
-        pick(0)
-        level(3, 7)
-        w, rw = win(3)
-        act(T.G1[:, 3 * C:4 * C], w.indirect(T.LL[:, 0:12]), [rw, "LL"], [("G1", 3, 4)])
-        cut("s")
-        pick(1)
-        plus(0)
-        pick(2)
-        pick(3)
-        plus(1)
-        plus(2)
-        plus(3)
+        steps = [(k + LAG[b], 0, level, (b, k)) for b in range(4) for k in range(1, 8)]
+        steps += [(7 + LAG[b], 1, left, (b,)) for b in range(4)]
+        steps += [(PICK[b], 2, pick, (b,)) for b in range(4)] + [(PLUS[b], 3, plus, (b,)) for b in range(4)]
+        for i, (_, _, fn, args) in enumerate(sorted(steps, key=lambda z: z[:2])):
+            fn(*args)
+            if i == 0:
+                together([lambda: ts(R("LL", 0, 12), sm(11), 0.25, A.add), lambda: ts(R("LL", 12, 24), sm(9), -0.75, A.add)])
 
-    quant(T.qx2[:], T.sx2[:], T.X2[:], ["X2b%d" % b for b in range(4)], ["qx2"])
-    mm(4, T.qv[:], T.sv[:], T.qx2[:], T.sx2[:], ["qv", "qx2"])
-    dma("s", "doc", T.oc[:], T.qx2[:].bitcast(dt.uint8), ["qx2"], [])
+    quant(R("qx2"), R("sx2"), R("X2"))
+    mm(4, R("qv"), R("sv"), R("qx2"), R("sx2"))
+    dma("s", "doc", T.oc[:], u8(R("qx2")))
     for k, e in enumerate(("y", "s", "y", "s")):
-        dma(e, "ds%d" % k, T.osc[4 * k:4 * k + 4, :], T.sx2[32 * k:32 * k + 4, :], ["qx2"], [])
-    cp(T.Y[:], bank(4), [("ps", 4, 5)], ["Y"])
-    dma("y", "dy", T.y[:], T.Y[:], ["Y"], [])
+        dma(e, "ds%d" % k, T.osc[4 * k:4 * k + 4, :], (T.sx2[32 * k:32 * k + 4, :], R("sx2")[1]))
+    cp(R("Y"), bank(4))
+    dma("y", "dy", T.y[:], R("Y"))
     g.wait_ge(T.sem.ls, sent[0])
     for sem in SEMAPHORES:
         if sem in last and not last[sem]["waited"]:

@@ -1,3 +1,4 @@
+import numpy as np
 from concourse.mybir import dt, AluOpType, ActivationFunctionType
 
 A = AluOpType
@@ -10,13 +11,37 @@ W16 = [4913.0, 289.0, 17.0, 1.0]
 W64 = [278920.0, 4290.0, 65.0]
 KB0 = [0, 64, 192]
 XB0 = [0, 0, 128]
-HB = [0, 192, 480]
+HB = [0, 192, 576]
 TW = 1296
+NV = 6
 NE = 3
+ENTER_V = [0]
+STEP = [(0, 4), (4, 8), (8, 12)]
+HOLD = [(0, 64), (64, 128), (128, 192)]
+ROW_V = [0]
+DIGIT_V = [0, 1]
+BLOCK_V = []
+LEAVE_V = [0]
+LAST = 1
+TWO = [0]
+FIRST = [(0, 4), (4, 8)]
+LEAF_V = [1]
+CHAIN_V = [0, 1]
+UNPACK_V = []
+EARLY = [4000, 600, 600]
+JOIN = 6.0
+COPY_V = [0, 1]
 OFF = [193 * k - 2 ** k + 1 for k in range(9)]
-LAG = [0.0, 0.5, 1.6, 2.7]
-PICK = [8.9, 9.65, 10.5, 11.5]
-PLUS = [10.6, 11.4, 11.6, 12.0]
+WL = [193.0 - 2.0 ** m for m in range(7)]
+WR = [193.0 - 2.0 ** (m + 1) for m in range(7)]
+WAKE, LEAST, GATHER, SCATTER, LOAD, REMOTE, ISSUE = 277, 64, 1.56, 3.8, 1100, 1050, 360
+SCALAR = [80, 33]
+PLAN = 1.05
+MACHINES = [(1 / 1.05, 0, 0), (1 / 1.05, 15, -10), (1.35 / 1.05, 0, 0)]
+WALKS, NOISE, PART, SWAPS, TABU, SPEEDS, STARTS = 901, 700, 0.025, 0, 20, (1.0,), []
+WAVE = [(0, 1), (1, 1), (2, 1), (0, 2), (3, 1), (1, 2), (0, 3), (2, 2), (1, 3), (0, 4), (3, 2), (2, 3), (1, 4), (0, 5), (3, 3),
+        (1, 5), (0, 6), (2, 4), (3, 4), (0, 7), (1, 6), (2, 5), (3, 5), (1, 7), (2, 6), (3, 6), (2, 7), (0, 8), (3, 7), (1, 8),
+        (0, 9), (2, 8), (3, 8), (1, 9), (2, 9), (3, 9)]
 X4, U8, U16, F32, B16 = "float8_e4m3fn_x4", "uint8", "uint16", "float32", "bfloat16"
 
 SCRATCH = {}
@@ -27,32 +52,166 @@ for _n, _w, _d in [
     ("ol0", 12, U16), ("ol1", 12, U16), ("lo0", 12, U16), ("lo1", 12, U16),
     ("Bt0", 768, B16), ("Bt1", 768, B16), ("qf0", C, X4), ("qf1", C, X4), ("sf0", C, U8), ("sf1", C, U8),
     ("ut", 512, B16), ("vt", 512, B16), ("qu", 128, X4), ("su", 128, U8), ("qv", 128, X4), ("sv", 128, U8),
-    ("qw", 512, X4), ("sw", 512, U8), ("Z", 528, B16), ("qe", 512, X4), ("se", 512, U8),
-    ("Tp", 768, B16), ("TB", 384, B16), ("RB", 384, B16), ("cf", 384, B16),
-    ("PT", 224, F32), ("PC", 224, F32), ("col", 16, F32), ("tmp", 64, F32), ("c16", 12, F32), ("c16f", 12, F32),
-    ("wm", 12, F32), ("wsh", 12, F32), ("wf", C, F32), ("IO", 288, F32), ("IOb", C, B16), ("MOD", 480, F32), ("ext", C, B16), ("ones", 256, B16),
-    ("m16", C, B16), ("m64", 256, B16), ("exa", 64, F32), ("RA", 128, F32), ("tie", C, F32), ("TE", 216, F32), ("D1", 16, F32),
-    ("TH", H, F32), ("RL", H, F32), ("RR", H, F32), ("FL", H, F32), ("SL", C, F32),
-    ("PA", 480, F32), ("PB", 480, F32), ("V0", 480, F32), ("VA", 480, F32), ("VB", 480, F32), ("VD", C, F32),
-    ("K16", C, F32), ("KS", C, F32), ("RAW", C, F32), ("RAW2", C, F32), ("RK", C, F32), ("RE", C, F32),
-    ("RX", 128, F32), ("RG", 128, F32), ("sm", 192, F32),
-    ("LS", 24, U16), ("LX", 24, U16), ("LR", 12, U16), ("LR2", 8, U16), ("LE", 12, U16), ("LY", 8, U16),
-    ("LP", 12, U16), ("LL", 24, U16), ("L15", 6, U16), ("L8", 6, U16),
-    ("CMP", 960, B16), ("CNT", 960, B16), ("C16", C, B16), ("N16", C, B16), ("N64", 512, B16),
-    ("JK", 1344, B16), ("AC", 48, F32),
-    ("U", C, F32), ("KB", 384, F32), ("XS", 320, F32), ("GE", 320, F32), ("UE", C, F32),
+    ("qh", 256, X4), ("sh", 256, U8), ("qw", 512, X4), ("sw", 512, U8), ("Z", 528, B16), ("qe", 512, X4), ("se", 512, U8),
+    ("Tp", 768, B16), ("TB", 384, B16), ("RB", 384, F32), ("cf", 384, F32),
+    ("PT", 224, F32), ("PC", 224, F32), ("col", 16, F32), ("tmp", 128, F32), ("c16", 12, F32), ("c16f", 12, F32),
+    ("e16", 288, B16), ("wm", 36, F32), ("wf", C, F32), ("IO", 384, F32), ("IOb", C, B16), ("MOD", 384, F32),
+    ("ext", C, B16), ("ones", 256, B16), ("m16", C, B16), ("m64", 256, B16),
+    ("TE", 216, F32), ("D1", 16, F32), ("TH", 7, F32), ("RL", 216, F32), ("FL", 108, F32), ("SL", 216, F32),
+    ("PA", 576, F32), ("PB", 576, F32), ("V0", 576, F32), ("VA", 576, F32), ("VB", 576, F32), ("VD", C, F32),
+    ("K16", C, F32), ("KS", C, F32), ("R4", C, F32), ("R16", C, F32), ("RP", C, F32), ("RK", 576, F32), ("RE", C, F32),
+    ("RA", 36, F32), ("RX", C, F32), ("RG", 128, F32), ("sm", 320, F32),
+    ("LS", 36, U16), ("LX", 24, U16), ("LR", 36, U16), ("LR2", 8, U16), ("LE", 12, U16), ("LY", 16, U16),
+    ("LP", 12, U16), ("LL", 24, U16), ("L15", 12, U16),
+    ("C16", 2 * C, B16), ("N16", 2 * C, B16), ("KE", C, F32), ("C64", 1280, B16), ("N64", 1280, B16), ("CMP", 14 * C, B16), ("CNT", 14 * H, B16),
+    ("JK", 7552, B16), ("AC", 64, F32),
+    ("U", C, F32), ("KB", 384, F32), ("XS", 320, F32), ("GE", 384, F32), ("UE", 128, F32),
+    ("tie", 128, F32), ("T1", 128, F32), ("T2", 64, F32), ("XZ", 64, F32),
     ("O", C, B16), ("RO", C, B16), ("PR", C, F32),
     ("TAB", 4 * TW, F32), ("G1", 768, F32), ("MX", 768, F32), ("Y", C, F32),
 ]:
     SCRATCH[_n] = ("sbuf", [128, _w], _d)
 SCRATCH["BT"] = ("sbuf", [128, 12, 32], B16)
 SCRATCH["cm"] = ("sbuf", [128, 12, 32], B16)
-SCRATCH["w16"] = ("sbuf", [128, 12, 16], F32)
 SCRATCH["ps"] = ("psum", [128, 4096], F32)
 
-POOL = {"v": 64, "s": 44, "t": 10, "g": 12}
-DMAS = ["dx", "du", "dv", "dwc", "dws", "dop", "doc", "ds0", "ds1", "ds2", "ds3", "dy"]
+POOL = {"v": 63, "s": 44, "t": 10, "g": 12}
+DMAS = ["dx", "du", "dv", "dwc", "dws", "dop", "doc", "dod", "ds0", "ds1", "ds2", "ds3", "dy", "dz"]
 SEMAPHORES = [e + str(i) for e in POOL for i in range(POOL[e])] + DMAS + ["ax0", "ax1", "al0", "al1", "ls"]
+
+
+def order_calls(calls):
+    def gap(early, late):
+        return 0 if late["behind"] is early else early["lat"] + (WAKE if late["e"] else 0)
+
+    def walk(ahead):
+        prev, nxt = ("prev", "next") if ahead else ("next", "prev")
+        free, ready, start, opn, at = {}, {}, {}, {}, {}
+        for c in calls:
+            opn[c["id"]], at[c["id"]] = len(c[prev]), 0 if ahead else c["lat"]
+            if not c[prev]:
+                ready.setdefault(c["e"], []).append(c)
+        while len(start) < len(calls):
+            best = None
+            for e, cs in ready.items():
+                if not cs:
+                    continue
+                now = free.get(e, 0) if e else 0
+                top = max(cs, key=lambda c: c["chain"])
+
+                def merit(c):
+                    st = max(now, at[c["id"]])
+                    late = st + c["chain"]
+                    if c is not top:
+                        late = max(late, max(st + c["len"], at[top["id"]]) + top["chain"])
+                    return (late, st, -c["chain"])
+                c = min(cs, key=merit) if e else min(cs, key=lambda c: at[c["id"]])
+                st = max(now, at[c["id"]])
+                if best is None or st < best[0]:
+                    best = (st, c)
+            st, c = best
+            ready[c["e"]].remove(c)
+            start[c["id"]] = st
+            free[c["e"]] = st + c["len"]
+            for s in c[nxt]:
+                early, late = (c, s) if ahead else (s, c)
+                opn[s["id"]] -= 1
+                at[s["id"]] = max(at[s["id"]], st + c["len"] + gap(early, late))
+                if not opn[s["id"]]:
+                    ready.setdefault(s["e"], []).append(s)
+        return start
+
+    for c in reversed(calls):
+        c["chain"] = c["len"] + max([gap(c, s) + s["chain"] for s in c["next"]], default=c["lat"])
+
+    def length(order, slow, scalar, wake):
+        free, end = {}, {}
+        for c in order:
+            at = max([end[p["id"]] + (gap(p, c) and gap(p, c) + (wake if c["e"] else 0)) for p in c["prev"]], default=0)
+            at = max(at, free.get(c["e"], 0) if c["e"] else 0)
+            end[c["id"]] = free[c["e"]] = at + slow * c["len"] + (scalar if c["e"] == "s" else 0)
+        return max(end[c["id"]] + c["lat"] for c in calls) / slow ** 0.6
+
+    best, rng = None, np.random.default_rng(1)
+    for k in range(WALKS):
+        start = walk(k % 2 == 0)
+        if k % 2 == 0:
+            order = sorted(calls, key=lambda c: (start[c["id"]], c["id"]))
+            end = sum(length(order, *m) for m in MACHINES)
+            if best is None or end <= best[0]:
+                best = (end, start)
+            start = best[1]
+        lead = (NOISE * rng.random(len(calls)) * (rng.random(len(calls)) < PART)).tolist()
+        for c in calls:
+            c["chain"] = start[c["id"]] + c["len"] + lead[c["twin"]]
+    return [best[1][c["id"]] for c in calls]
+    n = len(calls)
+    queues = {}
+    for c in sorted(calls, key=lambda c: (best[1][c["id"]], c["id"])):
+        if c["e"]:
+            queues.setdefault(c["e"], []).append(c["id"])
+    succ = [[(s["id"], gap(c, s)) for s in c["next"]] for c in calls]
+    lens = [[c["len"] * f for c in calls] for f in SPEEDS]
+    base = [len(c["prev"]) for c in calls]
+
+    def times(ln):
+        after, opn, at, why = [-1] * n, list(base), [0] * n, [-1] * n
+        for q in queues.values():
+            for a, b in zip(q, q[1:]):
+                after[a] = b
+                opn[b] += 1
+        todo, seen = [i for i in range(n) if not opn[i]], []
+        while todo:
+            i = todo.pop()
+            seen.append(i)
+            e = at[i] + ln[i]
+            for j, d in succ[i] + ([(after[i], 0)] if after[i] >= 0 else []):
+                if e + d > at[j]:
+                    at[j], why[j] = e + d, i
+                opn[j] -= 1
+                if not opn[j]:
+                    todo.append(j)
+        tail, own = [0] * n, [0] * n
+        for i in reversed(seen):
+            own[i] = max([d + ln[j] + tail[j] for j, d in succ[i]], default=lats[i])
+            tail[i] = own[i] if after[i] < 0 else max(own[i], ln[after[i]] + tail[after[i]])
+        end = max((at[i] + ln[i] + lats[i], i) for i in range(n))
+        return end[0], end[1], at, why, after, tail, own
+
+    def swapped(r, ln, i, j, h):
+        at, after, tail, own = r[2], r[4], r[5], r[6]
+        first = max([at[p] + ln[p] + d for p, d in pred[j]] + [at[h] + ln[h] if h >= 0 else 0])
+        second = max([at[p] + ln[p] + d for p, d in pred[i]] + [first + ln[j]])
+        ti = own[i] if after[j] < 0 else max(own[i], ln[after[j]] + tail[after[j]])
+        tj = max(own[j], ln[i] + ti)
+        new, old = max(first + ln[j] + tj, second + ln[i] + ti), max(at[x] + ln[x] + tail[x] for x in (i, j))
+        return new if old >= r[0] - 1 else max(new, r[0])
+
+    lats = [c["lat"] for c in calls]
+    pred = [[(p["id"], gap(p, c)) for p in c["prev"]] for c in calls]
+    top, kept, tabu = None, None, {}
+    for k in range(SWAPS + 1):
+        rs = [times(ln) for ln in lens]
+        now = sum(r[0] / f for r, f in zip(rs, SPEEDS))
+        if top is None or now < top:
+            top, kept = now, rs[0][2]
+        tried = []
+        for r in rs:
+            j = r[1]
+            while r[3][j] >= 0:
+                i = r[3][j]
+                if r[4][i] == j and all(s != j for s, _ in succ[i]) and tabu.get((i, j), -1) < k:
+                    q = queues[calls[i]["e"]]
+                    p = q.index(i)
+                    tried.append((sum(swapped(x, ln, i, j, q[p - 1] if p else -1) / f for x, ln, f in zip(rs, lens, SPEEDS)), i, j, p))
+                j = i
+        if not tried:
+            break
+        _, i, j, p = min(tried)
+        q = queues[calls[i]["e"]]
+        q[p], q[p + 1] = j, i
+        tabu[(j, i)] = k + TABU
+    return kept
 
 
 def rank_program(g, core, T, topo):
@@ -60,27 +219,26 @@ def rank_program(g, core, T, topo):
     if rank is None:
         return
     Q = {"v": g.vector, "s": g.scalar, "t": g.tensor, "g": g, "y": g.sync}
-    known = {e: set() for e in Q}
-    cur = {e: None for e in Q}
-    nxt = {e: 0 for e in Q}
-    joined = [False]
-    last = {}
-    batches = []
-    hist = {}
+    calls, hist, back, began = [], {}, [0], []
 
     def R(n, a=0, b=None, s=1):
         b = SCRATCH[n][1][1] if b is None else b
-        return (T[n][:, a:b:s] if s != 1 else T[n][:, a:b], [(n, frozenset(range(a, b, s)))])
+        cols = frozenset(range(a, b, s))
+        return (T[n][:, a:b:s] if s != 1 else T[n][:, a:b], [(n, cols)], len(cols), SCRATCH[n][2] in (B16, U16), "sbuf")
 
-    def R3(n, a, b, c, d):
+    def R3(n, a, b, c, d, s=1):
         w = SCRATCH[n][1][2]
-        return (T[n][:, a:b, c:d], [(n, frozenset(i * w + j for i in range(a, b) for j in range(c, d)))])
+        cols = frozenset(i * w + j for i in range(a, b, s) for j in range(c, d))
+        return (T[n][:, a:b:s, c:d] if s != 1 else T[n][:, a:b, c:d], [(n, cols)], len(cols), SCRATCH[n][2] == B16, "sbuf")
 
     def bank(b, lo=0, hi=C):
-        return (T.ps[:, 512 * b + lo:512 * b + hi], [("ps", frozenset([b]))])
+        return (T.ps[:, 512 * b + lo:512 * b + hi], [("ps", frozenset([b]))], hi - lo, False, "psum")
 
     def ind(win, off):
-        return (win[0].indirect(off[0]), win[1] + off[1])
+        return (win[0].indirect(off[0]), win[1] + off[1], 16 * off[2], False, "list")
+
+    def u8(x):
+        return (x[0].bitcast(dt.uint8),) + x[1:]
 
     def ap(x):
         return x[0] if isinstance(x, tuple) else x
@@ -88,11 +246,420 @@ def rank_program(g, core, T, topo):
     def regs(*xs):
         return [r for x in xs if isinstance(x, tuple) for r in x[1]]
 
+    def op(e, fn, reads, writes, length, lat=0, sem=None, count=1, after=()):
+        c = {"id": len(calls), "e": e, "fn": fn, "len": PLAN * length, "lat": lat, "sem": sem, "count": count, "next": [],
+             "behind": None, "twin": len(calls) - back[0]}
+        prev = {p["id"]: p for p in after}
+        for w, rs in ((False, reads), (True, writes)):
+            for n, cols in rs:
+                for (c2, w2, p) in hist.get(n, []):
+                    if (w or w2 or (n == "ps" and p["e"] != e)) and not cols.isdisjoint(c2):
+                        prev[p["id"]] = p
+        c["prev"] = list(prev.values())
+        for p in c["prev"]:
+            p["next"].append(c)
+        for w, rs in ((False, reads), (True, writes)):
+            for n, cols in rs:
+                h = hist.setdefault(n, [])
+                if w:
+                    h[:] = [x for x in h if not x[0] <= cols]
+                h.append((cols, w, c))
+        calls.append(c)
+        return c
+
+    def follow(p):
+        c = calls[-1]
+        if p is not None and all(p is not x for x in c["prev"]):
+            c["prev"].append(p)
+            p["next"].append(c)
+            c["behind"] = p
+        return c
+
+    def cycles(fixed, src, *sides):
+        if src[4] == "list":
+            return fixed + GATHER * src[2]
+        return max(LEAST, src[2] / (2 if all(x[3] for x in (src,) + sides) else 1))
+
+    def dma(e, sem, out, in_, size, also=()):
+        op(e, lambda: Q[e].dma_start(ap(out), ap(in_)), regs(in_, *also), regs(out), 100, LOAD + size / 150, sem, 16)
+
+    def ts(out, in0, s1, o0, s2=None, o1=None):
+        if o1 is None:
+            fn = lambda: g.vector.tensor_scalar(out[0], in0[0], ap(s1), None, o0)
+        else:
+            fn = lambda: g.vector.tensor_scalar(out[0], in0[0], ap(s1), ap(s2), o0, o1)
+        op("v", fn, regs(in0, s1, s2), out[1], cycles(60, in0, out))
+
+    def tt(out, in0, in1, o):
+        n = cycles(60, in0) if in0[4] == "list" else max(LEAST, in0[2] * (1 if "psum" in (in0[4], in1[4]) else 2))
+        op("v", lambda: g.vector.tensor_tensor(out[0], in0[0], in1[0], o), regs(in0, in1), out[1], n)
+
+    def scan(out, d0, d1, o0=A.mult, o1=A.add, init=0.0):
+        op("v", lambda: g.vector.tensor_tensor_scan(out[0], d0[0], d1[0], init, o0, o1), regs(d0, d1), out[1],
+           cycles(0, d0, d1, out))
+
+    def cp(out, in_):
+        op("v", lambda: g.vector.tensor_copy(out[0], in_[0]), in_[1], out[1], cycles(60, in_, out))
+
+    def turn(out, in_):
+        op("v", lambda: g.vector.transpose(out[0], in_[0]), in_[1], out[1], cycles(0, in_, out))
+
+    def ms(out, c):
+        op("v", lambda: g.vector.memset(out[0], c), [], out[1], cycles(0, out))
+
+    def act(out, in_, scale=None, bias=None, func=None, acc=None):
+        kw = {}
+        if scale is not None:
+            kw["scale"] = ap(scale)
+        if bias is not None:
+            kw["bias"] = ap(bias)
+        if acc is not None:
+            kw["accum_out"] = acc[0]
+        fu = func if func is not None else (F.Identity if bias is not None else F.Copy)
+        n = (80 + GATHER * in_[2] if in_[4] == "list" else max(SCALAR[0], in_[2] + SCALAR[1])) + (24 if acc else 0)
+        op("s", lambda: g.scalar.activation(out[0], in_[0], fu, **kw), regs(in_, scale, bias), regs(out, acc), n)
+
+    def quant(q, s, x, early=0):
+        op("v", lambda: g.vector.quantize_mx(q[0], s[0], x[0]), x[1], regs(q, s), 15 + 0.265 * x[2], early)
+
+    def mm(b, lq, ls, rq, rs):
+        op("t", lambda: g.tensor.matmul_mx(bank(b, 0, rq[2])[0], lq[0], ls[0], rq[0], rs[0], True, True),
+           regs(lq, ls, rq, rs), bank(b)[1], 0.72 * (rq[2] + 16))
+
+    def iota(out, pattern, base):
+        op("g", lambda: g.iota(out[0], pattern, base, 0, allow_small_or_imprecise_dtypes=True), [], out[1], 160 + 2 * out[2])
+
+    def select(out, pattern, compare, step, after=()):
+        op("g", lambda: g.affine_select(out[0], T.ones[:, 0:out[2]], pattern, compare, 0.0, 0, step), R("ones")[1], out[1],
+           200 + 2 * out[2], after=after)
+
+    sent = [0]
+
+    def exchange(peer, sem, pairs):
+        rid, pid, _ = topo.addr(peer)
+        sends = []
+        for dst, src, size in pairs:
+            fn = lambda dst=dst, src=src: g.remote_dma(dst[0], src[0], T.sem[sem], T.sem.ls, pid, rid, topo.mask(core, peer))
+            sends.append(op("g", fn, src[1], [], ISSUE if sent[0] else 18 * ISSUE, REMOTE + (size / 150 + EARLY[1] if size else 0), "", 0))
+            sent[0] += len(topo.engines(core, peer))
+        op(None, None, [], regs(*[p[0] for p in pairs]), 0, 0, sem, len(pairs) * len(topo.engines(peer, core)), sends)
+
+    def fill(out, c):
+        act(out, R("ones", 0, out[2]), scale=c)
+
+    cw, cthr, cq, ch, cM, cim, cown = [R("PC", 32 * i, 32 * i + 1) for i in range(7)]
+    cj, cjq, cA, cB, c16B, cih, cnM, cnMe, cE, cq1, c8, cS = [R("col", i, i + 1) for i in range(12)]
+    sm = lambda k, a=0, b=12: R("sm", 16 * k + a, 16 * k + b)
+    blocks = lambda n: [R(n, 128 * b, 128 * b + 128) for b in range(4)]
+
+    dma("y", "dx", R("X0"), T.x[:], 128 * 1536)
+    dma("s", "du", R("ut"), T.u[:], 128 * 1024)
+    quant(R("qu"), R("su"), R("ut"))
+    dma("y", "dwc", u8(R("qw")), T.wc[:], 128 * 2048, [R("X0"), R("ut")])
+    dma("y", "dws", R("sw"), T.ws[:], 128 * 512, [R("X0"), R("ut")])
+    dma("y", "dv", R("vt"), T.v[:], 128 * 1024, [R("X0"), R("ut")])
+    quant(R("qv"), R("sv"), R("vt"))
+
+    ms(R("ones"), 1.0)
+    ms(R("Z"), 0.0)
+    iota(R("PT", 64, 96), [[0, 2], [1, 16]], 0)
+    iota(R("PT", 96, 128), [[1, 2], [0, 16]], 0)
+    iota(R("c16"), [[16, 12]], 0)
+    iota(R("IO", 0, C), [[1, C]], 0)
+    act(R("IO", C, 384), R("IO", 0, C), bias=float(C))
+    for a, b, c in ((0, 32, 0.0), (32, 64, -1e29), (128, 160, BIG), (160, 192, 1.0 / BIG)):
+        ms(R("PT", a, b), c)
+    for a, b, s, c in ((0, 8, 1, 1.0), (16, 24, 1, 1.0), (24, 25, 1, -0.498046875), (25, 29, 3, MAGIC), (26, 30, 3, -MAGIC),
+                       (27, 28, 1, 1.25), (32, 40, 1, 0.0), (48, 56, 1, 0.0), (143, 192, 16, 1.0)):
+        fill(R("PT", a, b, s), c)
+    ms(R("tmp", 0, 16), 0.5)
+    for k in range(2):
+        scan(R("PT", 192 + 16 * k, 208 + 16 * k), R("tmp", 0, 16), R("Z", 0, 16), init=65536.0)
+    turn(R("PC"), R("PT"))
+    select(R("Z", 3, 515, 4), [[-1, 128]], A.is_equal, 1)
+    for b in range(4):
+        quant(blocks("qe")[b], blocks("se")[b], R("Z", 3 - b, 515 - b), EARLY[0])
+    act(cj, ch, scale=0.5, bias=0.5 / BIG)
+    act(cA, ch, scale=0.5, bias=0.5)
+    act(cB, ch, scale=-0.5, bias=1.0)
+    act(c16B, ch, scale=-BIG, bias=BIG)
+    act(cjq, cq, scale=cj)
+    act(cih, cim, scale=0.5)
+    cmc = lambda a, b, lo=0, hi=12: R3("cm", lo, hi, a, b)
+    ms(cmc(0, 32), 1.0)
+    for a, b, c in ((0, 1, ch), (1, 8, cA), (16, 17, c16B), (17, 24, cB)):
+        fill(cmc(a, b), c)
+    act(cmc(24, 25), R("c16"), scale=cj, bias=cjq)
+    for h in range(2):
+        act(R("cf", C * h, C * h + C), R3("cm", 6 * h, 6 * h + 6, 0, 32))
+    iota(R("c16f"), [[32, 12]], -1)
+    op("v", lambda: g.vector.reciprocal(sm(1)[0], T.c16f[:]), R("c16f")[1], sm(1)[1], 300)
+    act(R("cf", 59, 384, 32), sm(1, 1, 12), scale=-1.5, bias=2.0)
+    fill(R("cf", 27, 28), 8.0)
+    ts(R("cf", 28, 29), cq, 0.0, A.is_equal, 0.25, A.max)
+    ts(cq1, cq, 1.0, A.add)
+    iota(R("e16", 0, H), [[0, 6], [1, 16]], 0)
+    ts(R("e16", H, C), R("e16", 0, H), cq, A.not_equal)
+    ts(R("e16", C, 288), R("e16", 0, H), cq1, A.is_equal, BIG, A.mult)
+    tt(R("ext", 0, H), R("e16", H, C), R("e16", C, 288), A.add)
+    act(R("ext", H, C), R("ext", 0, H))
+    act(cnM, cM, scale=-1.0)
+    act(cnMe, cM, scale=-(1.0 + 2.0 ** -22))
+    ts(cE, cown, -0.5, A.add, cM, A.mult)
+    for k in range(3):
+        act(R("V0", 64 * k, 64 * k + 64, 2), R("PT", 192, 224))
+    act(R("V0", 384, 576, 2), R("V0", 0, C, 2))
+    for a, b, s, i in ((1, C, 2, 1), (C, 384, 1, 0), (385, 576, 2, 193)):
+        fill(R("V0", a, b, s), 0.0)
+        ms(R("VA", a, b, s), 0.0)
+        ms(R("VB", a, b, s), 0.0)
+        act(R("PA", a, b, s), R("IO", i, i + b - a, s))
+        iota(R("PB", a, b, s), [[s, len(range(a, b, s))]], i)
+    iota(R("KB", 64, 128), [[0, 64]], 0)
+    iota(R("KB", C, 320), [[0, 128]], 0)
+    iota(R("XS", 0, 64), [[1, 64]], 0)
+    iota(R("XS", 128, 256), [[1, 128]], 0)
+    iota(R("MOD"), [[1, C], [0, 2]], 0)
+    select(R("m16"), [[0, 12], [1, 16]], A.not_equal, 0)
+    select(R("m64"), [[0, 4], [1, 64]], A.not_equal, 0)
+    iota(R("D1"), [[1, 16]], 1)
+    iota(R("UE", 0, 64), [[0, 64]], 0)
+    iota(R("tie"), [[0, 2], [-1, 64]], -33)
+    act(R("IOb"), R("IO", 0, C))
+    for c in range(4):
+        iota(R("wf", 16 * c, 16 * c + 16), [[0, 16]], int(W16[c]))
+    for s in (1, 2):
+        act(R("wf", 64 * s, 64 * s + 64), R("wf", 0, 64))
+    iota(R("wm"), [[0, 12], [1, 3]], 0)
+    ts(R("wm", 2, 36, 3), R("wf", 0, C, 16), cM, A.mult, 0.5, A.mult)
+    act(R("TE", 0, 72), R("IO", 0, 72), scale=W64[0], bias=-32.0 * W64[0])
+    for s in (1, 2):
+        iota(R("TE", 72 * s, 72 * s + 72), [[int(W64[s]), 72]], int(W64[s]))
+    ts(R("L15"), R("c16"), 15.25, A.add)
+    for m in range(7):
+        fill(R("TH", m, m + 1), 0.5 - 2.0 ** (m + 1))
+    for k, w in enumerate((WL + [2.0, 2.0], WR + [2.0, 2.0])):
+        for m in range(9):
+            fill(R("RL", 108 * k + m, 108 * k + 108, 9), w[m - 1] / w[m] if m else 0.0)
+
+    def unwrap(out, row):
+        scan(out, R("ext", 0, row[2]), row)
+
+    def signs(j0, cols, row, thr, scale, a0, to="AC", step=1):
+        for i, c in enumerate(cols):
+            n, a = row(c)[2], a0 + step * c
+            act(R("JK", j0 + n * i, j0 + n * i + n), row(c), scale=scale, bias=thr(c), func=F.Sign, acc=R(to, a, a + 1))
+
+    hw = lambda n, h: R(n, HB[h], HB[h + 1])
+    hl = lambda n, h: R(n, HB[h] + C * h, HB[h + 1], 2)
+    half = lambda n, h, w=H, o=0: R(n, o + w * h, o + w * h + w)
+
+    def scores(x, q, s):
+        for h in range(2):
+            quant(half("qh", h, 128), half("sh", h, 128), R(x, 256 * h, 256 * h + 512))
+            mm(4 + h, R(q), R(s), half("qh", h, 128), half("sh", h, 128))
+
+    for t in range(2):
+        began.append(len(calls))
+        back[0] = began[t] - began[0]
+        peer = T.cores[rank ^ (1 << t)]
+        X, qx, sx = R("X%d" % t), R("qx%d" % t), R("sx%d" % t)
+        lq, lp, ol, lo, qf, sf = [R("%s%d" % (n, t)) for n in ("lq", "lp", "ol", "lo", "qf", "sf")]
+        Bt, Xn = "Bt%d" % t, "X%d" % (t + 1)
+        scores("X%d" % t, "qu", "su")
+        quant(qx, sx, X)
+        exchange(peer, "ax%d" % t, [(u8(lq), u8(qx), 128 * 768), (lp, sx, 128 * C)])
+        for h in range(2):
+            for k in range(2):
+                ts(R3("BT", 6 * h, 6 * h + 6, 16 * k, 16 * k + 16), bank(4 + h, 32 * h, 32 * h + H), cthr, A.is_gt, cw, A.mult)
+            turn(half("TB", h, C), R3("BT", 6 * h, 6 * h + 6, 0, 32))
+            scan(half("RB", h, C), half("cf", h, C), half("TB", h, C))
+            cp(half("LS", h, 6), R("RB", C * h + 29, C * h + C, 32))
+        for b in range(4):
+            mm(4 + b, blocks("qe")[b], blocks("se")[b], lq, lp)
+            (cp if b in UNPACK_V else act)(R("Tp", C * b, C * b + C), bank(4 + b))
+            calls[-1]["lat"] = EARLY[2]
+            mm(b, blocks("qe")[b], blocks("se")[b], qx, sx)
+        for h in range(2):
+            L1, L4 = half("LS", h, 6), half("LS", h, 6, 12)
+            (cp if h in ROW_V else act)(hl("PA", h), ind(R("IO", 0, HB[h + 1] - HB[h]), L1))
+            for p0, p1, v0, v1 in (("PA", "PB", "V0", "VA"), ("PB", "PA", "VA", "VB"), ("PA", "PB", "VB", "VA")):
+                act(hl(p1, h), ind(hw(p0, h), L1))
+                tt(hl(v1, h), ind(hw(v0, h), L1), hl("V0", 1 - h), A.add)
+            (cp if h in CHAIN_V else act)(half("VD", h), hl("VA", h))
+            unwrap(half("R4", h), hl("PB", h))
+            ts(L4, R("R4", H * h + 15, H * h + H, 16), cim, A.mult, 0.25, A.add)
+            for p0, p1, v0, v1 in (("PB", "PA", "VA", "VB"), ("PA", "PB", "VB", "VA"), ("PB", "PA", "VA", "K16")):
+                act(hl(p1, h), ind(hw(p0, h), L4))
+                tt(half(v1, h) if v1 == "K16" else hl(v1, h), ind(hw(v0, h), L4), half("VD", h), A.add)
+            act(half("KS", h), half("K16", h), scale=cM)
+            unwrap(half("R16", h), half("K16", h))
+            tt(half("C16", h), ind(half("R16", h), R("L15", 0, 6)), half("KS", h), A.is_gt)
+            scan(half("N16", h), R("m16", 0, H), half("C16", h))
+            cp(half("LR", h, 6), R("N16", H * h + 15, H * h + H, 16))
+            for a, b in ((0, 4), (4, 6)) if h == 0 else ((6, 8), (8, 12)):
+                o0 = KB0[a // 4] + 16 * a
+                tt(R("KB", o0, o0 + 16 * (b - a)), ind(R("D1"), R("LR", a, b)), R("wf", 16 * a, 16 * b), A.mult)
+            unwrap(half("RP", h), hl("PA", h))
+        ts(R("LX", 0, 24, 2), R("RP", 15, C, 16), cih, A.mult, -0.25, A.add)
+        for h in range(2):
+            if h in BLOCK_V:
+                ts(sm(2, 6 * h, 6 * h + 6), R("R16", H * h + 15, H * h + H, 16), cE, A.add)
+            else:
+                act(sm(2, 6 * h, 6 * h + 6), R("R16", H * h + 15, H * h + H, 16), bias=cE)
+            signs(H * h, range(6 * h, 6 * h + 6), lambda c: R("K16", 16 * c, 16 * c + 16), lambda c: sm(2, c, c + 1), cnM,
+                  29, "RK", 48)
+        for c in range(12):
+            s, lx = c // 4, R("LX", 2 * c, 2 * c + 1)
+            o0 = KB0[s] + 16 * c
+            if c % 4:
+                tt(R("KB", o0, o0 + 16), ind(R("KB", KB0[s], o0), lx), R("KB", o0, o0 + 16), A.add)
+            if s:
+                o0, p0 = XB0[s] + 16 * c, HB[c // 6] + 32 * c
+                if c % 4:
+                    act(R("XS", o0, o0 + 16), ind(R("XS", XB0[s], o0), lx))
+                else:
+                    act(R("XS", o0, o0 + 16), R("PA", p0, p0 + 32, 2), scale=0.5, bias=-0.5)
+        for s in (1, 2):
+            unwrap(R("RX", 64 * s - 64, 64 * s), R("XS", XB0[s] + 64 * s, XB0[s] + 64 * s + 64))
+        ts(R("LY", 8, 16), R("RX", 15, 128, 16), cim, A.mult, 0.25, A.add)
+        act(R("XZ"), ind(R("XS", 0, 128), R("LY", 12, 16)))
+        unwrap(R("RX", 128, C), R("XZ"))
+        ts(R("LY", 4, 8), R("RX", 143, C, 16), cim, A.mult, 0.25, A.add)
+        live = lambda s: R("KB", KB0[s] + 64 * s, KB0[s] + 64 * s + 64)
+        act(R("RK", 13, 576, 48), R("N16", 15, C, 16), scale=-2.0, bias=16.0)
+        for s in range(3):
+            unwrap(R("RK", C * s, C * s + C, 3), live(s))
+        held = lambda c: R("RK", 48 * c + 45, 48 * c + 46)
+        for s in range(3):
+            if s in LEAF_V:
+                for c in range(4 * s, 4 * s + 4):
+                    ts(R("C64", 768 + 64 * c, 832 + 64 * c), live(s), cM, A.mult, held(c), A.is_lt)
+                scan(half("N64", 3 + s, 256), R("m64"), half("C64", 3 + s, 256))
+                cp(R("LR2", 4 * s, 4 * s + 4), R("N64", 256 * s + 831, 256 * s + 1024, 64))
+            else:
+                signs(192 + 256 * s, range(4 * s, 4 * s + 4), lambda c: live(s), held, cnMe, 12)
+                if s < 2:
+                    ts(R("LR2", 4 * s, 4 * s + 4), R("AC", 12 + 4 * s, 16 + 4 * s), 0.5, A.mult, 32.25, A.add)
+        for a, b in STEP:
+            scan(R("RA", 3 * a, 3 * b), R("wm", 3 * a, 3 * b), R("RK", 48 * a + 13, 48 * b, 16))
+        thr = lambda c: R("RA", 3 * c + 2, 3 * c + 3)
+        for s in range(3):
+            cols = range(4 * s, 4 * s + 4)
+            if s in ENTER_V:
+                for c in cols:
+                    ts(R("C64", 64 * c, 64 * c + 64), live(s), cM, A.mult, thr(c), A.is_lt)
+                scan(half("N64", s, 256), R("m64"), half("C64", s, 256))
+                cp(R("LE", 4 * s, 4 * s + 4), R("N64", 256 * s + 63, 256 * s + 256, 64))
+            else:
+                signs(3520 + 256 * s, cols, lambda c: live(s), thr, cnMe, 48)
+                ts(R("LE", 4 * s, 4 * s + 4), R("AC", 48 + 4 * s, 52 + 4 * s), 0.5, A.mult, 32.25, A.add)
+        for s, out, c in ((0, R("GE", 0, 64), -32.0), (1, R("UE", 64, 128), 1.0)):
+            src = ind(R("IO", 0, 72), R("LR2", 4 * s, 4 * s + 4))
+            if s in LEAVE_V:
+                ts(out, src, c, A.add, W64[s], A.mult)
+            else:
+                act(out, src, scale=W64[s], bias=c * W64[s])
+        digit = lambda s: ind(R("TE", 72 * s, 72 * s + 72), R("LE", 4 * s, 4 * s + 4))
+        tie = R("tie", 0, 64)
+        for a, b in FIRST:
+            tt(R("T1", 16 * a, 16 * b), ind(R("GE", 0, 64), R("LY", 4 + a, 4 + b)), R("tie", 16 * a, 16 * b), A.add)
+        tt(R("GE", C, 256), digit(1), R("T1", 64, 128), A.add)
+        both = [digit(2), ind(R("UE"), R("LY", 12, 16))]
+        tt(R("T2"), both[LAST], R("T1", 0, 64), A.add)
+        tt(R("GE", 256, 320), both[1 - LAST], R("T2"), A.add)
+        tt(R("GE", 320, 384), digit(0), tie, A.add)
+        tt(R("GE", 64, 128), ind(R("GE", 0, 64), R("LY", 8, 12)), R("UE", 64, 128), A.add)
+        for a, b in HOLD:
+            unwrap(R("RE", a, b), R("GE", C + a, C + b))
+        unwrap(R("RG"), R("GE", 0, 128))
+        E = R("GE", C, 384)
+        ent = lambda c: R("RE", 16 * ((c - 4) % 12) + 15, 16 * ((c - 4) % 12) + 16)
+        lea = lambda c: R("RG", 16 * c + 15, 16 * c + 16)
+
+        def above(k, thr):
+            ts(R("CMP", C * k, C * k + C), E, cM, A.mult, thr, A.is_gt)
+            scan(half("CNT", k), half("CMP", 2 * k), half("CMP", 2 * k + 1), A.add, A.add)
+
+        for c in range(NV):
+            above(c, ent(12 - NV + c))
+        signs(5824, range(12 - NV), lambda c: E, ent, cnM, 28)
+        cp(R("LP", 12 - NV, 12), R("CNT", H - 1, NV * H, H))
+        ts(R("LP", 0, 12 - NV), R("AC", 28, 40 - NV), -0.5, A.mult, 95.75, A.add)
+        op("v", lambda: g.vector.tensor_copy(T.O[:].indirect(T.LP[:]), T.IOb[:]), regs(R("IOb"), R("LP")), R("O")[1],
+           60 + SCATTER * C)
+        unwrap(R("RO"), R("O"))
+        ts(ol, R("RO", 15, C, 16), cim, A.mult, 0.25, A.add)
+        exchange(peer, "al%d" % t, [(lo, ol, 0)])
+        place, size = lambda a, b: R("FL", 9 * a + 7, 9 * b, 9), lambda a, b: R("FL", 9 * a + 8, 9 * b, 9)
+        cp(place(0, 12), R("LP"))
+        for c in range(NE):
+            above(6 + c, lea(c))
+        signs(4288, range(NE, 8), lambda c: E, lea, cnM, 40)
+        act(sm(9, NE, 8), R("AC", 40 + NE, 48), scale=-0.5, bias=96.0)
+        if NE:
+            tt(size(0, NE), R("CNT", 7 * H - 1, (6 + NE) * H, H), place(0, NE), A.subtract)
+        tt(size(NE, 8), sm(9, NE, 8), place(NE, 8), A.subtract)
+        if 2 in ENTER_V:
+            act(sm(13, 0, 4), R("AC", 20, 24), scale=-0.5, bias=-32.0)
+            tt(size(8, 12), sm(13, 0, 4), R("N64", 575, 768, 64), A.add)
+        else:
+            for c in range(8, 12):
+                act(sm(13, c, c + 1), R("AC", 12 + c, 13 + c), scale=-0.5)
+                act(size(c, c + 1), R("AC", 48 + c, 49 + c), scale=0.5, bias=sm(13, c, c + 1))
+        for c in range(12):
+            act(R("FL", 9 * c, 9 * c + 7), R("TH"), bias=size(c, c + 1), func=F.Sign)
+        for k, w in enumerate((WL, WR)):
+            scan(half("SL", k, 108), half("RL", k, 108), R("FL"))
+            ts(half("LL", k, 12), R("SL", 109 * k + 7, 108 * k + 108, 9), 0.5 * sum(w) + 0.25 - k, A.add)
+        for b in range(4):
+            (act if b > 1 else cp)(R(Bt, b, 768, 4), ind(R("Tp", C * b, C * b + C), lo))
+        quant(qf, sf, R(Bt))
+        for b in range(4):
+            mm(4 + b, blocks("qw")[b], blocks("sw")[b], qf, sf)
+            if b not in COPY_V:
+                act(R("TAB", TW * b, TW * b + C), bank(4 + b), scale=0.03125)
+            else:
+                ts(R("TAB", TW * b, TW * b + C), bank(4 + b), 0.03125, A.mult)
+        before = None
+        for b, k in WAVE:
+            win = R("TAB", TW * b, TW * b + OFF[8])
+            if k < 8:
+                n, h, a, o = 193 - 2 ** k, 2 ** (k - 1), TW * b + OFF[k - 1], TW * b + OFF[k]
+                scan(R("TAB", o, o + n), R("TAB", a, a + n), R("TAB", a + h, a + h + n), A.min, A.max, 1e29)
+            elif k == 8:
+                tt(R("MX", C * b, C * b + C), ind(win, R("LL", 12, 24)), R("G1", C * b, C * b + C), A.max)
+            else:
+                tt(R(Xn, b, 768, 4), R("MX", C * b, C * b + C), bank(b), A.add)
+            before = follow(before)
+            if k == 7:
+                act(R("G1", C * b, C * b + C), ind(win, R("LL", 0, 12)))
+
+    back[0] = 0
+    act(R("PR"), ind(R("MOD"), R("LS", 0, 12)))
+    dma("y", "dop", T.op[:], (T.PR[0:128:16, :], R("PR")[1]), 0)
+    scores("X2", "qv", "sv")
+    quant(R("qx2"), R("sx2"), R("X2"))
+    dma("y", "doc", T.oc[:, 0:512], u8(R("qh", 0, 128)), 128 * 512)
+    dma("s", "dod", T.oc[:, 512:768], u8(R("qh", C, 256)), 128 * 256)
+    for k, e in enumerate(("y", "s", "y", "s")):
+        dma(e, "ds%d" % k, T.osc[4 * k:4 * k + 4, :], (T.sx2[32 * k:32 * k + 4, :], R("sx2")[1]), 0)
+    act(R("Y", 0, 112), bank(4, 0, 112))
+    cp(R("Y", 112, C), bank(5, 48, 128))
+    dma("s", "dy", T.y[:, 0:112], R("Y", 0, 112), 128 * 448)
+    dma("y", "dz", T.y[:, 112:C], R("Y", 112, C), 128 * 320)
+
+    known = {e: set() for e in Q}
+    cur = {e: None for e in Q}
+    nxt = {e: 0 for e in Q}
+    last = {}
+    count = [0]
+
     def new_batch(e, sem, base):
-        b = {"id": len(batches), "e": e, "sem": sem, "n": base, "known": set(known[e]) if e else set(), "waited": False}
-        batches.append(b)
-        last[sem] = b
-        return b
+        count[0] += 1
+        last[sem] = {"id": count[0], "e": e, "sem": sem, "n": base, "known": set(known[e]) if e else set(), "waited": False,
+                     "calls": []}
+        return last[sem]
 
     def wait(e, b):
         if b["id"] in known[e]:
@@ -105,477 +672,41 @@ def rank_program(g, core, T, topo):
         known[e].update(b["known"])
         cur[e] = None
 
-    def depend(e, reads, writes):
-        deps = {}
-        for w, rs in ((False, reads), (True, writes)):
-            for n, cols in rs:
-                for (c2, w2, b) in hist.get(n, []):
-                    if (w or w2 or (n == "ps" and b["e"] != e)) and not cols.isdisjoint(c2):
-                        deps[b["id"]] = b
-        for i in sorted(deps, reverse=True):
-            wait(e, deps[i])
-
-    def note(b, reads, writes):
-        for w, rs in ((False, reads), (True, writes)):
-            for n, cols in rs:
-                h = hist.setdefault(n, [])
-                if w:
-                    h[:] = [x for x in h if not x[0] <= cols]
-                h.append((cols, w, b))
-
-    def op(e, fn, reads, writes):
-        depend(e, reads, writes)
-        if cur[e] is None:
-            sem = e + str(nxt[e] % POOL[e])
-            nxt[e] += 1
-            base = 0
-            if sem in last:
-                wait(e, last[sem])
-                base = last[sem]["n"]
-            cur[e] = new_batch(e, sem, base)
-        b = cur[e]
-        fn().then_inc(T.sem[b["sem"]], 1)
-        b["n"] += 1
-        note(b, reads, writes)
-        if not joined[0]:
-            cur[e] = None
-
-    def together(calls):
-        joined[0] = True
-        for c in calls:
-            c()
-        joined[0] = False
-        for e in cur:
-            cur[e] = None
-
-    def dma(e, sem, out, in_):
-        depend(e, regs(in_), regs(out))
-        Q[e].dma_start(ap(out), ap(in_)).then_inc(T.sem[sem], 16)
-        note(new_batch(e, sem, 16), regs(in_), regs(out))
-
-    def ts(out, in0, s1, o0, s2=None, o1=None):
-        if o1 is None:
-            op("v", lambda: g.vector.tensor_scalar(out[0], in0[0], ap(s1), None, o0), regs(in0, s1), out[1])
+    if not STARTS:
+        STARTS.extend(order_calls(calls))
+    for c in calls:
+        c["start"] = STARTS[c["id"]]
+        c["end"] = c["start"] + c["len"] + c["lat"]
+    for c in sorted(calls, key=lambda c: (c["start"], c["id"])):
+        e = c["e"]
+        if e is None:
+            c["batch"] = new_batch(None, c["sem"], c["count"])
+            continue
+        for b in sorted([p["batch"] for p in c["prev"] if p is not c["behind"]], key=lambda b: -b["id"]):
+            wait(e, b)
+        if c["sem"] == "":
+            c["fn"]()
+        elif c["sem"]:
+            c["fn"]().then_inc(T.sem[c["sem"]], c["count"])
+            c["batch"] = new_batch(e, c["sem"], c["count"])
         else:
-            op("v", lambda: g.vector.tensor_scalar(out[0], in0[0], ap(s1), ap(s2), o0, o1), regs(in0, s1, s2), out[1])
-
-    def tt(out, in0, in1, o):
-        op("v", lambda: g.vector.tensor_tensor(out[0], in0[0], in1[0], o), regs(in0, in1), out[1])
-
-    def scan(out, d0, d1, o0=A.mult, o1=A.add, init=0.0):
-        op("v", lambda: g.vector.tensor_tensor_scan(out[0], d0[0], d1[0], init, o0, o1), regs(d0, d1), out[1])
-
-    def cp(out, in_):
-        op("v", lambda: g.vector.tensor_copy(out[0], in_[0]), in_[1], out[1])
-
-    def ms(out, c):
-        op("v", lambda: g.vector.memset(out[0], c), [], out[1])
-
-    def act(out, in_, scale=None, bias=None, func=None, acc=None):
-        kw = {}
-        if scale is not None:
-            kw["scale"] = ap(scale)
-        if bias is not None:
-            kw["bias"] = ap(bias)
-        if acc is not None:
-            kw["accum_out"] = acc[0]
-        fu = func if func is not None else (F.Identity if bias is not None else F.Copy)
-        op("s", lambda: g.scalar.activation(out[0], in_[0], fu, **kw), regs(in_, scale, bias), regs(out, acc))
-
-    def quant(q, s, x):
-        op("v", lambda: g.vector.quantize_mx(q[0], s[0], x[0]), x[1], regs(q, s))
-
-    def mm(b, lq, ls, rq, rs):
-        op("t", lambda: g.tensor.matmul_mx(bank(b)[0], lq[0], ls[0], rq[0], rs[0], True, True), regs(lq, ls, rq, rs),
-           bank(b)[1])
-
-    def iota(out, pattern, base):
-        op("g", lambda: g.iota(out[0], pattern, base, 0, allow_small_or_imprecise_dtypes=True), [], out[1])
-
-    def mask(name, n, period):
-        op("g", lambda: g.affine_select(T[name][:], T.ones[:, 0:n], [[0, n // period], [1, period]], A.not_equal,
-                                        0.0, 0, 0), R("ones")[1], R(name)[1])
-
-    sent = [0]
-
-    def u8(x):
-        return (x[0].bitcast(dt.uint8), x[1])
-
-    def send(peer, dst, src, sem):
-        depend("g", src[1], [])
-        rid, pid, _ = topo.addr(peer)
-        g.remote_dma(dst[0], src[0], T.sem[sem], T.sem.ls, pid, rid, topo.mask(core, peer))
-        sent[0] += len(topo.engines(core, peer))
-
-    def arrival(peer, sem, calls, *lands):
-        note(new_batch(None, sem, calls * len(topo.engines(peer, core))), [], regs(*lands))
-
-    def fill(out, n, c):
-        act(out, R("ones", 0, n), scale=c)
-
-    cw, cthr, cq, ch, cM, cim, cown = [R("PC", 32 * i, 32 * i + 1) for i in range(7)]
-    cj, cjq, cA, cB, c16B, cH0, cnM, cnMe, cE, cq1, c8, cS = [R("col", i, i + 1) for i in range(12)]
-    sm = lambda k, a=0, b=12: R("sm", 16 * k + a, 16 * k + b)
-
-    dma("y", "dx", R("X0"), T.x[:])
-    dma("s", "du", R("ut"), T.u[:])
-    dma("y", "dwc", u8(R("qw")), T.wc[:])
-    dma("y", "dws", R("sw"), T.ws[:])
-    dma("y", "dv", R("vt"), T.v[:])
-
-    iota(R("PT", 64, 96), [[0, 2], [1, 16]], 0)
-    iota(R("PT", 96, 128), [[1, 2], [0, 16]], 0)
-    iota(R("c16"), [[16, 12]], 0)
-    iota(R("IO"), [[1, 288]], 0)
-    ms(R("ones"), 1.0)
-    together([lambda: ms(R("PT", 0, 32), 0.0), lambda: ms(R("PT", 32, 64), -1e29), lambda: ms(R("PT", 128, 160), BIG),
-              lambda: ms(R("PT", 160, 192), 1.0 / BIG), lambda: ms(R("tmp", 0, 16), 0.5), lambda: ms(R("Z"), 0.0)])
-    together([lambda: fill(R("PT", 0, 8), 8, 1.0), lambda: fill(R("PT", 16, 24), 8, 1.0),
-              lambda: fill(R("PT", 24, 25), 1, -0.498046875), lambda: fill(R("PT", 25, 29, 3), 2, MAGIC),
-              lambda: fill(R("PT", 26, 30, 3), 2, -MAGIC), lambda: fill(R("PT", 27, 28), 1, 1.25),
-              lambda: fill(R("PT", 32, 40), 8, 0.0), lambda: fill(R("PT", 48, 56), 8, 0.0),
-              lambda: fill(R("PT", 143, 192, 16), 4, 1.0)])
-
-    def zero_window(n):
-        together([lambda a=a, b=b: ms(R(n, a, b), 0.0) for a, b in ((H, C), (288, 480))])
-
-    zero_window("VA")
-    together([lambda k=k: scan(R("PT", 192 + 16 * k, 208 + 16 * k), R("tmp", 0, 16), R("Z", 0, 16), init=65536.0)
-              for k in range(2)])
-    ms(R3("cm", 0, 12, 0, 32), 1.0)
-    ts(R("c16f"), R("c16"), -0.5, A.add)
-    zero_window("VB")
-    op("v", lambda: g.vector.transpose(T.PC[:], T.PT[:]), R("PT")[1], R("PC")[1])
-    op("v", lambda: g.vector.reciprocal(sm(1)[0], T.c16f[:]), R("c16f")[1], sm(1)[1])
-    op("g", lambda: g.affine_select(T.Z[:, 3:515:4], T.ones[:, 0:128], [[-1, 128]], A.is_equal, 0.0, 0, 1),
-       R("ones")[1], R("Z")[1])
-    together([lambda: act(cj, ch, scale=0.5, bias=0.5 / BIG), lambda: act(cA, ch, scale=0.5, bias=0.5),
-              lambda: act(cB, ch, scale=-0.5, bias=1.0), lambda: act(c16B, ch, scale=-BIG, bias=BIG)])
-    together([lambda: ts(cH0, cq, 0.0, A.is_equal, float(H), A.mult), lambda: ts(cq1, cq, 1.0, A.add),
-              lambda: ts(R("tmp", 16, 32), R("IO", 0, 16), cq, A.not_equal)])
-    act(cjq, cq, scale=cj)
-    cmc = lambda a, b, lo=0, hi=12: R3("cm", lo, hi, a, b)
-    together([lambda: act(cmc(0, 1), R("ones", 0, 12), scale=ch), lambda: act(cmc(1, 8), R("ones", 0, 84), scale=cA),
-              lambda: act(cmc(16, 17), R("ones", 0, 12), scale=c16B), lambda: act(cmc(17, 24), R("ones", 0, 84), scale=cB),
-              lambda: act(cmc(24, 25), R("c16"), scale=cj, bias=cjq), lambda: act(cmc(27, 28), sm(1), scale=-0.75),
-              lambda: act(cmc(30, 31, 0, 1), R("ones", 0, 1), scale=cH0), lambda: fill(cmc(30, 31, 1, 6), 5, float(H)),
-              lambda: fill(cmc(30, 31, 6, 12), 6, float(C))])
-    ts(R("tmp", 32, 48), R("IO", 0, 16), cq1, A.is_equal, BIG, A.mult)
-    quant(R("qu"), R("su"), R("ut"))
-
-    def after_scores_vector():
-        tt(R("ext", 0, 16), R("tmp", 16, 32), R("tmp", 32, 48), A.add)
-        rank_constants()
-
-    def after_scores_scalar():
-        act(R("V0", 0, 32), R("PT", 192, 224))
-        act(R("PA", H, C), R("IO", H, C))
-        act(R("PA", 288, 480), R("IO", H, 288))
-        for h in range(2):
-            act(R("cf", C * h, C * h + C), R3("cm", 6 * h, 6 * h + 6, 0, 32))
-        together([lambda k=k: act(R("V0", 32 * k, 32 * k + 32), R("V0", 0, 32)) for k in (1, 2, 6, 7, 8)] +
-                 [lambda: fill(R("V0", H, C), H, 0.0), lambda: fill(R("V0", 288, 480), C, 0.0)])
-        together([lambda a=a, b=b, c=c: act(R("PB", a, b), R("IO", c, c + b - a)) for a, b, c in ((H, C, H), (288, 480, H))])
-
-    def spread_ext():
-        together([lambda k=k: act(R("ext", 16 * k, 16 * k + 16), R("ext", 0, 16)) for k in range(1, 6)])
-
-    def late_gpsimd():
-        mask("m16", C, 16)
-        iota(R("D1"), [[1, 16]], 1)
-        iota(R("XS", 0, 64), [[1, 64]], 0)
-        iota(R("XS", 128, 256), [[1, 128]], 0)
-        mask("m64", 256, 64)
-        iota(R("tie"), [[0, 3], [-1, 64]], -33)
-        iota(R("IOb"), [[1, C]], 0)
-        iota(R("MOD", 0, C), [[0, 2], [1, H]], 0)
-        iota(R("MOD", C, 288), [[1, H]], H)
-        iota(R("MOD", 288, 480), [[1, C]], 0)
-
-    def rank_constants():
-        together([lambda: ts(R("L15"), R("c16", 0, 6), 15.25, A.add), lambda: ts(c8, cq, 7.5, A.is_gt, 0.25, A.add),
-                  lambda: ts(cE, cown, -0.5, A.add, cM, A.mult)])
-
-    def hold_constants():
-        ts(R("tmp"), R("ext", 0, 64), 1.0 + 2.0 ** -10, A.min, -1.0, A.add)
-        ts(cS, cM, -1.0, A.add, 2.0 ** 20, A.min)
-        ts(R("L8"), R("c16", 0, 6), 0.125, A.mult, c8, A.add)
-
-    def rank_constants_scalar():
-        w16 = lambda k: (T.w16[:, k:12:4, :], [("w16", frozenset(16 * c + i for c in range(k, 12, 4) for i in range(16)))])
-        together([lambda: act(cnM, cM, scale=-1.0), lambda: act(cnMe, cM, scale=-(1.0 + 2.0 ** -22)),
-                  lambda: act(R("ext", H, C), R("ext", 0, H))] + [lambda k=k: fill(w16(k), 48, W16[k]) for k in range(4)] +
-                 [lambda: fill(R("KB", 64, 128), 64, 0.0), lambda: fill(R("KB", C, 320), 128, 0.0)])
-
-    def segment_constants_scalar():
-        together([lambda k=k: fill(R("wm", k, 12, 4), 3, -0.5 * W16[k]) for k in range(4)] +
-                 [lambda: act(R("exa"), R("tmp"), scale=2.0 ** 30), lambda: act(R("wf"), R3("w16", 0, 12, 0, 16))])
-
-    def key_constants_scalar():
-        together([lambda s=s: act(R("TE", 72 * s, 72 * s + 72), R("IO", 0, 72), scale=W64[s],
-                                  bias=W64[s] * (-32.0 if s == 0 else 1.0)) for s in range(3)])
-
-    def pick_constants_scalar():
-        wl = [193.0 - 2.0 ** m for m in range(7)] + [1.0]
-        wr = [193.0 - 2.0 ** (m + 1) for m in range(7)] + [1.0]
-        together([lambda m=m: fill(R("TH", m, H, 8), 12, 2.0 ** (m + 1) if m < 7 else 1e9) for m in range(8)] +
-                 [lambda m=m, n=n, w=w: fill(R(n, m, H, 8), 12, w[m - 1] / w[m] if m else 0.0)
-                  for n, w in (("RL", wl), ("RR", wr)) for m in range(8)])
-
-    def unwrap(out, row, n):
-        scan(out, R("ext", 0, n), row)
-
-    def signs(c0, cols, row, thr, scale, a0):
-        n = len(row(cols[0])[1][0][1])
-        together([lambda c=c: act(R("JK", n * (c - c0), n * (c - c0) + n), row(c), scale=scale, bias=thr(c), func=F.Sign,
-                                  acc=R("AC", a0 + c, a0 + c + 1)) for c in cols])
-
-    hw = lambda n, h: R(n, HB[h], HB[h + 1])
-    hl = lambda n, h: R(n, HB[h], HB[h] + H)
-    half = lambda n, h, w=H, o=0: R(n, o + w * h, o + w * h + w)
-
-    for t in range(2):
-        first = t == 0
-        peer = T.cores[rank ^ (1 << t)]
-        X, qx, sx = R("X%d" % t), R("qx%d" % t), R("sx%d" % t)
-        lq, lp, ol, lo, qf, sf = [R("%s%d" % (n, t)) for n in ("lq", "lp", "ol", "lo", "qf", "sf")]
-        Bt, Xn = "Bt%d" % t, "X%d" % (t + 1)
-        quant(qx, sx, X)
-        mm(4, R("qu"), R("su"), qx, sx)
-        send(peer, u8(lq), u8(qx), "ax%d" % t)
-        send(peer, lp, sx, "ax%d" % t)
-        arrival(peer, "ax%d" % t, 2, lq, lp)
-        if first:
-            after_scores_vector()
-            after_scores_scalar()
-            spread_ext()
-            late_gpsimd()
-        for h in range(2):
-            together([lambda k=k: ts(R3("BT", 6 * h, 6 * h + 6, 16 * k, 16 * k + 16), bank(4, H * h, H * h + H), cthr, A.is_gt,
-                                     cw, A.mult) for k in range(2)])
-        for h in range(2):
-            o, i = half("TB", h, C), R3("BT", 6 * h, 6 * h + 6, 0, 32)
-            op("v", lambda: g.vector.transpose(o[0], i[0]), i[1], o[1])
-        for h in range(2):
-            scan(half("RB", h, C), half("cf", h, C), half("TB", h, C))
-        for h in range(2):
-            tt(sm(0, 6 * h, 6 * h + 6), R("RB", C * h + 26, C * h + C, 32), R("RB", C * h + 30, C * h + C, 32), A.add)
-        for h in range(2):
-            ts(half("LS", h, 6), sm(0, 6 * h, 6 * h + 6), 0.25 - H * h, A.add)
-        for h in range(2):
-            act(hl("PA", h), ind(R("IO", 0, HB[h + 1] - HB[h]), half("LS", h, 6)))
-        pn, vn = ["PA", "PB", "PA", "PB", "PA", "PB", "PA"], ["V0", "VA", "VB", "VA", "VB", "VA"]
-        for r in range(6):
-            for h in range(2):
-                L = half("LS", h, 6, 12 * (r // 3))
-                act(hl(pn[r + 1], h), ind(hw(pn[r], h), L))
-                tt(hl(vn[r + 1], h) if r < 5 else half("K16", h), ind(hw(vn[r], h), L),
-                   hl("V0", 1 - h) if r < 3 else half("VD", h), A.add)
-            if r == 2:
-                for h in range(2):
-                    cp(half("VD", h), hl("VA", h))
-                if first:
-                    rank_constants_scalar()
-                    together([lambda b=b: quant(R("qe", 128 * b, 128 * b + 128), R("se", 128 * b, 128 * b + 128),
-                                                R("Z", 3 - b, 515 - b)) for b in range(2)])
-                for h in range(2):
-                    unwrap(half("RAW", h), hl("PB", h), H)
-                if first:
-                    together([lambda b=b: quant(R("qe", 128 * b, 128 * b + 128), R("se", 128 * b, 128 * b + 128),
-                                                R("Z", 3 - b, 515 - b)) for b in range(2, 4)])
-                for h in range(2):
-                    ts(half("LS", h, 6, 12), R("RAW", H * h + 15, H * h + H, 16), cim, A.mult, 0.25, A.add)
-        for b in range(4):
-            mm(4 + b, R("qe", 128 * b, 128 * b + 128), R("se", 128 * b, 128 * b + 128), lq, lp)
-        together([lambda b=b: mm(b, R("qe", 128 * b, 128 * b + 128), R("se", 128 * b, 128 * b + 128), qx, sx) for b in range(4)])
-        for h in range(2):
-            act(half("KS", h), half("K16", h), scale=cM)
-        for h in range(2):
-            unwrap(half("RAW2", h), half("K16", h), H)
-            if first and h == 0:
-                hold_constants()
-                segment_constants_scalar()
-        for h in range(2):
-            unwrap(half("RAW", h), hl("PA", h), H)
-            tt(half("C16", h), ind(half("RAW2", h), R("L15")), half("KS", h), A.is_gt)
-            ts(sm(2, 6 * h, 6 * h + 6), R("RAW2", H * h + 15, H * h + H, 16), cE, A.add)
-        scan(half("N16", 0), half("m16", 0), half("C16", 0))
-        ts(R("LX", 0, 24, 2), R("RAW", 15, C, 16), cim, A.mult, 0.25 - H, A.add)
-        scan(half("N16", 1), half("m16", 1), half("C16", 1))
-        for h in range(2):
-            cp(half("LR", h, 6), R("N16", H * h + 15, H * h + H, 16))
-        enter16 = lambda cols: signs(0, cols, lambda c: R("K16", 16 * c, 16 * c + 16), lambda c: sm(2, c, c + 1), cnM, 24)
-
-        def outside(be):
-            for s in (1, 2):
-                c = 4 * s + be
-                o0 = XB0[s] + 16 * c
-                act(R("XS", o0, o0 + 16), ind(R("XS", XB0[s], o0), R("LX", 2 * c, 2 * c + 1)))
-
-        def unpack(b):
-            act(R("Tp", C * b, C * b + C), bank(4 + b))
-
-        enter16(list(range(6)))
-        enter16([6, 7, 8])
-        for s in range(3):
-            o0 = KB0[s] + 64 * s
-            act(R("KB", o0, o0 + 16), ind(R("D1"), R("LR", 4 * s, 4 * s + 1)), scale=W16[0])
-        for h in range(2):
-            tt(half("U", h), ind(R("D1"), half("LR", h, 6)), half("wf", h), A.mult)
-        tt(sm(11), R("N16", 15, C, 16), R("wf", 0, C, 16), A.mult)
-        outside(0)
-        enter16([9, 10, 11])
-        outside(1)
-        unpack(0)
-        outside(2)
-        unpack(1)
-        outside(3)
-        if first:
-            ts(R("wsh"), R("wm"), 16.0, A.mult, cS, A.add)
-            key_constants_scalar()
-        for be in range(1, 4):
-            for s in range(3):
-                c = 4 * s + be
-                o0 = KB0[s] + 16 * c
-                tt(R("KB", o0, o0 + 16), ind(R("KB", KB0[s], o0), R("LX", 2 * c, 2 * c + 1)), R("U", 16 * c, 16 * c + 16), A.add)
-            if be == 1:
-                tt(sm(3), R("wsh"), sm(11), A.add)
-            elif be == 2:
-                tt(sm(4), R("AC", 24, 36), R("wm"), A.mult)
-            else:
-                tt(sm(5), sm(3), sm(4), A.add)
-        live = lambda s: R("KB", KB0[s] + 64 * s, KB0[s] + 64 * s + 64)
-        hold = lambda s: scan(R("RA", 64 * s - 64, 64 * s), R("exa"), live(s), A.add, A.max)
-        unwrap(R("RK", 0, 64), live(0), 64)
-        unwrap(R("RK", 64, 128), live(1), 64)
-        hold(1)
-        hold(2)
-        ts(sm(6, 0, 4), sm(5, 0, 4), cS, A.subtract, cnM, A.mult)
-        for s in (1, 2):
-            o0 = XB0[s] + 64 * s
-            unwrap(R("RX", 64 * s - 64, 64 * s), R("XS", o0, o0 + 64), 64)
-        rk = lambda c: R("RK", 16 * c + 15, 16 * c + 16)
-        for s in range(2):
-            signs(0, list(range(4 * s, 4 * s + 4)), lambda c: live(c // 4), rk, cnMe, 0)
-
-        def below(s):
-            together([lambda c=c: ts(R("CMP", 64 * c - 256, 64 * c - C), live(s), sm(5, c, c + 1), A.add,
-                                     R("RA", 16 * c - 49, 16 * c - 48), A.is_lt) for c in range(4 * s, 4 * s + 4)])
-
-        below(1)
-        tt(sm(4, 0, 4), R("RK", 15, 64, 16), sm(6, 0, 4), A.add)
-        below(2)
-        ts(R("LR2", 0, 4), R("AC", 0, 4), 0.5, A.mult, 32.25, A.add)
-        signs(-8, [0, 1, 2, 3], lambda c: live(0), lambda c: sm(4, c, c + 1), cnMe, 12)
-        scan(half("N64", 0, 256), R("m64"), half("CMP", 0, 256))
-        ts(R("LY"), R("RX", 15, 128, 16), cim, A.mult, 0.25, A.add)
-        unwrap(R("RK", 128, C), live(2), 64)
-        ts(R("LR2", 4, 8), R("AC", 4, 8), 0.5, A.mult, 32.25, A.add)
-        act(R("GE", 0, 64), ind(R("IO", 0, 72), R("LR2", 0, 4)), scale=W64[0], bias=-32.0 * W64[0])
-        act(R("UE", 0, 64), ind(R("IO", 0, 72), R("LR2", 4, 8)), scale=W64[1], bias=W64[1])
-        scan(half("N64", 1, 256), R("m64"), half("CMP", 1, 256))
-        cp(R("LE", 4, 8), R("N64", 63, 256, 64))
-        ts(R("LE", 0, 4), R("AC", 12, 16), 0.5, A.mult, 32.25, A.add)
-        cp(R("LE", 8, 12), R("N64", 319, 512, 64))
-
-        def enter64(s, out):
-            tt(out, ind(R("TE", 72 * s, 72 * s + 72), R("LE", 4 * s, 4 * s + 4)), R("tie", 64 * s, 64 * s + 64), A.add)
-
-        signs(-4, [8, 9, 10, 11], lambda c: live(2), rk, cnMe, 0)
-        unpack(2)
-        unpack(3)
-        enter64(1, R("UE", 64, 128))
-        enter64(2, R("UE", 128, C))
-        tt(R("GE", 64, 128), ind(R("GE", 0, 64), R("LY", 0, 4)), R("UE", 0, 64), A.add)
-        enter64(0, R("GE", 256, 320))
-        ts(sm(6, 0, 4), R("AC", 8, 12), -0.5, A.mult, -32.0, A.add)
-        tt(R("GE", 128, 256), ind(R("GE", 0, 128), R("LY")), R("UE", 64, C), A.add)
-        unwrap(R("RE", 128, C), R("GE", 256, 320), 64)
-        unwrap(R("RG"), R("GE", 0, 128), 128)
-        tt(sm(7, 8, 12), sm(6, 0, 4), R("N64", 319, 512, 64), A.add)
-        unwrap(R("RE", 0, 128), R("GE", 128, 256), 128)
-        E = R("GE", 128, 320)
-        pos = lambda c: 16 * ((c - 4) % 12) + 15
-        ent = lambda c: R("RE", pos(c), pos(c) + 1)
-        above = lambda k, thr: ts(R("CMP", C * k, C * k + C), E, cM, A.mult, thr, A.is_gt)
-        total = lambda k: scan(R("CNT", C * k, C * k + C), R("ones", 0, C), R("CMP", C * k, C * k + C))
-        signs(1, [1, 2, 3], lambda c: E, ent, cnM, 24)
-        signs(1, [4, 5, 6, 7], lambda c: E, ent, cnM, 24)
-        for k, c in enumerate((0, 8, 9, 10, 11)):
-            above(k, ent(c))
-            if k == 2:
-                total(0)
-        total(1)
-        cp(R("LP", 0, 1), R("CNT", C - 1, C))
-        together([lambda k=k: total(k) for k in (2, 3, 4)])
-        together([lambda: ts(R("LP", 1, 8), R("AC", 25, 32), -0.5, A.mult, 95.75, A.add),
-                  lambda: cp(R("LP", 8, 12), R("CNT", 2 * C - 1, 5 * C, C))])
-        lea = lambda c: R("RG", 16 * c + 15, 16 * c + 16)
-        signs(NE, list(range(NE, 8)), lambda c: E, lea, cnM, 36)
-        op("v", lambda: g.vector.tensor_copy(T.O[:].indirect(T.LP[:]), T.IOb[:]), regs(R("IOb"), R("LP")), R("O")[1])
-        cp(sm(8), R("LP"))
-        ts(R("CMP", 0, C), E, cM, A.mult, lea(0), A.is_gt)
-        unwrap(R("RO"), R("O"), C)
-        ts(R("CMP", C, 2 * C), E, cM, A.mult, lea(1), A.is_gt)
-        ts(ol, R("RO", 15, C, 16), cim, A.mult, 0.25, A.add)
-        send(peer, lo, ol, "al%d" % t)
-        arrival(peer, "al%d" % t, 1, lo)
-        if first:
-            pick_constants_scalar()
-        else:
-            together([lambda h=h: act(half("PR", h), ind(hw("MOD", h), half("LS", h, 6))) for h in range(2)])
-            dma("y", "dop", T.op[:], (T.PR[0:128:16, :], R("PR")[1]))
-        for c in range(2, NE):
-            ts(R("CMP", C * c, C * c + C), E, cM, A.mult, lea(c), A.is_gt)
-        together([lambda c=c: scan(R("CNT", C * c, C * c + C), R("ones", 0, C), R("CMP", C * c, C * c + C)) for c in range(NE)])
-        ts(sm(9, NE, 8), R("AC", 36 + NE, 44), -0.5, A.mult, 96.0, A.add)
-        if first:
-            quant(R("qv"), R("sv"), R("vt"))
-        together([lambda: tt(sm(7, 0, NE), R("CNT", C - 1, NE * C, C), sm(8, 0, NE), A.subtract),
-                  lambda: tt(sm(7, NE, 8), sm(9, NE, 8), sm(8, NE, 8), A.subtract)])
-        tt(sm(10), sm(7), sm(8), A.add)
-        tt(R("FL"), ind(sm(7), R("L8")), R("TH"), A.is_ge)
-        together([lambda b=b: act(R(Bt, b, 768, 4), ind(R("Tp", C * b, C * b + C), lo)) for b in (2, 3)])
-        together([lambda b=b: cp(R(Bt, b, 768, 4), ind(R("Tp", C * b, C * b + C), lo)) for b in (0, 1)])
-        quant(qf, sf, R(Bt))
-        for b in range(4):
-            mm(4 + b, R("qw", 128 * b, 128 * b + 128), R("sw", 128 * b, 128 * b + 128), qf, sf)
-        together([lambda: scan(half("SL", 0), R("RL"), R("FL")), lambda: scan(half("SL", 1), R("RR"), R("FL"))])
-        ts(R("TAB", 0, C), bank(4), 0.03125, A.mult)
-        for b in range(1, 4):
-            act(R("TAB", TW * b, TW * b + C), bank(4 + b), scale=0.03125)
-        together([lambda: tt(sm(11), R("SL", 7, H, 8), sm(8), A.add), lambda: tt(sm(9), R("SL", H + 7, C, 8), sm(10), A.add)])
-
-        def level(b, k):
-            n, h, a, o = 193 - 2 ** k, 2 ** (k - 1), TW * b + OFF[k - 1], TW * b + OFF[k]
-            scan(R("TAB", o, o + n), R("TAB", a, a + n), R("TAB", a + h, a + h + n), A.min, A.max, 1e29)
-
-        win = lambda b: R("TAB", TW * b, TW * b + OFF[8])
-
-        def left(b):
-            act(R("G1", C * b, C * b + C), ind(win(b), R("LL", 0, 12)))
-
-        def pick(b):
-            tt(R("MX", C * b, C * b + C), ind(win(b), R("LL", 12, 24)), R("G1", C * b, C * b + C), A.max)
-
-        def plus(b):
-            tt(R(Xn, b, 768, 4), R("MX", C * b, C * b + C), bank(b), A.add)
-
-        steps = [(k + LAG[b], 0, level, (b, k)) for b in range(4) for k in range(1, 8)]
-        steps += [(7 + LAG[b], 1, left, (b,)) for b in range(4)]
-        steps += [(PICK[b], 2, pick, (b,)) for b in range(4)] + [(PLUS[b], 3, plus, (b,)) for b in range(4)]
-        for i, (_, _, fn, args) in enumerate(sorted(steps, key=lambda z: z[:2])):
-            fn(*args)
-            if i == 0:
-                together([lambda: ts(R("LL", 0, 12), sm(11), 0.25, A.add), lambda: ts(R("LL", 12, 24), sm(9), -0.75, A.add)])
-
-    quant(R("qx2"), R("sx2"), R("X2"))
-    mm(4, R("qv"), R("sv"), R("qx2"), R("sx2"))
-    dma("s", "doc", T.oc[:], u8(R("qx2")))
-    for k, e in enumerate(("y", "s", "y", "s")):
-        dma(e, "ds%d" % k, T.osc[4 * k:4 * k + 4, :], (T.sx2[32 * k:32 * k + 4, :], R("sx2")[1]))
-    cp(R("Y"), bank(4))
-    dma("y", "dy", T.y[:], R("Y"))
+            b = cur[e]
+            if b and any(s["start"] < c["end"] + JOIN * WAKE and s["behind"] is not p and (s["behind"] is c or all(s is not n for n in c["next"]))
+                         for p in b["calls"] for s in p["next"]):
+                b = None
+            if b is None:
+                ring = [e + str((nxt[e] + i) % POOL[e]) for i in range(POOL[e])]
+                sem = next((s for s in ring if s not in last or last[s]["id"] in known[e]), ring[0])
+                nxt[e] = int(sem[1:]) + 1
+                base = 0
+                if sem in last:
+                    wait(e, last[sem])
+                    base = last[sem]["n"]
+                b = cur[e] = new_batch(e, sem, base)
+            c["fn"]().then_inc(T.sem[b["sem"]], 1)
+            b["n"] += 1
+            b["calls"].append(c)
+            c["batch"] = b
     g.wait_ge(T.sem.ls, sent[0])
     for sem in SEMAPHORES:
         if sem in last and not last[sem]["waited"]:

import numpy as np
from concourse.mybir import dt, AluOpType, ActivationFunctionType

A = AluOpType
F = ActivationFunctionType
C = 192
H = 96
BIG = 2.0 ** 60
MAGIC = 12582912.0
W16 = [4913.0, 289.0, 17.0, 1.0]
W64 = [278920.0, 4290.0, 65.0]
KB0 = [0, 64, 192]
XB0 = [0, 0, 128]
HB = [0, 192, 576]
TW = 1296
NV = 6
NE = 3
ENTER_V = [0]
STEP = [(0, 4), (4, 8), (8, 12)]
HOLD = [(0, 64), (64, 128), (128, 192)]
ROW_V = [0]
DIGIT_V = [0, 1]
BLOCK_V = []
LEAVE_V = [0]
LAST = 1
TWO = [0]
FIRST = [(0, 4), (4, 8)]
LEAF_V = [1]
CHAIN_V = [0, 1]
UNPACK_V = []
EARLY = [4000, 600, 600]
JOIN = 6.0
COPY_V = [0, 1]
OFF = [193 * k - 2 ** k + 1 for k in range(9)]
WL = [193.0 - 2.0 ** m for m in range(7)]
WR = [193.0 - 2.0 ** (m + 1) for m in range(7)]
WAKE, LEAST, GATHER, SCATTER, LOAD, REMOTE, ISSUE = 277, 64, 1.56, 3.8, 1100, 1050, 360
SCALAR = [80, 33]
PLAN = 1.05
MACHINES = [(1 / 1.05, 0, 0), (1 / 1.05, 15, -10), (1.35 / 1.05, 0, 0)]
WALKS, NOISE, PART, SWAPS, TABU, SPEEDS, STARTS = 901, 700, 0.025, 0, 20, (1.0,), []
WAVE = [(0, 1), (1, 1), (2, 1), (0, 2), (3, 1), (1, 2), (0, 3), (2, 2), (1, 3), (0, 4), (3, 2), (2, 3), (1, 4), (0, 5), (3, 3),
        (1, 5), (0, 6), (2, 4), (3, 4), (0, 7), (1, 6), (2, 5), (3, 5), (1, 7), (2, 6), (3, 6), (2, 7), (0, 8), (3, 7), (1, 8),
        (0, 9), (2, 8), (3, 8), (1, 9), (2, 9), (3, 9)]
X4, U8, U16, F32, B16 = "float8_e4m3fn_x4", "uint8", "uint16", "float32", "bfloat16"

SCRATCH = {}
for _n, _w, _d in [
    ("X0", 768, B16), ("X1", 768, B16), ("X2", 768, B16),
    ("qx0", C, X4), ("qx1", C, X4), ("qx2", C, X4), ("sx0", C, U8), ("sx1", C, U8), ("sx2", C, U8),
    ("lq0", C, X4), ("lq1", C, X4), ("lp0", C, U8), ("lp1", C, U8),
    ("ol0", 12, U16), ("ol1", 12, U16), ("lo0", 12, U16), ("lo1", 12, U16),
    ("Bt0", 768, B16), ("Bt1", 768, B16), ("qf0", C, X4), ("qf1", C, X4), ("sf0", C, U8), ("sf1", C, U8),
    ("ut", 512, B16), ("vt", 512, B16), ("qu", 128, X4), ("su", 128, U8), ("qv", 128, X4), ("sv", 128, U8),
    ("qh", 256, X4), ("sh", 256, U8), ("qw", 512, X4), ("sw", 512, U8), ("Z", 528, B16), ("qe", 512, X4), ("se", 512, U8),
    ("Tp", 768, B16), ("TB", 384, B16), ("RB", 384, F32), ("cf", 384, F32),
    ("PT", 224, F32), ("PC", 224, F32), ("col", 16, F32), ("tmp", 128, F32), ("c16", 12, F32), ("c16f", 12, F32),
    ("e16", 288, B16), ("wm", 36, F32), ("wf", C, F32), ("IO", 384, F32), ("IOb", C, B16), ("MOD", 384, F32),
    ("ext", C, B16), ("ones", 256, B16), ("m16", C, B16), ("m64", 256, B16),
    ("TE", 216, F32), ("D1", 16, F32), ("TH", 7, F32), ("RL", 216, F32), ("FL", 108, F32), ("SL", 216, F32),
    ("PA", 576, F32), ("PB", 576, F32), ("V0", 576, F32), ("VA", 576, F32), ("VB", 576, F32), ("VD", C, F32),
    ("K16", C, F32), ("KS", C, F32), ("R4", C, F32), ("R16", C, F32), ("RP", C, F32), ("RK", 576, F32), ("RE", C, F32),
    ("RA", 36, F32), ("RX", C, F32), ("RG", 128, F32), ("sm", 320, F32),
    ("LS", 36, U16), ("LX", 24, U16), ("LR", 36, U16), ("LR2", 8, U16), ("LE", 12, U16), ("LY", 16, U16),
    ("LP", 12, U16), ("LL", 24, U16), ("L15", 12, U16),
    ("C16", 2 * C, B16), ("N16", 2 * C, B16), ("KE", C, F32), ("C64", 1280, B16), ("N64", 1280, B16), ("CMP", 14 * C, B16), ("CNT", 14 * H, B16),
    ("JK", 7552, B16), ("AC", 64, F32),
    ("U", C, F32), ("KB", 384, F32), ("XS", 320, F32), ("GE", 384, F32), ("UE", 128, F32),
    ("tie", 128, F32), ("T1", 128, F32), ("T2", 64, F32), ("XZ", 64, F32),
    ("O", C, B16), ("RO", C, B16), ("PR", C, F32),
    ("TAB", 4 * TW, F32), ("G1", 768, F32), ("MX", 768, F32), ("Y", C, F32),
]:
    SCRATCH[_n] = ("sbuf", [128, _w], _d)
SCRATCH["BT"] = ("sbuf", [128, 12, 32], B16)
SCRATCH["cm"] = ("sbuf", [128, 12, 32], B16)
SCRATCH["ps"] = ("psum", [128, 4096], F32)

POOL = {"v": 63, "s": 44, "t": 10, "g": 12}
DMAS = ["dx", "du", "dv", "dwc", "dws", "dop", "doc", "dod", "ds0", "ds1", "ds2", "ds3", "dy", "dz"]
SEMAPHORES = [e + str(i) for e in POOL for i in range(POOL[e])] + DMAS + ["ax0", "ax1", "al0", "al1", "ls"]


def order_calls(calls):
    def gap(early, late):
        return 0 if late["behind"] is early else early["lat"] + (WAKE if late["e"] else 0)

    def walk(ahead):
        prev, nxt = ("prev", "next") if ahead else ("next", "prev")
        free, ready, start, opn, at = {}, {}, {}, {}, {}
        for c in calls:
            opn[c["id"]], at[c["id"]] = len(c[prev]), 0 if ahead else c["lat"]
            if not c[prev]:
                ready.setdefault(c["e"], []).append(c)
        while len(start) < len(calls):
            best = None
            for e, cs in ready.items():
                if not cs:
                    continue
                now = free.get(e, 0) if e else 0
                top = max(cs, key=lambda c: c["chain"])

                def merit(c):
                    st = max(now, at[c["id"]])
                    late = st + c["chain"]
                    if c is not top:
                        late = max(late, max(st + c["len"], at[top["id"]]) + top["chain"])
                    return (late, st, -c["chain"])
                c = min(cs, key=merit) if e else min(cs, key=lambda c: at[c["id"]])
                st = max(now, at[c["id"]])
                if best is None or st < best[0]:
                    best = (st, c)
            st, c = best
            ready[c["e"]].remove(c)
            start[c["id"]] = st
            free[c["e"]] = st + c["len"]
            for s in c[nxt]:
                early, late = (c, s) if ahead else (s, c)
                opn[s["id"]] -= 1
                at[s["id"]] = max(at[s["id"]], st + c["len"] + gap(early, late))
                if not opn[s["id"]]:
                    ready.setdefault(s["e"], []).append(s)
        return start

    for c in reversed(calls):
        c["chain"] = c["len"] + max([gap(c, s) + s["chain"] for s in c["next"]], default=c["lat"])

    def length(order, slow, scalar, wake):
        free, end = {}, {}
        for c in order:
            at = max([end[p["id"]] + (gap(p, c) and gap(p, c) + (wake if c["e"] else 0)) for p in c["prev"]], default=0)
            at = max(at, free.get(c["e"], 0) if c["e"] else 0)
            end[c["id"]] = free[c["e"]] = at + slow * c["len"] + (scalar if c["e"] == "s" else 0)
        return max(end[c["id"]] + c["lat"] for c in calls) / slow ** 0.6

    best, rng = None, np.random.default_rng(1)
    for k in range(WALKS):
        start = walk(k % 2 == 0)
        if k % 2 == 0:
            order = sorted(calls, key=lambda c: (start[c["id"]], c["id"]))
            end = sum(length(order, *m) for m in MACHINES)
            if best is None or end <= best[0]:
                best = (end, start)
            start = best[1]
        lead = (NOISE * rng.random(len(calls)) * (rng.random(len(calls)) < PART)).tolist()
        for c in calls:
            c["chain"] = start[c["id"]] + c["len"] + lead[c["twin"]]
    return [best[1][c["id"]] for c in calls]
    n = len(calls)
    queues = {}
    for c in sorted(calls, key=lambda c: (best[1][c["id"]], c["id"])):
        if c["e"]:
            queues.setdefault(c["e"], []).append(c["id"])
    succ = [[(s["id"], gap(c, s)) for s in c["next"]] for c in calls]
    lens = [[c["len"] * f for c in calls] for f in SPEEDS]
    base = [len(c["prev"]) for c in calls]

    def times(ln):
        after, opn, at, why = [-1] * n, list(base), [0] * n, [-1] * n
        for q in queues.values():
            for a, b in zip(q, q[1:]):
                after[a] = b
                opn[b] += 1
        todo, seen = [i for i in range(n) if not opn[i]], []
        while todo:
            i = todo.pop()
            seen.append(i)
            e = at[i] + ln[i]
            for j, d in succ[i] + ([(after[i], 0)] if after[i] >= 0 else []):
                if e + d > at[j]:
                    at[j], why[j] = e + d, i
                opn[j] -= 1
                if not opn[j]:
                    todo.append(j)
        tail, own = [0] * n, [0] * n
        for i in reversed(seen):
            own[i] = max([d + ln[j] + tail[j] for j, d in succ[i]], default=lats[i])
            tail[i] = own[i] if after[i] < 0 else max(own[i], ln[after[i]] + tail[after[i]])
        end = max((at[i] + ln[i] + lats[i], i) for i in range(n))
        return end[0], end[1], at, why, after, tail, own

    def swapped(r, ln, i, j, h):
        at, after, tail, own = r[2], r[4], r[5], r[6]
        first = max([at[p] + ln[p] + d for p, d in pred[j]] + [at[h] + ln[h] if h >= 0 else 0])
        second = max([at[p] + ln[p] + d for p, d in pred[i]] + [first + ln[j]])
        ti = own[i] if after[j] < 0 else max(own[i], ln[after[j]] + tail[after[j]])
        tj = max(own[j], ln[i] + ti)
        new, old = max(first + ln[j] + tj, second + ln[i] + ti), max(at[x] + ln[x] + tail[x] for x in (i, j))
        return new if old >= r[0] - 1 else max(new, r[0])

    lats = [c["lat"] for c in calls]
    pred = [[(p["id"], gap(p, c)) for p in c["prev"]] for c in calls]
    top, kept, tabu = None, None, {}
    for k in range(SWAPS + 1):
        rs = [times(ln) for ln in lens]
        now = sum(r[0] / f for r, f in zip(rs, SPEEDS))
        if top is None or now < top:
            top, kept = now, rs[0][2]
        tried = []
        for r in rs:
            j = r[1]
            while r[3][j] >= 0:
                i = r[3][j]
                if r[4][i] == j and all(s != j for s, _ in succ[i]) and tabu.get((i, j), -1) < k:
                    q = queues[calls[i]["e"]]
                    p = q.index(i)
                    tried.append((sum(swapped(x, ln, i, j, q[p - 1] if p else -1) / f for x, ln, f in zip(rs, lens, SPEEDS)), i, j, p))
                j = i
        if not tried:
            break
        _, i, j, p = min(tried)
        q = queues[calls[i]["e"]]
        q[p], q[p + 1] = j, i
        tabu[(j, i)] = k + TABU
    return kept


def rank_program(g, core, T, topo):
    rank = T.rank_of(core)
    if rank is None:
        return
    Q = {"v": g.vector, "s": g.scalar, "t": g.tensor, "g": g, "y": g.sync}
    calls, hist, back, began = [], {}, [0], []

    def R(n, a=0, b=None, s=1):
        b = SCRATCH[n][1][1] if b is None else b
        cols = frozenset(range(a, b, s))
        return (T[n][:, a:b:s] if s != 1 else T[n][:, a:b], [(n, cols)], len(cols), SCRATCH[n][2] in (B16, U16), "sbuf")

    def R3(n, a, b, c, d, s=1):
        w = SCRATCH[n][1][2]
        cols = frozenset(i * w + j for i in range(a, b, s) for j in range(c, d))
        return (T[n][:, a:b:s, c:d] if s != 1 else T[n][:, a:b, c:d], [(n, cols)], len(cols), SCRATCH[n][2] == B16, "sbuf")

    def bank(b, lo=0, hi=C):
        return (T.ps[:, 512 * b + lo:512 * b + hi], [("ps", frozenset([b]))], hi - lo, False, "psum")

    def ind(win, off):
        return (win[0].indirect(off[0]), win[1] + off[1], 16 * off[2], False, "list")

    def u8(x):
        return (x[0].bitcast(dt.uint8),) + x[1:]

    def ap(x):
        return x[0] if isinstance(x, tuple) else x

    def regs(*xs):
        return [r for x in xs if isinstance(x, tuple) for r in x[1]]

    def op(e, fn, reads, writes, length, lat=0, sem=None, count=1, after=()):
        c = {"id": len(calls), "e": e, "fn": fn, "len": PLAN * length, "lat": lat, "sem": sem, "count": count, "next": [],
             "behind": None, "twin": len(calls) - back[0]}
        prev = {p["id"]: p for p in after}
        for w, rs in ((False, reads), (True, writes)):
            for n, cols in rs:
                for (c2, w2, p) in hist.get(n, []):
                    if (w or w2 or (n == "ps" and p["e"] != e)) and not cols.isdisjoint(c2):
                        prev[p["id"]] = p
        c["prev"] = list(prev.values())
        for p in c["prev"]:
            p["next"].append(c)
        for w, rs in ((False, reads), (True, writes)):
            for n, cols in rs:
                h = hist.setdefault(n, [])
                if w:
                    h[:] = [x for x in h if not x[0] <= cols]
                h.append((cols, w, c))
        calls.append(c)
        return c

    def follow(p):
        c = calls[-1]
        if p is not None and all(p is not x for x in c["prev"]):
            c["prev"].append(p)
            p["next"].append(c)
            c["behind"] = p
        return c

    def cycles(fixed, src, *sides):
        if src[4] == "list":
            return fixed + GATHER * src[2]
        return max(LEAST, src[2] / (2 if all(x[3] for x in (src,) + sides) else 1))

    def dma(e, sem, out, in_, size, also=()):
        op(e, lambda: Q[e].dma_start(ap(out), ap(in_)), regs(in_, *also), regs(out), 100, LOAD + size / 150, sem, 16)

    def ts(out, in0, s1, o0, s2=None, o1=None):
        if o1 is None:
            fn = lambda: g.vector.tensor_scalar(out[0], in0[0], ap(s1), None, o0)
        else:
            fn = lambda: g.vector.tensor_scalar(out[0], in0[0], ap(s1), ap(s2), o0, o1)
        op("v", fn, regs(in0, s1, s2), out[1], cycles(60, in0, out))

    def tt(out, in0, in1, o):
        n = cycles(60, in0) if in0[4] == "list" else max(LEAST, in0[2] * (1 if "psum" in (in0[4], in1[4]) else 2))
        op("v", lambda: g.vector.tensor_tensor(out[0], in0[0], in1[0], o), regs(in0, in1), out[1], n)

    def scan(out, d0, d1, o0=A.mult, o1=A.add, init=0.0):
        op("v", lambda: g.vector.tensor_tensor_scan(out[0], d0[0], d1[0], init, o0, o1), regs(d0, d1), out[1],
           cycles(0, d0, d1, out))

    def cp(out, in_):
        op("v", lambda: g.vector.tensor_copy(out[0], in_[0]), in_[1], out[1], cycles(60, in_, out))

    def turn(out, in_):
        op("v", lambda: g.vector.transpose(out[0], in_[0]), in_[1], out[1], cycles(0, in_, out))

    def ms(out, c):
        op("v", lambda: g.vector.memset(out[0], c), [], out[1], cycles(0, out))

    def act(out, in_, scale=None, bias=None, func=None, acc=None):
        kw = {}
        if scale is not None:
            kw["scale"] = ap(scale)
        if bias is not None:
            kw["bias"] = ap(bias)
        if acc is not None:
            kw["accum_out"] = acc[0]
        fu = func if func is not None else (F.Identity if bias is not None else F.Copy)
        n = (80 + GATHER * in_[2] if in_[4] == "list" else max(SCALAR[0], in_[2] + SCALAR[1])) + (24 if acc else 0)
        op("s", lambda: g.scalar.activation(out[0], in_[0], fu, **kw), regs(in_, scale, bias), regs(out, acc), n)

    def quant(q, s, x, early=0):
        op("v", lambda: g.vector.quantize_mx(q[0], s[0], x[0]), x[1], regs(q, s), 15 + 0.265 * x[2], early)

    def mm(b, lq, ls, rq, rs):
        op("t", lambda: g.tensor.matmul_mx(bank(b, 0, rq[2])[0], lq[0], ls[0], rq[0], rs[0], True, True),
           regs(lq, ls, rq, rs), bank(b)[1], 0.72 * (rq[2] + 16))

    def iota(out, pattern, base):
        op("g", lambda: g.iota(out[0], pattern, base, 0, allow_small_or_imprecise_dtypes=True), [], out[1], 160 + 2 * out[2])

    def select(out, pattern, compare, step, after=()):
        op("g", lambda: g.affine_select(out[0], T.ones[:, 0:out[2]], pattern, compare, 0.0, 0, step), R("ones")[1], out[1],
           200 + 2 * out[2], after=after)

    sent = [0]

    def exchange(peer, sem, pairs):
        rid, pid, _ = topo.addr(peer)
        sends = []
        for dst, src, size in pairs:
            fn = lambda dst=dst, src=src: g.remote_dma(dst[0], src[0], T.sem[sem], T.sem.ls, pid, rid, topo.mask(core, peer))
            sends.append(op("g", fn, src[1], [], ISSUE if sent[0] else 18 * ISSUE, REMOTE + (size / 150 + EARLY[1] if size else 0), "", 0))
            sent[0] += len(topo.engines(core, peer))
        op(None, None, [], regs(*[p[0] for p in pairs]), 0, 0, sem, len(pairs) * len(topo.engines(peer, core)), sends)

    def fill(out, c):
        act(out, R("ones", 0, out[2]), scale=c)

    cw, cthr, cq, ch, cM, cim, cown = [R("PC", 32 * i, 32 * i + 1) for i in range(7)]
    cj, cjq, cA, cB, c16B, cih, cnM, cnMe, cE, cq1, c8, cS = [R("col", i, i + 1) for i in range(12)]
    sm = lambda k, a=0, b=12: R("sm", 16 * k + a, 16 * k + b)
    blocks = lambda n: [R(n, 128 * b, 128 * b + 128) for b in range(4)]

    dma("y", "dx", R("X0"), T.x[:], 128 * 1536)
    dma("s", "du", R("ut"), T.u[:], 128 * 1024)
    quant(R("qu"), R("su"), R("ut"))
    dma("y", "dwc", u8(R("qw")), T.wc[:], 128 * 2048, [R("X0"), R("ut")])
    dma("y", "dws", R("sw"), T.ws[:], 128 * 512, [R("X0"), R("ut")])
    dma("y", "dv", R("vt"), T.v[:], 128 * 1024, [R("X0"), R("ut")])
    quant(R("qv"), R("sv"), R("vt"))

    ms(R("ones"), 1.0)
    ms(R("Z"), 0.0)
    iota(R("PT", 64, 96), [[0, 2], [1, 16]], 0)
    iota(R("PT", 96, 128), [[1, 2], [0, 16]], 0)
    iota(R("c16"), [[16, 12]], 0)
    iota(R("IO", 0, C), [[1, C]], 0)
    act(R("IO", C, 384), R("IO", 0, C), bias=float(C))
    for a, b, c in ((0, 32, 0.0), (32, 64, -1e29), (128, 160, BIG), (160, 192, 1.0 / BIG)):
        ms(R("PT", a, b), c)
    for a, b, s, c in ((0, 8, 1, 1.0), (16, 24, 1, 1.0), (24, 25, 1, -0.498046875), (25, 29, 3, MAGIC), (26, 30, 3, -MAGIC),
                       (27, 28, 1, 1.25), (32, 40, 1, 0.0), (48, 56, 1, 0.0), (143, 192, 16, 1.0)):
        fill(R("PT", a, b, s), c)
    ms(R("tmp", 0, 16), 0.5)
    for k in range(2):
        scan(R("PT", 192 + 16 * k, 208 + 16 * k), R("tmp", 0, 16), R("Z", 0, 16), init=65536.0)
    turn(R("PC"), R("PT"))
    select(R("Z", 3, 515, 4), [[-1, 128]], A.is_equal, 1)
    for b in range(4):
        quant(blocks("qe")[b], blocks("se")[b], R("Z", 3 - b, 515 - b), EARLY[0])
    act(cj, ch, scale=0.5, bias=0.5 / BIG)
    act(cA, ch, scale=0.5, bias=0.5)
    act(cB, ch, scale=-0.5, bias=1.0)
    act(c16B, ch, scale=-BIG, bias=BIG)
    act(cjq, cq, scale=cj)
    act(cih, cim, scale=0.5)
    cmc = lambda a, b, lo=0, hi=12: R3("cm", lo, hi, a, b)
    ms(cmc(0, 32), 1.0)
    for a, b, c in ((0, 1, ch), (1, 8, cA), (16, 17, c16B), (17, 24, cB)):
        fill(cmc(a, b), c)
    act(cmc(24, 25), R("c16"), scale=cj, bias=cjq)
    for h in range(2):
        act(R("cf", C * h, C * h + C), R3("cm", 6 * h, 6 * h + 6, 0, 32))
    iota(R("c16f"), [[32, 12]], -1)
    op("v", lambda: g.vector.reciprocal(sm(1)[0], T.c16f[:]), R("c16f")[1], sm(1)[1], 300)
    act(R("cf", 59, 384, 32), sm(1, 1, 12), scale=-1.5, bias=2.0)
    fill(R("cf", 27, 28), 8.0)
    ts(R("cf", 28, 29), cq, 0.0, A.is_equal, 0.25, A.max)
    ts(cq1, cq, 1.0, A.add)
    iota(R("e16", 0, H), [[0, 6], [1, 16]], 0)
    ts(R("e16", H, C), R("e16", 0, H), cq, A.not_equal)
    ts(R("e16", C, 288), R("e16", 0, H), cq1, A.is_equal, BIG, A.mult)
    tt(R("ext", 0, H), R("e16", H, C), R("e16", C, 288), A.add)
    act(R("ext", H, C), R("ext", 0, H))
    act(cnM, cM, scale=-1.0)
    act(cnMe, cM, scale=-(1.0 + 2.0 ** -22))
    ts(cE, cown, -0.5, A.add, cM, A.mult)
    for k in range(3):
        act(R("V0", 64 * k, 64 * k + 64, 2), R("PT", 192, 224))
    act(R("V0", 384, 576, 2), R("V0", 0, C, 2))
    for a, b, s, i in ((1, C, 2, 1), (C, 384, 1, 0), (385, 576, 2, 193)):
        fill(R("V0", a, b, s), 0.0)
        ms(R("VA", a, b, s), 0.0)
        ms(R("VB", a, b, s), 0.0)
        act(R("PA", a, b, s), R("IO", i, i + b - a, s))
        iota(R("PB", a, b, s), [[s, len(range(a, b, s))]], i)
    iota(R("KB", 64, 128), [[0, 64]], 0)
    iota(R("KB", C, 320), [[0, 128]], 0)
    iota(R("XS", 0, 64), [[1, 64]], 0)
    iota(R("XS", 128, 256), [[1, 128]], 0)
    iota(R("MOD"), [[1, C], [0, 2]], 0)
    select(R("m16"), [[0, 12], [1, 16]], A.not_equal, 0)
    select(R("m64"), [[0, 4], [1, 64]], A.not_equal, 0)
    iota(R("D1"), [[1, 16]], 1)
    iota(R("UE", 0, 64), [[0, 64]], 0)
    iota(R("tie"), [[0, 2], [-1, 64]], -33)
    act(R("IOb"), R("IO", 0, C))
    for c in range(4):
        iota(R("wf", 16 * c, 16 * c + 16), [[0, 16]], int(W16[c]))
    for s in (1, 2):
        act(R("wf", 64 * s, 64 * s + 64), R("wf", 0, 64))
    iota(R("wm"), [[0, 12], [1, 3]], 0)
    ts(R("wm", 2, 36, 3), R("wf", 0, C, 16), cM, A.mult, 0.5, A.mult)
    act(R("TE", 0, 72), R("IO", 0, 72), scale=W64[0], bias=-32.0 * W64[0])
    for s in (1, 2):
        iota(R("TE", 72 * s, 72 * s + 72), [[int(W64[s]), 72]], int(W64[s]))
    ts(R("L15"), R("c16"), 15.25, A.add)
    for m in range(7):
        fill(R("TH", m, m + 1), 0.5 - 2.0 ** (m + 1))
    for k, w in enumerate((WL + [2.0, 2.0], WR + [2.0, 2.0])):
        for m in range(9):
            fill(R("RL", 108 * k + m, 108 * k + 108, 9), w[m - 1] / w[m] if m else 0.0)

    def unwrap(out, row):
        scan(out, R("ext", 0, row[2]), row)

    def signs(j0, cols, row, thr, scale, a0, to="AC", step=1):
        for i, c in enumerate(cols):
            n, a = row(c)[2], a0 + step * c
            act(R("JK", j0 + n * i, j0 + n * i + n), row(c), scale=scale, bias=thr(c), func=F.Sign, acc=R(to, a, a + 1))

    hw = lambda n, h: R(n, HB[h], HB[h + 1])
    hl = lambda n, h: R(n, HB[h] + C * h, HB[h + 1], 2)
    half = lambda n, h, w=H, o=0: R(n, o + w * h, o + w * h + w)

    def scores(x, q, s):
        for h in range(2):
            quant(half("qh", h, 128), half("sh", h, 128), R(x, 256 * h, 256 * h + 512))
            mm(4 + h, R(q), R(s), half("qh", h, 128), half("sh", h, 128))

    for t in range(2):
        began.append(len(calls))
        back[0] = began[t] - began[0]
        peer = T.cores[rank ^ (1 << t)]
        X, qx, sx = R("X%d" % t), R("qx%d" % t), R("sx%d" % t)
        lq, lp, ol, lo, qf, sf = [R("%s%d" % (n, t)) for n in ("lq", "lp", "ol", "lo", "qf", "sf")]
        Bt, Xn = "Bt%d" % t, "X%d" % (t + 1)
        scores("X%d" % t, "qu", "su")
        quant(qx, sx, X)
        exchange(peer, "ax%d" % t, [(u8(lq), u8(qx), 128 * 768), (lp, sx, 128 * C)])
        for h in range(2):
            for k in range(2):
                ts(R3("BT", 6 * h, 6 * h + 6, 16 * k, 16 * k + 16), bank(4 + h, 32 * h, 32 * h + H), cthr, A.is_gt, cw, A.mult)
            turn(half("TB", h, C), R3("BT", 6 * h, 6 * h + 6, 0, 32))
            scan(half("RB", h, C), half("cf", h, C), half("TB", h, C))
            cp(half("LS", h, 6), R("RB", C * h + 29, C * h + C, 32))
        for b in range(4):
            mm(4 + b, blocks("qe")[b], blocks("se")[b], lq, lp)
            (cp if b in UNPACK_V else act)(R("Tp", C * b, C * b + C), bank(4 + b))
            calls[-1]["lat"] = EARLY[2]
            mm(b, blocks("qe")[b], blocks("se")[b], qx, sx)
        for h in range(2):
            L1, L4 = half("LS", h, 6), half("LS", h, 6, 12)
            (cp if h in ROW_V else act)(hl("PA", h), ind(R("IO", 0, HB[h + 1] - HB[h]), L1))
            for p0, p1, v0, v1 in (("PA", "PB", "V0", "VA"), ("PB", "PA", "VA", "VB"), ("PA", "PB", "VB", "VA")):
                act(hl(p1, h), ind(hw(p0, h), L1))
                tt(hl(v1, h), ind(hw(v0, h), L1), hl("V0", 1 - h), A.add)
            (cp if h in CHAIN_V else act)(half("VD", h), hl("VA", h))
            unwrap(half("R4", h), hl("PB", h))
            ts(L4, R("R4", H * h + 15, H * h + H, 16), cim, A.mult, 0.25, A.add)
            for p0, p1, v0, v1 in (("PB", "PA", "VA", "VB"), ("PA", "PB", "VB", "VA"), ("PB", "PA", "VA", "K16")):
                act(hl(p1, h), ind(hw(p0, h), L4))
                tt(half(v1, h) if v1 == "K16" else hl(v1, h), ind(hw(v0, h), L4), half("VD", h), A.add)
            act(half("KS", h), half("K16", h), scale=cM)
            unwrap(half("R16", h), half("K16", h))
            tt(half("C16", h), ind(half("R16", h), R("L15", 0, 6)), half("KS", h), A.is_gt)
            scan(half("N16", h), R("m16", 0, H), half("C16", h))
            cp(half("LR", h, 6), R("N16", H * h + 15, H * h + H, 16))
            for a, b in ((0, 4), (4, 6)) if h == 0 else ((6, 8), (8, 12)):
                o0 = KB0[a // 4] + 16 * a
                tt(R("KB", o0, o0 + 16 * (b - a)), ind(R("D1"), R("LR", a, b)), R("wf", 16 * a, 16 * b), A.mult)
            unwrap(half("RP", h), hl("PA", h))
        ts(R("LX", 0, 24, 2), R("RP", 15, C, 16), cih, A.mult, -0.25, A.add)
        for h in range(2):
            if h in BLOCK_V:
                ts(sm(2, 6 * h, 6 * h + 6), R("R16", H * h + 15, H * h + H, 16), cE, A.add)
            else:
                act(sm(2, 6 * h, 6 * h + 6), R("R16", H * h + 15, H * h + H, 16), bias=cE)
            signs(H * h, range(6 * h, 6 * h + 6), lambda c: R("K16", 16 * c, 16 * c + 16), lambda c: sm(2, c, c + 1), cnM,
                  29, "RK", 48)
        for c in range(12):
            s, lx = c // 4, R("LX", 2 * c, 2 * c + 1)
            o0 = KB0[s] + 16 * c
            if c % 4:
                tt(R("KB", o0, o0 + 16), ind(R("KB", KB0[s], o0), lx), R("KB", o0, o0 + 16), A.add)
            if s:
                o0, p0 = XB0[s] + 16 * c, HB[c // 6] + 32 * c
                if c % 4:
                    act(R("XS", o0, o0 + 16), ind(R("XS", XB0[s], o0), lx))
                else:
                    act(R("XS", o0, o0 + 16), R("PA", p0, p0 + 32, 2), scale=0.5, bias=-0.5)
        for s in (1, 2):
            unwrap(R("RX", 64 * s - 64, 64 * s), R("XS", XB0[s] + 64 * s, XB0[s] + 64 * s + 64))
        ts(R("LY", 8, 16), R("RX", 15, 128, 16), cim, A.mult, 0.25, A.add)
        act(R("XZ"), ind(R("XS", 0, 128), R("LY", 12, 16)))
        unwrap(R("RX", 128, C), R("XZ"))
        ts(R("LY", 4, 8), R("RX", 143, C, 16), cim, A.mult, 0.25, A.add)
        live = lambda s: R("KB", KB0[s] + 64 * s, KB0[s] + 64 * s + 64)
        act(R("RK", 13, 576, 48), R("N16", 15, C, 16), scale=-2.0, bias=16.0)
        for s in range(3):
            unwrap(R("RK", C * s, C * s + C, 3), live(s))
        held = lambda c: R("RK", 48 * c + 45, 48 * c + 46)
        for s in range(3):
            if s in LEAF_V:
                for c in range(4 * s, 4 * s + 4):
                    ts(R("C64", 768 + 64 * c, 832 + 64 * c), live(s), cM, A.mult, held(c), A.is_lt)
                scan(half("N64", 3 + s, 256), R("m64"), half("C64", 3 + s, 256))
                cp(R("LR2", 4 * s, 4 * s + 4), R("N64", 256 * s + 831, 256 * s + 1024, 64))
            else:
                signs(192 + 256 * s, range(4 * s, 4 * s + 4), lambda c: live(s), held, cnMe, 12)
                if s < 2:
                    ts(R("LR2", 4 * s, 4 * s + 4), R("AC", 12 + 4 * s, 16 + 4 * s), 0.5, A.mult, 32.25, A.add)
        for a, b in STEP:
            scan(R("RA", 3 * a, 3 * b), R("wm", 3 * a, 3 * b), R("RK", 48 * a + 13, 48 * b, 16))
        thr = lambda c: R("RA", 3 * c + 2, 3 * c + 3)
        for s in range(3):
            cols = range(4 * s, 4 * s + 4)
            if s in ENTER_V:
                for c in cols:
                    ts(R("C64", 64 * c, 64 * c + 64), live(s), cM, A.mult, thr(c), A.is_lt)
                scan(half("N64", s, 256), R("m64"), half("C64", s, 256))
                cp(R("LE", 4 * s, 4 * s + 4), R("N64", 256 * s + 63, 256 * s + 256, 64))
            else:
                signs(3520 + 256 * s, cols, lambda c: live(s), thr, cnMe, 48)
                ts(R("LE", 4 * s, 4 * s + 4), R("AC", 48 + 4 * s, 52 + 4 * s), 0.5, A.mult, 32.25, A.add)
        for s, out, c in ((0, R("GE", 0, 64), -32.0), (1, R("UE", 64, 128), 1.0)):
            src = ind(R("IO", 0, 72), R("LR2", 4 * s, 4 * s + 4))
            if s in LEAVE_V:
                ts(out, src, c, A.add, W64[s], A.mult)
            else:
                act(out, src, scale=W64[s], bias=c * W64[s])
        digit = lambda s: ind(R("TE", 72 * s, 72 * s + 72), R("LE", 4 * s, 4 * s + 4))
        tie = R("tie", 0, 64)
        for a, b in FIRST:
            tt(R("T1", 16 * a, 16 * b), ind(R("GE", 0, 64), R("LY", 4 + a, 4 + b)), R("tie", 16 * a, 16 * b), A.add)
        tt(R("GE", C, 256), digit(1), R("T1", 64, 128), A.add)
        both = [digit(2), ind(R("UE"), R("LY", 12, 16))]
        tt(R("T2"), both[LAST], R("T1", 0, 64), A.add)
        tt(R("GE", 256, 320), both[1 - LAST], R("T2"), A.add)
        tt(R("GE", 320, 384), digit(0), tie, A.add)
        tt(R("GE", 64, 128), ind(R("GE", 0, 64), R("LY", 8, 12)), R("UE", 64, 128), A.add)
        for a, b in HOLD:
            unwrap(R("RE", a, b), R("GE", C + a, C + b))
        unwrap(R("RG"), R("GE", 0, 128))
        E = R("GE", C, 384)
        ent = lambda c: R("RE", 16 * ((c - 4) % 12) + 15, 16 * ((c - 4) % 12) + 16)
        lea = lambda c: R("RG", 16 * c + 15, 16 * c + 16)

        def above(k, thr):
            ts(R("CMP", C * k, C * k + C), E, cM, A.mult, thr, A.is_gt)
            scan(half("CNT", k), half("CMP", 2 * k), half("CMP", 2 * k + 1), A.add, A.add)

        for c in range(NV):
            above(c, ent(12 - NV + c))
        signs(5824, range(12 - NV), lambda c: E, ent, cnM, 28)
        cp(R("LP", 12 - NV, 12), R("CNT", H - 1, NV * H, H))
        ts(R("LP", 0, 12 - NV), R("AC", 28, 40 - NV), -0.5, A.mult, 95.75, A.add)
        op("v", lambda: g.vector.tensor_copy(T.O[:].indirect(T.LP[:]), T.IOb[:]), regs(R("IOb"), R("LP")), R("O")[1],
           60 + SCATTER * C)
        unwrap(R("RO"), R("O"))
        ts(ol, R("RO", 15, C, 16), cim, A.mult, 0.25, A.add)
        exchange(peer, "al%d" % t, [(lo, ol, 0)])
        place, size = lambda a, b: R("FL", 9 * a + 7, 9 * b, 9), lambda a, b: R("FL", 9 * a + 8, 9 * b, 9)
        cp(place(0, 12), R("LP"))
        for c in range(NE):
            above(6 + c, lea(c))
        signs(4288, range(NE, 8), lambda c: E, lea, cnM, 40)
        act(sm(9, NE, 8), R("AC", 40 + NE, 48), scale=-0.5, bias=96.0)
        if NE:
            tt(size(0, NE), R("CNT", 7 * H - 1, (6 + NE) * H, H), place(0, NE), A.subtract)
        tt(size(NE, 8), sm(9, NE, 8), place(NE, 8), A.subtract)
        if 2 in ENTER_V:
            act(sm(13, 0, 4), R("AC", 20, 24), scale=-0.5, bias=-32.0)
            tt(size(8, 12), sm(13, 0, 4), R("N64", 575, 768, 64), A.add)
        else:
            for c in range(8, 12):
                act(sm(13, c, c + 1), R("AC", 12 + c, 13 + c), scale=-0.5)
                act(size(c, c + 1), R("AC", 48 + c, 49 + c), scale=0.5, bias=sm(13, c, c + 1))
        for c in range(12):
            act(R("FL", 9 * c, 9 * c + 7), R("TH"), bias=size(c, c + 1), func=F.Sign)
        for k, w in enumerate((WL, WR)):
            scan(half("SL", k, 108), half("RL", k, 108), R("FL"))
            ts(half("LL", k, 12), R("SL", 109 * k + 7, 108 * k + 108, 9), 0.5 * sum(w) + 0.25 - k, A.add)
        for b in range(4):
            (act if b > 1 else cp)(R(Bt, b, 768, 4), ind(R("Tp", C * b, C * b + C), lo))
        quant(qf, sf, R(Bt))
        for b in range(4):
            mm(4 + b, blocks("qw")[b], blocks("sw")[b], qf, sf)
            if b not in COPY_V:
                act(R("TAB", TW * b, TW * b + C), bank(4 + b), scale=0.03125)
            else:
                ts(R("TAB", TW * b, TW * b + C), bank(4 + b), 0.03125, A.mult)
        before = None
        for b, k in WAVE:
            win = R("TAB", TW * b, TW * b + OFF[8])
            if k < 8:
                n, h, a, o = 193 - 2 ** k, 2 ** (k - 1), TW * b + OFF[k - 1], TW * b + OFF[k]
                scan(R("TAB", o, o + n), R("TAB", a, a + n), R("TAB", a + h, a + h + n), A.min, A.max, 1e29)
            elif k == 8:
                tt(R("MX", C * b, C * b + C), ind(win, R("LL", 12, 24)), R("G1", C * b, C * b + C), A.max)
            else:
                tt(R(Xn, b, 768, 4), R("MX", C * b, C * b + C), bank(b), A.add)
            before = follow(before)
            if k == 7:
                act(R("G1", C * b, C * b + C), ind(win, R("LL", 0, 12)))

    back[0] = 0
    act(R("PR"), ind(R("MOD"), R("LS", 0, 12)))
    dma("y", "dop", T.op[:], (T.PR[0:128:16, :], R("PR")[1]), 0)
    scores("X2", "qv", "sv")
    quant(R("qx2"), R("sx2"), R("X2"))
    dma("y", "doc", T.oc[:, 0:512], u8(R("qh", 0, 128)), 128 * 512)
    dma("s", "dod", T.oc[:, 512:768], u8(R("qh", C, 256)), 128 * 256)
    for k, e in enumerate(("y", "s", "y", "s")):
        dma(e, "ds%d" % k, T.osc[4 * k:4 * k + 4, :], (T.sx2[32 * k:32 * k + 4, :], R("sx2")[1]), 0)
    act(R("Y", 0, 112), bank(4, 0, 112))
    cp(R("Y", 112, C), bank(5, 48, 128))
    dma("s", "dy", T.y[:, 0:112], R("Y", 0, 112), 128 * 448)
    dma("y", "dz", T.y[:, 112:C], R("Y", 112, C), 128 * 320)

    known = {e: set() for e in Q}
    cur = {e: None for e in Q}
    nxt = {e: 0 for e in Q}
    last = {}
    count = [0]

    def new_batch(e, sem, base):
        count[0] += 1
        last[sem] = {"id": count[0], "e": e, "sem": sem, "n": base, "known": set(known[e]) if e else set(), "waited": False,
                     "calls": []}
        return last[sem]

    def wait(e, b):
        if b["id"] in known[e]:
            return
        if b["e"] and cur[b["e"]] is b:
            cur[b["e"]] = None
        Q[e].wait_ge(T.sem[b["sem"]], b["n"])
        b["waited"] = True
        known[e].add(b["id"])
        known[e].update(b["known"])
        cur[e] = None

    if not STARTS:
        STARTS.extend(order_calls(calls))
    for c in calls:
        c["start"] = STARTS[c["id"]]
        c["end"] = c["start"] + c["len"] + c["lat"]
    for c in sorted(calls, key=lambda c: (c["start"], c["id"])):
        e = c["e"]
        if e is None:
            c["batch"] = new_batch(None, c["sem"], c["count"])
            continue
        for b in sorted([p["batch"] for p in c["prev"] if p is not c["behind"]], key=lambda b: -b["id"]):
            wait(e, b)
        if c["sem"] == "":
            c["fn"]()
        elif c["sem"]:
            c["fn"]().then_inc(T.sem[c["sem"]], c["count"])
            c["batch"] = new_batch(e, c["sem"], c["count"])
        else:
            b = cur[e]
            if b and any(s["start"] < c["end"] + JOIN * WAKE and s["behind"] is not p and (s["behind"] is c or all(s is not n for n in c["next"]))
                         for p in b["calls"] for s in p["next"]):
                b = None
            if b is None:
                ring = [e + str((nxt[e] + i) % POOL[e]) for i in range(POOL[e])]
                sem = next((s for s in ring if s not in last or last[s]["id"] in known[e]), ring[0])
                nxt[e] = int(sem[1:]) + 1
                base = 0
                if sem in last:
                    wait(e, last[sem])
                    base = last[sem]["n"]
                b = cur[e] = new_batch(e, sem, base)
            c["fn"]().then_inc(T.sem[b["sem"]], 1)
            b["n"] += 1
            b["calls"].append(c)
            c["batch"] = b
    g.wait_ge(T.sem.ls, sent[0])
    for sem in SEMAPHORES:
        if sem in last and not last[sem]["waited"]:
            Q["g" if sem in DMAS else "t"].wait_ge(T.sem[sem], last[sem]["n"])
